import numpy as np, ml_dtypes
CORES = [23,119,17,113]
N = 4
import mx_ref
BF = ml_dtypes.bfloat16
def gentries(a):
    return np.ascontiguousarray(a.reshape(8, 16, -1).transpose(0, 2, 1)).reshape(8, -1)
def gtable(e):
    e = np.asarray(e); return np.ascontiguousarray(e.reshape(8, -1, 16).transpose(0, 2, 1)).reshape(128, -1).astype(np.int32)
def gcols(t, e):
    v = np.concatenate([t.reshape(8, 16, -1, 4), np.zeros((8, 16, 1, 4), BF)], axis=2)
    return np.ascontiguousarray(np.stack([v[g][:, e[g]] for g in range(8)])).reshape(128, -1)
def tile(rs):
    return np.stack(rs, axis=2).reshape(128, -1).astype(BF)
def pick(q, e):
    c = np.concatenate([q[0].reshape(128, -1, 4), np.zeros((128, 1, 4), np.uint8)], axis=1); s = np.concatenate([q[1], np.ones((16, 1), np.uint8)], axis=1)
    return (np.ascontiguousarray(c[:, e].reshape(128, -1)), np.ascontiguousarray(s[:, e]))
def join(*qs):
    return (np.concatenate([q[0] for q in qs], axis=1), np.concatenate([q[1] for q in qs], axis=1))
def put(q, e, v):
    c, s = q[0].reshape(128, -1, 4).copy(), q[1].copy(); c[:, e] = v[0].reshape(128, -1, 4); s[:, e] = v[1]
    return (c.reshape(128, -1), s)
def pk(c, s):
    return (np.ascontiguousarray(c), mx_ref.live(s))
def emit(q):
    return q[0], q[1]
def packed(v, rng):
    q = [mx_ref.quantize(np.ascontiguousarray(v[r])) for r in range(N)]
    return np.stack([a for a, b in q]), np.stack([mx_ref.plane(b, rng) for a, b in q])
def values_of_codes():
    e, c = np.zeros((128, 128, 4), np.float32), np.zeros((128, 2, 4), np.uint8)
    e[np.arange(128), np.arange(128), 0] = 1
    c[:127, :, 0] = np.arange(256).reshape(2, 128).T[:127]
    return mx_ref.matmul(mx_ref.quantize(e.reshape(128, 512).astype(BF)), (c.reshape(128, 8), np.full((16, 2), 127, np.uint8))).T.reshape(-1).astype(np.float64)
CODE_VALUE, SCALE_VALUE = values_of_codes(), 2.0 ** (np.arange(256) - 127.0)
def decode(q):
    return (CODE_VALUE[q[0]].reshape(16, 8, -1, 4) * SCALE_VALUE[q[1]][:, None, :, None] + 0.0).reshape(128, -1).astype(np.float32)
def f(rng, *shape):
    return mx_ref.flush((rng.standard_normal(shape, dtype=np.float32) * np.exp2(rng.integers(-2, 3, shape[:-1] + (1,)))).astype(BF))
def wide(rng, *shape, cols=0):
    v = rng.standard_normal(shape, dtype=np.float32) * np.exp2(rng.integers(-12, 13, shape)).astype(np.float32)
    if cols: v *= np.repeat(np.exp2(rng.integers(-cols, cols + 1, shape[:-2] + (1, shape[-1] // 4))) * (rng.random(shape[:-2] + (1, shape[-1] // 4)) > 0.0625), 4, axis=-1).astype(np.float32)
    return mx_ref.flush(v.astype(BF))
C = 384
STEP = [1, 2, 3]
GAPS = [[2, 4, 5, 6, 7, 8], [3, 4, 5, 6, 7, 8]]
def numbers_of(rng):
    return {"x": np.array(f(rng, N, 128, 4 * C)), "u": np.array(f(rng, N, 128, 512)), "v": np.array(f(rng, N, 128, 512))}
def full(rng, k):
    h = 128 + rng.permutation(128)[:k]
    low = rng.permutation(np.concatenate([2 * h, 2 * h + 1]))[:C - 127 - k]
    return np.sort(np.concatenate([np.arange(1, 128), h, low]))
def below(h):
    return np.concatenate([np.arange(h << n, (h + 1) << n) for n in range(10 - h.bit_length())])
def lean(side, slot):
    c = 3 - side
    return np.sort(np.concatenate([[1], below(2 + side), np.concatenate([[c], below(2 * c + slot)])[:C - 256]]))
def ragged(rng, first):
    cuts, left = [], 511 - C
    for n, most in [(n, 1) for n in first] + [(n, 9) for n in range(3, 9)]:
        size = 2 ** (9 - n) - 1
        k = min(most, left // size)
        cuts += [n] * k
        left -= k * size
    keep = np.arange(512) > 0
    for n in sorted(cuts):
        h = np.arange(2 ** n, 2 ** (n + 1))
        h = int(rng.choice(h[keep[h] & keep[h ^ 1]]))
        keep[below(h)] = False
    return np.flatnonzero(keep)
def grown(h, places):
    at = np.zeros(512, np.int64)
    at[h] = places
    e = np.zeros(C, np.int64)
    e[places[1:]] = 2 * at[h[1:] >> 1] + (h[1:] & 1)
    return e
def shuffled(rng):
    return np.concatenate([[0], 1 + rng.permutation(C - 1)])
def trees(rng):
    t = np.stack([np.stack([grown(full(rng, int(rng.integers(112, 129))), shuffled(rng)) for g in range(8)]) for r in range(N)])
    o = rng.permutation(8)
    for r in range(N):
        for n in range(2): t[r, o[(r + 4 * n) % 8]] = grown(ragged(rng, GAPS[n]), shuffled(rng))
    return t
def stored(t):
    return {"se": np.stack([gtable(t[r]) for r in range(N)])}
def weights(rng, w):
    c, s = packed(np.ascontiguousarray(w).reshape(N, 128, 2048), rng)
    return {"wc": c, "ws": s}
def layers(rng, still=[], pairs=False):
    w = np.array(f(rng, N, 128, 2048)).reshape(N, 8, 16, 4, 8, 16, 4)
    for i in still:
        w[:, :, i] = 0
        w[:, :, :, :, :, i] = 0
    if pairs:
        w[:, :, :, :, :, 8:] = 0
        for g in range(8):
            w[:, g, 8, 0, g, 8, 0] = -28.0
            for b in range(4): w[:, g, 10, b, g, 9, 0] = -2.0 ** (b - 5)
    return weights(rng, w)
def setup_inputs(rng):
    return {**numbers_of(rng), **stored(trees(rng)), **layers(rng)}
def setup_inputs_ties(rng):
    d = numbers_of(rng)
    o = rng.permutation(N)
    k = rng.integers(-1, 2, (N, 8, C)).astype(np.float32)
    k[o[1]] = -1
    x = d["x"].reshape(N, 8, 16, C, 4)
    x[:, :, 0] = 0
    x[:, :, 0, :, 0] = k.astype(BF)
    a = np.exp2(rng.integers(-3, 4, (1, 8, 1)).astype(np.float32))
    x[:, :, 8:] = 0
    x[:, :, 8, :, 0] = (-1.125 * a).astype(BF)
    x[:, :, 10, :, 0] = (-0.0703125 * a).astype(BF)
    c = np.ones(N, np.float32)
    c[o[0]] = 0
    c[o[2]] = -1
    u = d["u"].reshape(N, 128, 128, 4)
    u[:, :, ::16] = 0
    for h in range(0, 128, 16): u[:, h, h, 0] = c.astype(BF)
    return {"x": x.reshape(N, 128, 4 * C), "u": u.reshape(N, 128, 512), "v": d["v"], **stored(trees(rng)), **layers(rng, [0], True)}
def setup_inputs_near(rng):
    d = numbers_of(rng)
    o = rng.permutation(N) % 2
    k = np.where(o == 0, 2.0 ** -30, 1.0).astype(np.float32)
    x = np.zeros((N, 8, 16, C, 4), np.float32)
    s = rng.integers(-1, 2, (N, 8, C)) * k[:, None, None]
    x[:, :, 0, :, 0] = 1.125 * s
    x[:, :, 1, :, 0] = -1.25 * s
    s = rng.choice([-1.0, 1.0], (N, 8, C)) * 2.0 ** -30
    x[:, :, 8, :, 0] = 1.125 * s
    x[:, :, 9, :, 0] = -1.25 * s
    x[:, :, 2, :, 0] = 2.0 ** -28
    x[:, :, 10, :, 0] = 2.0 ** -28
    for r in range(N):
        at = [0, C - 1, int(rng.integers(C)), int(rng.integers(C))]
        for g, j in zip(rng.permutation(8)[:4], at): x[r, g, 0, j, 0] = 2.0 ** 30 * rng.choice([-1.0, 1.0])
    u = d["u"].astype(np.float32).reshape(N, 128, 128, 4)
    u[:, :, ::16] = 0
    w = np.zeros((N, 128, 4, 128, 4), np.float32)
    for h in range(0, 128, 16):
        u[:, h, h, 0] = 1.125 * k
        u[:, h + 1, h, 0] = k
        w[:, h + 8, 0, h, 0] = 0.5
        w[:, h + 9, 0, h + 1, 0] = 0.5
        w[:, h + 10, 0, h + 2, 0] = 32.0
        w[:, h + 10, 0, h + 10, 0] = 32.0
    return {"x": x.reshape(N, 128, 4 * C).astype(BF), "u": u.reshape(N, 128, 512).astype(BF), "v": d["v"], **stored(trees(rng)), **weights(rng, w.astype(BF))}
def setup_inputs_odd(rng):
    d = numbers_of(rng)
    x = (1.0 + (2 * rng.integers(0, 64, (N, 16, 8, C, 4)) + 1) * 2.0 ** -7) * np.exp2(-rng.integers(0, 7, (N, 16, 8, C, 4)).astype(np.float64)) * rng.choice([-1.0, 1.0], (N, 16, 8, C, 4))
    x[:, :, 0, :, 0] = 1.96875 * 2.0 ** 8 * rng.choice([-1.0, 1.0], (N, 16, C))
    e = rng.choice([-1.0, 1.0], (N, 8, C)) * 2.0 ** -5
    x[:, ::2, 1, :, 0] = 1.125 * e
    x[:, ::2, 2, :, 0] = -e
    u = d["u"].reshape(N, 128, 128, 4)
    u[:, :, ::16] = 0
    for h in range(0, 128, 16): u[:, h + 1:h + 3, h, 0] = 1
    return {"x": x.astype(np.float32).reshape(N, 128, 4 * C).astype(BF), "u": u.reshape(N, 128, 512), "v": d["v"], **stored(trees(rng)), **layers(rng, [0, 8])}
def setup_inputs_ends(rng):
    d = numbers_of(rng)
    o, e = rng.permutation(N) % 4, rng.permutation(N) % 4
    x = np.zeros((N, 128, C, 4))
    u = d["u"].astype(np.float32).reshape(N, 128, 128, 4)
    v = d["v"].astype(np.float32)
    w = np.zeros((N, 128, 4, 128, 4), np.float32)
    t = np.zeros((N, 8, C), np.int64)
    i = np.arange(128)
    last = i % 16 == 15
    for r in range(N):
        h = rng.permutation(8)
        c = np.where(h < 2, 0.0, h % 2 * 2.0 - 1.0)[None, :, None]
        a = -(0.9 + 0.1 * rng.random((128, C, 4))) * 2.0 ** 30
        if o[r] == 1: a = a * rng.choice([-1.0, 1.0], (C, 1))
        if o[r] == 2: a = -(1.0 + 0.125 * rng.integers(0, 8, (128, C, 4))) * 2.0 ** -30
        if o[r] == 3: a = d["x"][r].astype(np.float32).reshape(128, C, 4)[:, :1]
        x[r] = a
        if o[r] < 2:
            x[r, last] = 2.0 ** -30
            u[r, :, ::16] = c * (0.9 + 0.1 * rng.random((128, 8, 4))) * 2.0 ** 30
            v[r] = rng.choice([-1.0, 1.0], (128, 512)) * (0.9 + 0.1 * rng.random((128, 512))) * 2.0 ** 30
        if o[r] == 2:
            u[r, :, ::16] = c * (1.0 + 0.125 * rng.integers(0, 8, (128, 8, 4))) * 2.0 ** -30
            v[r] = rng.choice([-1.0, 1.0], (128, 512)) * (1.0 + 0.125 * rng.integers(0, 8, (128, 512))) * 2.0 ** -30
        if o[r] == 3: u[r, :, ::16] *= np.abs(c).astype(np.float32)
        k = np.where(last, [32.0, 32.0, 256.0, 2.0 ** -8][o[r]], 32.0)
        for b in range(4): w[r, i, b, i, b] = k
        for g in range(8):
            if e[r] == 0: t[r, g] = grown(lean(0, g % 2), np.arange(C))
            if e[r] == 1: t[r, g] = grown(lean(1, g % 2), np.concatenate([[0], np.arange(C - 1, 0, -1)]))
            if e[r] >= 2: t[r, g] = grown(ragged(rng, GAPS[g - 6]) if g >= 6 else full(rng, 128 if e[r] == 2 else (C - 125) // 3), shuffled(rng))
    return {"x": x.astype(np.float32).reshape(N, 128, 4 * C).astype(BF), "u": u.reshape(N, 128, 512).astype(BF), "v": v.astype(BF), **stored(t), **weights(rng, w.astype(BF))}
def setup_inputs_spread(rng):
    d = setup_inputs(rng)
    d["x"] = wide(rng, N, 128, 4 * C, cols=6)
    return d
def check_inputs(d):
    b = []
    for k in ("x", "u", "v"):
        a = np.abs(d[k].astype(np.float32))
        if not (np.isfinite(a).all() and ((a == 0) | (a >= 2.0 ** -30) & (a <= 2.0 ** 30)).all()): b.append("a value of " + k)
    e = np.stack([gentries(d["se"][r]) for r in range(N)])
    if not ((e >= 0) & (e < 2 * C)).all(): b.append("an entry of se")
    else:
        if e[:, :, 0].any(): b.append("se: entry 0")
        if (np.diff(np.sort(e[:, :, 1:], axis=2), axis=2) == 0).any(): b.append("se: equal seats")
        a = e >> 1
        for n in range(7): a = np.take_along_axis(e >> 1, a, 2)
        if a.any(): b.append("se: a place from which eight steps don't lead to place 0")
    none, least, most = [emit(mx_ref.quantize(np.full((128, 16), k, np.float32).astype(BF)))[1][0, 0] for k in (0.0, 2.0 ** -8, 2.0 ** 8)]
    for r in range(N):
        if ((d["wc"][r] == 0x7F) | (d["wc"][r] == 0xFF)).any(): b.append("wc: a code that is no number")
        s = mx_ref.live(d["ws"][r])
        if ((s != none) & ((s < least) | (s > most))).any(): b.append("ws: a scale out of range")
        if (((d["wc"][r].reshape(16, 8, 512, 4) & 0x7F) != 0) & (s == none)[:, None, :, None]).any(): b.append("wc: a code other than zero under the scale of zeros")
    return b
def reference(x, u, v, se, wc, ws):
    qu = [mx_ref.quantize(u[r]) for r in range(N)]
    lay = [pk(wc[r], ws[r]) for r in range(N)]
    seat = [gentries(se[r]).astype(np.int64) for r in range(N)]
    par = [seat[r] >> 1 for r in range(N)]
    now = [x[r] for r in range(N)]
    y, im = np.zeros((N, 128, C), np.float32), np.zeros((N, 8, C), np.float32)
    oc, osc = np.zeros((N, 128, 4 * C), np.uint8), np.zeros((N, 16, C), np.uint8)
    for step in STEP:
        q = [mx_ref.quantize(now[r]) for r in range(N)]
        layered, child = [], []
        for r in range(N):
            layered.append(tile([mx_ref.matmul(pick(lay[r], np.arange(128 * b, 128 * b + 128)), q[r]) * np.float32(0.03125) for b in range(4)]))
            turn = (mx_ref.matmul(qu[r], q[r])[::16] < 0).astype(np.int64)
            seat[r] = seat[r] ^ np.take_along_axis(turn, par[r], 1)
            c = np.full((8, 2 * C), -1, np.int64)
            np.put_along_axis(c, seat[r][:, 1:], np.tile(np.arange(1, C), (8, 1)), 1)
            child.append(c)
        for r in range(N):
            p = r ^ step
            m = np.zeros((8, C), np.int64)
            for depth in range(8):
                at = np.take_along_axis(m, par[r], 1)
                c = np.take_along_axis(child[p], 2 * at + (seat[r] & 1), 1)
                m = np.where(c < 0, at, c)
                m[:, 0] = 0
            e = mx_ref.quantize(gcols(layered[p], m))
            above = gcols(decode(q[r]).astype(BF), par[r]).astype(np.float32)
            now[r] = ((decode(e) + above) * np.float32(0.5)).astype(BF)
            im[r] = m
    for r in range(N):
        z = mx_ref.quantize(now[r])
        y[r] = mx_ref.matmul(mx_ref.quantize(v[r]), z)
        oc[r], osc[r] = emit(z)
    return {"y": y, "im": im, "oc": oc, "osc": osc}

@@ -1,0 +1,525 @@
+from concourse.bass import DstId, RemoteDMATransfer
+from concourse.mybir import dt, AluOpType, AxisListType, ActivationFunctionType as AF
+
+C = 384
+CH = [(0, 192), (192, 384)]
+HC = [(0, 128), (128, 384)]
+FQ = ["AAAA", "AVVV", "AVVV"]
+SCRATCH = {
+    "KX": ("sbuf", [128, 32], "int32"), "KF": ("sbuf", [128, 32], "float32"), "tm": ("sbuf", [128, 128], "int32"),
+    "AD": ("sbuf", [128, 8], "float32"), "rL": ("sbuf", [128, 16], "float32"), "rA": ("sbuf", [128, 16], "float32"),
+    "rK": ("sbuf", [128, 16], "float32"), "rN": ("sbuf", [128, 8], "float32"), "bh": ("sbuf", [128, 16], "float32"),
+    "eqm": ("sbuf", [128, 16], "float32"), "sx": ("sbuf", [128, 16], "float32"), "ow": ("sbuf", [128, 16], "float32"),
+    "NK": ("sbuf", [128, 8], "float32"), "OH": ("sbuf", [128, 4], "float32"), "H2": ("sbuf", [128, 2], "float32"),
+    "iC": ("sbuf", [128, 512], "bfloat16"), "mk": ("sbuf", [128, 512], "bfloat16"), "R0": ("sbuf", [128, 512], "bfloat16"),
+    "TB": ("sbuf", [128, 288], "float32"), "MX": ("sbuf", [128, 384], "bfloat16"), "SF": ("sbuf", [128, 384], "float32"),
+    "R4": ("sbuf", [128, 128], "bfloat16"), "GA": ("sbuf", [128, 384], "bfloat16"), "SB2": ("sbuf", [128, 224], "bfloat16"),
+    "PL": ("sbuf", [128, 18], "uint16"), "PS": ("sbuf", [128, 128], "bfloat16"), "Ye": ("sbuf", [128, 32], "float32"),
+    "s5": ("sbuf", [128, 128], "float32"), "s6": ("sbuf", [128, 128], "float32"),
+    "ULi": ("sbuf", [128, 8], "int32"),
+    "UL": ("sbuf", [128, 8], "uint16"), "JC": ("sbuf", [128, 32], "float32"), "hf": ("sbuf", [128, 128], "bfloat16"),
+    "idn": ("sbuf", [128, 128], "bfloat16"), "EB": ("sbuf", [128, 2048], "bfloat16"),
+    "eq": ("sbuf", [128, 512], "float8_e4m3fn_x4"), "es": ("sbuf", [128, 512], "uint8"),
+    "seI": ("sbuf", [128, 24], "int32"), "paI": ("sbuf", [128, 24], "int32"), "paU": ("sbuf", [128, 24], "uint16"),
+    "slI": ("sbuf", [128, 24], "int32"), "sh": ("sbuf", [128, 24], "float32"), "sb": ("sbuf", [128, 24], "float32"),
+    "sw": ("sbuf", [128, 24], "float32"), "s24": ("sbuf", [128, 24], "float32"), "stU": ("sbuf", [128, 24], "uint16"),
+    "xb": ("sbuf", [128, 1536], "bfloat16"), "ub": ("sbuf", [128, 512], "bfloat16"),
+    "vb": ("sbuf", [128, 512], "bfloat16"), "wq": ("sbuf", [128, 512], "float8_e4m3fn_x4"), "wp": ("sbuf", [128, 512], "uint8"),
+    "uq": ("sbuf", [128, 128], "float8_e4m3fn_x4"), "us": ("sbuf", [128, 128], "uint8"),
+    "upq": ("sbuf", [128, 128], "float8_e4m3fn_x4"), "ups": ("sbuf", [128, 128], "uint8"),
+    "vq": ("sbuf", [128, 128], "float8_e4m3fn_x4"), "vs": ("sbuf", [128, 128], "uint8"),
+    "Nc": ("sbuf", [128, 784], "bfloat16"), "LT": ("sbuf", [128, 8], "uint16"), "LL": ("sbuf", [128, 32], "uint16"),
+    "ys": ("sbuf", [128, 8], "float32"), "st4": ("sbuf", [128, 8], "float32"), "t4": ("sbuf", [128, 8], "float32"),
+    "rd": ("sbuf", [128, 8], "float32"), "GM": ("sbuf", [128, 512], "bfloat16"), "SB": ("sbuf", [128, 512], "bfloat16"),
+    "YU": ("sbuf", [128, 34], "uint16"), "Yd": ("sbuf", [128, 40], "float32"), "s1": ("sbuf", [128, 32], "float32"),
+    "s2": ("sbuf", [128, 32], "float32"), "s3": ("sbuf", [128, 32], "float32"), "s4": ("sbuf", [128, 32], "float32"),
+    "oU": ("sbuf", [128, 32], "uint16"), "inv": ("sbuf", [128, 1024], "bfloat16"), "NP": ("sbuf", [128, 24], "uint16"),
+    "sg": ("sbuf", [128, 400], "bfloat16"), "C0": ("sbuf", [128, 272], "bfloat16"), "C1": ("sbuf", [128, 272], "bfloat16"),
+    "SC": ("sbuf", [128, 272], "bfloat16"), "P1": ("sbuf", [128, 128], "bfloat16"), "P4": ("sbuf", [128, 128], "bfloat16"),
+    "TU": ("sbuf", [128, 96], "uint16"), "Tr": ("sbuf", [128, 512], "bfloat16"),
+    "HL": ("sbuf", [128, 72], "uint16"), "yL": ("sbuf", [128, 96], "uint16"), "tL": ("sbuf", [128, 96], "uint16"),
+    "YR": ("sbuf", [128, 1536], "bfloat16"), "Z": ("sbuf", [128, 512], "bfloat16"), "MU": ("sbuf", [128, 72], "uint16"),
+    "mr": ("sbuf", [128, 384], "float32"),
+    "xq": ("sbuf", [128, 1536], "float8_e4m3fn_x4"), "xs": ("sbuf", [128, 1536], "uint8"), "hb": ("sbuf", [128, 1536], "bfloat16"),
+    "hq": ("sbuf", [128, 1152], "float8_e4m3fn_x4"), "hs": ("sbuf", [128, 1152], "uint8"),
+    "hL": ("sbuf", [128, 1152], "float8_e4m3fn_x4"), "hP": ("sbuf", [128, 1152], "uint8"),
+    "fb": ("sbuf", [128, 1536], "bfloat16"), "bb": ("sbuf", [128, 1536], "bfloat16"), "ab": ("sbuf", [128, 1536], "bfloat16"),
+    "xn": ("sbuf", [128, 1536], "bfloat16"), "yb": ("sbuf", [128, 384], "float32"),
+}
+for _k in range(8):
+    SCRATCH["ps%d" % _k] = ("psum", [128, 512], "float32")
+SEMAPHORES = (["cV", "cA", "cT", "cG", "loc"] + ["d%d" % k for k in range(24)] + ["ay%d" % k for k in range(3)]
+              + ["at%d" % k for k in range(3)] + ["as%d" % k for k in range(3)]
+              + ["ah%d_%d" % (r, k) for r in range(3) for k in range(len(HC))])
+
+
+def rank_program(g, core, T, topo):
+    rank = T.rank_of(core)
+    if rank is None:
+        return
+    op = AluOpType
+    eng = {"V": g.vector, "A": g.scalar, "T": g.tensor, "G": g, "Y": g.sync}
+    cnt = {q: 0 for q in eng}
+    know = {q: {} for q in eng}
+    snap = {}
+    acc = {}
+    dmas = []
+    loc = [0]
+
+    def R(n, a=0, b=None, s=1):
+        return (n, a, SCRATCH[n][1][1] if b is None else b, s)
+
+    def v(r):
+        n, a, b, s = r
+        return T[n][:, a:b] if s == 1 else T[n][:, a:b:s]
+
+    def meet(a, b):
+        if a[3] == b[3] and a[3] > 1 and (a[1] - b[1]) % a[3]:
+            return False
+        return a[1] < b[2] and b[1] < a[2]
+
+    def wait(q, tok):
+        if know[q].get(tok[0], 0) >= tok[1]:
+            return
+        eng[q].wait_ge(T.sem[tok[0]], tok[1])
+        for k, n in list(snap.get(tok, {}).items()) + [tok]:
+            know[q][k] = max(know[q].get(k, 0), n)
+
+    def order(q, rd, wr, dma=False):
+        need = {}
+        for r, w in [(r, False) for r in rd] + [(r, True) for r in wr]:
+            bank = r[0].startswith("ps")
+            for r0, w0, q0, tok in acc.get(r[0], []):
+                if bank:
+                    if q0 == q and not (w0 or w) or (q0 == q and q == "T"):
+                        continue
+                elif not (w or w0) or not meet(r, r0):
+                    continue
+                need[tok[0]] = max(need.get(tok[0], 0), tok[1])
+        for k in sorted(need):
+            wait(q, (k, need[k]))
+
+    def record(q, rd, wr, tok):
+        snap[tok] = dict(know[q])
+        for r, w in [(r, False) for r in rd] + [(r, True) for r in wr]:
+            l = acc.setdefault(r[0], [])
+            if w and r[3] == 1:
+                l[:] = [e for e in l if not (r[1] <= e[0][1] and e[0][2] <= r[2])]
+            if w and r[0].startswith("ps"):
+                l[:] = []
+            l.append((r, w, q, tok))
+
+    def emit(q, fn, rd, wr):
+        rd = [r for r in rd if isinstance(r, tuple)]
+        order(q, rd, wr)
+        cnt[q] += 1
+        fn().then_inc(T.sem["c" + q], 1)
+        record(q, rd, wr, ("c" + q, cnt[q]))
+
+    def dma(q, out, in_, rd, wr):
+        order(q, rd, wr, True)
+        s = "d%d" % len(dmas)
+        dmas.append((q, s))
+        eng[q].dma_start(out, in_).then_inc(T.sem[s], 16)
+        record(q, rd, wr, (s, 16))
+
+    def sc(x):
+        return v(x) if isinstance(x, tuple) else x
+
+    def tt(out, a, b, o, ind=None):
+        emit("V", lambda: g.vector.tensor_tensor(v(out), v(a).indirect(v(ind)) if ind else v(a), v(b), o), [a, b, ind], [out])
+
+    def ts(out, a, s1, s2, o1, o2=None):
+        if o2 is None:
+            emit("V", lambda: g.vector.tensor_scalar(v(out), v(a), sc(s1), None, o1), [a, s1], [out])
+        else:
+            emit("V", lambda: g.vector.tensor_scalar(v(out), v(a), sc(s1), sc(s2), o1, o2), [a, s1, s2], [out])
+
+    def tc(out, a, ind=None, oind=None):
+        emit("V", lambda: g.vector.tensor_copy(v(out).indirect(v(oind)) if oind else v(out), v(a).indirect(v(ind)) if ind else v(a)),
+             [a, ind, oind], [out])
+
+    def act(out, a, f=AF.Copy, ind=None, **k):
+        emit("A", lambda: g.scalar.activation(v(out), v(a).indirect(v(ind)) if ind else v(a), f, **k), [a, ind], [out])
+
+    def fill(out, x):
+        emit("V", lambda: g.vector.memset(v(out), x), [], [out])
+
+    def total(out, a):
+        emit("V", lambda: g.vector.tensor_reduce(v(out), v(a), AxisListType.X, op.add), [a], [out])
+
+    def scan(out, n, a, z="R0"):
+        emit("V", lambda: g.vector.tensor_tensor_scan(v(out), v(R(z, 0, n)), v(a), 0.0, op.mult, op.add), [R(z, 0, n), a], [out])
+
+    def hold(out, n, a):
+        f = R("SF", 0, n)
+        emit("V", lambda: g.vector.tensor_tensor_scan(v(f), v(R("MX", 0, n)), v(a), 0.0, op.add, op.max), [R("MX", 0, n), a], [f])
+        ts(out, R("SF", 15, n, 16), R("AD", 6, 7), None, op.add)
+
+    def quant(q, s, a):
+        emit("V", lambda: g.vector.quantize_mx(v(q), v(s), v(a)), [a], [q, s])
+
+    def mm(bank, n, lq, ls, rq, rs):
+        o = R("ps%d" % bank, 0, n)
+        emit("T", lambda: g.tensor.matmul_mx(v(o), v(lq), v(ls), v(rq), v(rs), True, True), [lq, ls, rq, rs], [o])
+
+    def iota(out, pat, base, cm=0):
+        kw = {} if SCRATCH[out[0]][2] == "int32" else {"allow_small_or_imprecise_dtypes": True}
+        emit("G", lambda: g.iota(v(out), pat, base, cm, **kw), [], [out])
+
+    rest = []
+
+    def slip():
+        if rest:
+            rest.pop(0)()
+
+    def dist(win, ind, n, o="SB", a=0):
+        tt(R("GM", 0, n), win, R("mk", 0, n), op.mult, ind)
+        slip()
+        scan(R(o, a, a + n), n, R("GM", 0, n))
+        slip()
+        return R(o, a + 15, a + n, 16)
+
+    def b8(r):
+        return v(r).bitcast(dt.uint8)
+
+    dma("Y", v(R("seI")), T.se[:, :], [], [R("seI")])
+    dma("Y", v(R("ub")), T.u[:, :], [], [R("ub")])
+    for a, b in CH:
+        dma("Y", v(R("xb", 4 * a, 4 * b)), T.x[:, 4 * a:4 * b], [], [R("xb", 4 * a, 4 * b)])
+    dma("Y", b8(R("wq")), T.wc[:, :], [], [R("wq")])
+    dma("Y", v(R("wp")), T.ws[:, :], [], [R("wp")])
+    dma("Y", v(R("vb")), T.v[:, :], [], [R("vb")])
+    part = [T.cores[rank ^ s] for s in (1, 2, 3)]
+
+    def engs(a, b):
+        return topo.engines(a, b)
+
+    def some(e):
+        m = 0
+        for k in e:
+            m |= 1 << k
+        return m
+    cut = [(0, 4), (4, 6), (6, 8)]
+    for r in range(3):
+        n = len(engs(part[r], core))
+        acc.setdefault("yL", []).append((R("yL", 32 * r, 32 * r + 32), True, "R", ("ay%d" % r, cut[r][1] - cut[r][0])))
+        acc.setdefault("tL", []).append((R("tL", 32 * r, 32 * r + 32), True, "R", ("at%d" % r, n)))
+        acc.setdefault("hP", []).append((R("hP", C * r, C * r + C), True, "R", ("as%d" % r, n)))
+        for k, (a, b) in enumerate(HC):
+            acc.setdefault("hL", []).append((R("hL", C * r + a, C * r + b), True, "R", ("ah%d_%d" % (r, k), n)))
+
+    iota(R("KX"), [[0, 32]], 0, 1)
+    iota(R("iC", 0, 384), [[1, 384]], -256)
+    iota(R("tm"), [[0, 8], [1, 16]], 0, -1)
+    iota(R("ULi"), [[16, 8]], 0)
+    for a, n in ((0, 2), (2, 2), (4, 4), (8, 8)):
+        iota(R("rL", a, a + n), [[1, n]], 0 if a else -1)
+        iota(R("rA", a, a + n), [[0, n]], 256 // max(a, 1))
+        iota(R("rK", a, a + n), [[0, n]], 2 * max(a, 1))
+    for a, n, w in ((0, 2, 1), (2, 2, 4), (4, 1, 16)):
+        iota(R("rN", a, a + n), [[w, n]], w)
+    iota(R("iC", 384, 512), [[1, 128]], 128)
+    fill(R("hf"), 0.5)
+    fill(R("R0"), 1.0)
+    fill(R("R0", 0, 512, 16), 0.0)
+    fill(R("PS"), 0.0)
+    fill(R("TB", 0, 128), -241.0)
+    fill(R("TB", 128, 288), -240.0)
+    fill(R("R4"), 1.0)
+    fill(R("R4", 0, 128, 4), 0.0)
+    for a, b, m in ((0, 2, 0), (2, 4, 1), (4, 8, 3), (8, 16, 7), (16, 17, 15), (17, 18, 1)):
+        ts(R("KX", a, b), R("KX", a, b), m, None, op.bitwise_and)
+    for k in range(1, 4):
+        w = R("KX", 16 + 2 ** k, 16 + 2 ** (k + 1))
+        ts(w, w, k, 1, op.logical_shift_right, op.bitwise_and)
+    tc(R("KF"), R("KX"))
+    q_ = R("KF", 16, 17)
+
+    def bit(k):
+        return R("KF", 16 + 2 ** k, 17 + 2 ** k)
+    ts(R("AD", 0, 1), q_, 0.0, None, op.is_equal)
+    ts(R("tm"), R("tm"), 15, None, op.bitwise_and)
+    ts(R("mk", 0, 128), R("tm"), 0.0, None, op.is_equal)
+    tc(R("LT", 0, 1), bit(0))
+    act(R("Nc", 0, 768, 2), R("iC", 0, 384))
+    act(R("Nc", 1, 768, 2), R("iC", 0, 384))
+    act(R("AD", 1, 2), R("AD", 0, 1), AF.Identity, scale=768.0)
+    act(R("AD", 2, 3), R("AD", 0, 1), AF.Identity, scale=128.0, bias=256.0)
+    for k in range(1, 4):
+        act(R("AD", 2 + k, 3 + k), bit(k), AF.Identity, bias=512.0)
+    act(R("mk", 128, 256), R("mk", 0, 128))
+    act(R("mk", 256, 512), R("mk", 0, 256))
+    act(R("AD", 6, 7), q_, AF.Identity, scale=512.0, bias=-7424.0)
+    act(R("MX"), R("mk", 0, 384), AF.Identity, scale=-33280.0, bias=512.0)
+    act(R("ys", 0, 1), q_, AF.Identity, scale=0.0, bias=-256.0)
+    act(R("H2", 0, 1), q_, AF.Identity, scale=0.0, bias=256.0)
+    act(R("H2", 1, 2), q_, AF.Identity, scale=0.0, bias=256.5)
+    act(R("sg", 384, 400), R("KF", 0, 16), AF.Identity, scale=0.0, bias=1.0)
+    act(R("Yd", 32, 40), R("KF", 0, 8), AF.Identity, scale=0.0, bias=1000.0)
+    act(R("bh"), R("KF", 16, 32), AF.Identity, bias=-0.5)
+    for m, n, w in ((0, 1, 8.0), (1, 2, 4.0), (3, 4, 2.0), (7, 8, 1.0)):
+        act(R("C0", 16 * m, 16 * (m + n)), R("mk", 16 * m, 16 * (m + n)), AF.Identity, scale=w)
+    ts(R("paI"), R("seI"), 1, None, op.arith_shift_right)
+    ts(R("slI"), R("seI"), 1, None, op.bitwise_and)
+    tc(R("paU"), R("paI"))
+    ts(R("sh"), R("slI"), -1.0, 0.5, op.mult, op.add)
+    tt(R("sb"), R("seI"), R("sh"), op.add)
+    ts(R("sb", 0, 1), R("sb", 0, 1), R("AD", 1, 2), None, op.add)
+    fill(R("EB"), 0.0)
+
+    def score(r, k):
+        a, b = CH[k]
+        bank = (0, 7)[k]
+        mm(bank, b - a, R("upq"), R("ups"), R("xq", C * r + a, C * r + b), R("xs", C * r + a, C * r + b))
+        act(R("sg", a, b), R("ps%d" % bank, 0, b - a), AF.Sign, bias=2.0 ** -93)
+
+    def pack_x(r, src):
+        for k, (a, b) in enumerate(CH):
+            quant(R("xq", C * r + a, C * r + b), R("xs", C * r + a, C * r + b), R(src, 4 * a, 4 * b))
+
+    HB = [[1, 2, 3, 4], [5, 6, 0, 7]]
+
+    def layer(r):
+        for k, (a, b) in enumerate(HC):
+            for t in range(4):
+                mm(HB[k][t], b - a, R("wq", 128 * t, 128 * t + 128), R("wp", 128 * t, 128 * t + 128),
+                   R("xq", C * r + a, C * r + b), R("xs", C * r + a, C * r + b))
+                act(R("hb", 4 * a + t, 4 * b, 4), R("ps%d" % HB[k][t], 0, b - a), scale=0.03125)
+
+    def pack_h(r, k):
+        a, b = HC[k]
+        quant(R("hq", C * r + a, C * r + b), R("hs", C * r + a, C * r + b), R("hb", 4 * a, 4 * b))
+
+    def remote(dst, out, in_, rd, sem):
+        order("G", rd, [], True)
+        rid, pid, _ = topo.addr(dst)
+        g.remote_dma(out_ap=out, in_ap=in_, remote_sem=T.sem[sem], local_sem=T.sem.loc, pid=pid, routing_id=rid,
+                     dma_engine_mask=topo.mask(core, dst))
+        loc[0] += len(engs(core, dst))
+
+    def send_h(r, k):
+        a, b = C * r + HC[k][0], C * r + HC[k][1]
+        remote(part[r], b8(R("hL", a, b)), b8(R("hq", a, b)), [R("hq", a, b)], "ah%d_%d" % (r, k))
+
+    def send_s(r):
+        w = (C * r, C * r + C)
+        remote(part[r], v(R("hP", *w)), v(R("hs", *w)), [R("hs", *w)], "as%d" % r)
+
+    def send_t(r):
+        w = (32 * r, 32 * r + 32)
+        remote(part[r], v(R("tL", *w)), v(R("TU", *w)), [R("TU", *w)], "at%d" % r)
+
+    def send_y():
+        order("G", [R("YU", 0, 32)], [], True)
+        tr = []
+        for r in range(3):
+            rid, pid, _ = topo.addr(part[r])
+            tr.append(RemoteDMATransfer(dst_ids=[DstId(rid=rid, pnc=pid)], remote_sem=T.sem["ay%d" % r], src=v(R("YU", 0, 32)),
+                                        dma_engine_mask=some(engs(core, part[r])[cut[r][0]:cut[r][1]]), dst=v(R("yL", 32 * r, 32 * r + 32))))
+            loc[0] += cut[r][1] - cut[r][0]
+        g.remote_dma_fused(tr, local_sem=T.sem.loc)
+
+    emit("G", lambda: g.affine_select(v(R("idn")), v(R("hf")), [[-1, 128]], op.is_equal, 0.0, 0, 1), [R("hf")], [R("idn")])
+    def table(n, o, s, items):
+        for a, pat, base in items:
+            m = 1
+            for _, c in pat:
+                m *= c
+            iota(R(n, o + s * a, o + s * (a + m - 1) + 1, s), pat, base - 256 if n == "TB" else base)
+    one = [[0, 1]]
+    table("TB", 0, 4, [(0, [[0, 2], [16, 8]], 127), (23, [[0, 2], [16, 4]], 63), (19, [[0, 2], [16, 2]], 31), (31, one, 271)])
+    table("TB", 1, 4, [(0, [[0, 4], [16, 4]], 63), (23, [[0, 4], [16, 2]], 31)])
+    table("TB", 2, 4, [(0, [[0, 8], [16, 2]], 31)])
+    up = [(0, [[0, 2], [1, 8]], 23), (23, [[0, 2], [1, 4]], 19), (19, [[0, 2], [1, 2]], 17)]
+    table("PS", 0, 4, [(0, [[2, 2], [0, 8]], -1), (23, [[2, 2], [0, 4]], -1), (19, [[2, 2], [0, 2]], -1), (17, [[2, 2]], -1), (31, one, 1)])
+    table("PS", 1, 4, [(0, [[0, 2], [2, 2], [0, 4]], -1), (23, [[0, 2], [2, 2], [0, 2]], -1), (19, [[0, 2], [2, 2]], -1)])
+    table("PS", 2, 4, [(0, [[0, 4], [2, 2], [0, 2]], -1), (23, [[0, 4], [2, 2]], -1)])
+    table("PS", 3, 4, [(0, [[0, 8], [2, 2]], -1)])
+    table("TB", 128, 4, [(0, [[1, 32]], 0)])
+    table("TB", 129, 4, up)
+    table("TB", 130, 4, [(0, [[0, 4], [1, 4]], 19), (23, [[0, 4], [1, 2]], 17)])
+    table("TB", 131, 4, [(0, [[0, 8], [1, 2]], 17)])
+    table("TB", 256, 1, up + [(16, one, 32), (31, one, 32)])
+    iota(R("JC"), [[16, 32]], 400, 1)
+    for b in range(4):
+        act(R("EB", 512 * b + b, 512 * b + 512, 4), R("idn"))
+
+    def yrep(r):
+        act(R("YR", 512 * r, 512 * r + 512), R("iC"), ind=R("yL", 32 * r, 32 * r + 32))
+
+    def unpack(r, t):
+        mm(1 + t, C, R("eq", 128 * t, 128 * t + 128), R("es", 128 * t, 128 * t + 128), R("xq", C * r, C * r + C), R("xs", C * r, C * r + C))
+        if FQ[r][t] == "V":
+            tc(R("fb", C * t, C * t + C), R("ps%d" % (1 + t), 0, C))
+        else:
+            act(R("fb", C * t, C * t + C), R("ps%d" % (1 + t), 0, C))
+
+    def above(t):
+        act(R("bb", C * t, C * t + C), R("fb", C * t, C * t + C), ind=R("paU"))
+
+    def level(l):
+        n, at, o = 2 << l, (2 << l) - 2, 16 * ((2 << l) - 2)
+        w = dist(R("Nc", 0, 768), R("LL", at, at + n), 16 * n, "SB2", o)
+        at += n
+        ts(R("LL", at, at + n), w, 2.0, 512.0, op.mult, op.add)
+        ts(R("LL", at + n, at + 2 * n), w, 2.0, 513.0, op.mult, op.add)
+
+    tc(R("UL"), R("ULi"))
+    ts(R("NK", 0, 5), R("rN", 0, 5), q_, -1.0, op.is_gt, op.mult)
+    tt(R("eqm"), R("rL"), R("KF", 0, 16), op.is_equal)
+    tt(R("OH"), R("NK", 0, 4), R("NK", 1, 5), op.subtract)
+    quant(R("uq"), R("us"), R("ub"))
+    act(R("ups"), R("us"), ind=R("UL"))
+    emit("V", lambda: g.vector.tensor_copy(v(R("upq")).bitcast(dt.uint32), v(R("uq")).bitcast(dt.uint32).indirect(v(R("UL")))),
+         [R("uq"), R("UL")], [R("upq")])
+    tt(R("sx"), R("bh"), R("rA"), op.mult)
+    ts(R("ow"), R("rK"), q_, -1.0, op.is_gt, op.mult)
+    tt(R("C0", 240, 256), R("eqm"), R("sx"), op.mult)
+    pack_x(0, "xb")
+    score(0, 0)
+    score(0, 1)
+    quant(R("eq"), R("es"), R("EB"))
+    tt(R("C0", 256, 272), R("C0", 240, 256), R("ow"), op.mult)
+    ts(R("C0", 256, 257), R("AD", 0, 1), -256.0, None, op.mult)
+    for t in range(4):
+        unpack(0, t)
+    layer(0)
+    for t in range(4):
+        above(t)
+    w = dist(R("sg", 0, 400), R("paU"), C)
+    tt(R("sw"), w, R("sh"), op.mult)
+    tt(R("s24"), R("sb"), R("sw"), op.subtract)
+    tc(R("stU"), R("s24"))
+    tc(R("Nc"), R("iC", 0, 384), oind=R("stU"))
+    for k in range(4):
+        tt(R("GM", 0, 16), R("Nc", 0, 768), R("mk", 0, 16), op.mult, R("LT", 2 * k, 2 * k + 1))
+        slip()
+        total(R("ys", k + 1, k + 2), R("GM", 0, 16))
+        slip()
+        if k < 3:
+            ts(R("LT", 2 * k + 2, 2 * k + 3), R("ys", k + 1, k + 2), 2.0, R("AD", k + 3, k + 4), op.mult, op.add)
+        if k == 1:
+            pack_h(0, 0)
+            pack_h(0, 1)
+            send_h(0, 0)
+            send_s(0)
+            send_h(0, 1)
+    ts(R("LL", 0, 2), R("H2"), R("ys", 4, 5), 2.0, op.add, op.mult)
+    rest.extend([
+        lambda: tt(R("t4", 0, 4), R("OH"), R("ys", 0, 4), op.mult),
+        lambda: ts(R("YU", 16, 17), R("ys", 4, 5), 256.0, None, op.add),
+    ])
+    slip()
+    level(0)
+    rest.extend([
+        lambda: total(R("rd", 0, 1), R("t4", 0, 4)),
+        lambda: tt(R("st4", 0, 4), R("ys", 0, 4), R("ys", 1, 5), op.is_equal),
+        lambda: ts(R("YU", 31, 32), R("rd", 0, 1), R("AD", 2, 3), None, op.add),
+        lambda: total(R("rd", 1, 2), R("st4", 0, 4)),
+        lambda: tt(R("t4", 4, 8), R("st4", 0, 4), R("NK", 1, 5), op.mult),
+        lambda: ts(R("YU", 32, 33), R("rd", 0, 1), R("AD", 2, 3), None, op.add),
+        lambda: total(R("rd", 2, 3), R("t4", 4, 8)),
+    ])
+    level(1)
+    level(2)
+    act(R("GA", 0, 256), R("Nc", 0, 768), ind=R("LL", 14, 30))
+    ts(R("YU", 17, 31), R("SB2", 15, 224, 16), 256.0, None, op.add)
+    while rest:
+        slip()
+    hold(R("YU", 0, 16), 256, R("GA", 0, 256))
+    send_y()
+    hold(R("PL"), 288, R("TB"))
+    yrep(0)
+
+    def turned(r):
+        c0, c1 = ("C0", "C1") if r == 1 else ("C1", "C0")
+        tt(R(c1), R("sg"), R(c0), op.mult, R("YU", 16, 33))
+        scan(R("SC"), 272, R(c1))
+        pack_h(r, 0)
+        tt(R("P1"), R("SC"), R("PS"), op.mult, R("PL", 0, 8))
+        scan(R("P4"), 128, R("P1"), "R4")
+        ts(R("TU", 32 * r, 32 * r + 32), R("P4", 3, 128, 4), 256.0, R("SC", 255, 256), op.add, op.add)
+        pack_h(r, 1)
+        send_h(r, 0)
+        send_t(r)
+        send_s(r)
+        send_h(r, 1)
+
+    def trep(r):
+        act(R("Tr"), R("iC"), ind=R("TU", 32 * r, 32 * r + 32))
+
+    def hlist(r):
+        w = dist(R("Tr"), R("NP"), C)
+        ts(R("HL", 24 * r, 24 * r + 24), w, 256.0, None, op.add)
+
+    def arrived(r):
+        for k, (a, b) in enumerate(HC):
+            for t in range(4):
+                bk = HB[1 - k][t]
+                mm(bk, b - a, R("eq", 128 * t, 128 * t + 128), R("es", 128 * t, 128 * t + 128),
+                   R("hL", C * r + a, C * r + b), R("hP", C * r + a, C * r + b))
+                act(R("ab", C * t + a, C * t + b), R("ps%d" % bk, 0, b - a))
+
+    def maps(r):
+        tc(R("Z"), R("YR", 512 * r, 512 * r + 512), oind=R("tL", 32 * r, 32 * r + 32))
+        w = dist(R("Z"), R("HL", 24 * r, 24 * r + 24), C)
+        ts(R("MU", 24 * r, 24 * r + 24), w, 256.0, None, op.add)
+
+    def renew(r):
+        for t in range(4):
+            tt(R("xn", t, 1536, 4), R("ab", C * t, C * t + C), R("bb", C * t, C * t + C), op.add, R("MU", 24 * r, 24 * r + 24))
+        pack_x(r + 1, "xn")
+
+
+    tc(R("Yd", 0, 32), R("YU", 0, 32))
+    tc(R("Ye"), R("YU", 0, 32))
+    tt(R("s1"), R("Yd"), R("Ye"), op.is_equal, R("PL", 16, 18))
+    tc(R("s5"), R("s1"), ind=R("PL", 8, 16))
+    scan(R("s6"), 128, R("s5"), "R4")
+    tt(R("s6", 127, 128), R("s6", 127, 128), R("rd", 2, 3), op.add)
+    ts(R("s4"), R("s6", 3, 128, 4), R("rd", 1, 2), 1.0, op.add, op.min)
+    tt(R("s2"), R("JC"), R("s4"), op.mult)
+    tt(R("s1"), R("s2"), R("Yd", 0, 32), op.max)
+    tc(R("oU"), R("s1"))
+    tc(R("inv"), R("iC"), oind=R("oU"))
+    hold(R("NP"), C, R("inv", 0, C))
+    arrived(0)
+    yrep(1)
+    yrep(2)
+    w = dist(R("YR", 0, 512), R("NP"), C)
+    ts(R("MU", 0, 24), w, 256.0, None, op.add)
+    renew(0)
+    for r in (1, 2):
+        score(r, 0)
+        score(r, 1)
+        layer(r)
+        turned(r)
+        if r == 1:
+            quant(R("vq"), R("vs"), R("vb"))
+        trep(r)
+        for t in range(4):
+            if t == 3:
+                hlist(r)
+            unpack(r, t)
+        for t in range(4):
+            above(t)
+        arrived(r)
+        maps(r)
+        if r == 2:
+            act(R("mr"), R("Z"), AF.Identity, ind=R("HL", 48, 72), bias=256.0)
+            dma("Y", T.im[:, :], T.mr[0:128:16, 0:C], [R("mr")], [])
+        renew(r)
+    for k, (a, b) in enumerate(CH):
+        q3, s3 = R("xq", 3 * C + a, 3 * C + b), R("xs", 3 * C + a, 3 * C + b)
+        mm((0, 7)[k], b - a, R("vq"), R("vs"), q3, s3)
+        act(R("yb", a, b), R("ps%d" % (0, 7)[k], 0, b - a))
+        dma("Y", T.oc[:, 4 * a:4 * b], b8(q3), [q3], [])
+        dma("A", T.y[:, a:b], v(R("yb", a, b)), [R("yb", a, b)], [])
+    for k in range(4):
+        dma("Y", T.osc[4 * k:4 * k + 4, :], T.xs[32 * k:32 * k + 4, 3 * C:4 * C], [R("xs", 3 * C, 4 * C)], [])
+    for q, s in dmas:
+        wait(q, (s, 16))
+    for q in ("V", "A", "T", "G"):
+        g.wait_ge(T.sem["c" + q], cnt[q])
+    g.wait_ge(T.sem.loc, loc[0])

@@ -4,36 +4,40 @@ from concourse.mybir import dt, AluOpType, AxisListType, ActivationFunctionType 
 C = 384
 CH = [(0, 192), (192, 384)]
 HC = [(0, 128), (128, 384)]
-FQ = ["AAAA", "AVVV", "AVVV"]
+LAST = [(0, 256), (256, 384)]
+FQ = ["AAAA", "VVAA", "VVAA"]
+CFG = {"ga": 1, "ac": 0}
 SCRATCH = {
-    "KX": ("sbuf", [128, 32], "int32"), "KF": ("sbuf", [128, 32], "float32"), "tm": ("sbuf", [128, 128], "int32"),
-    "AD": ("sbuf", [128, 8], "float32"), "rL": ("sbuf", [128, 16], "float32"), "rA": ("sbuf", [128, 16], "float32"),
-    "rK": ("sbuf", [128, 16], "float32"), "rN": ("sbuf", [128, 8], "float32"), "bh": ("sbuf", [128, 16], "float32"),
-    "eqm": ("sbuf", [128, 16], "float32"), "sx": ("sbuf", [128, 16], "float32"), "ow": ("sbuf", [128, 16], "float32"),
-    "NK": ("sbuf", [128, 8], "float32"), "OH": ("sbuf", [128, 4], "float32"), "H2": ("sbuf", [128, 2], "float32"),
-    "iC": ("sbuf", [128, 512], "bfloat16"), "mk": ("sbuf", [128, 512], "bfloat16"), "R0": ("sbuf", [128, 512], "bfloat16"),
-    "TB": ("sbuf", [128, 288], "float32"), "MX": ("sbuf", [128, 384], "bfloat16"), "SF": ("sbuf", [128, 384], "float32"),
-    "R4": ("sbuf", [128, 128], "bfloat16"), "GA": ("sbuf", [128, 384], "bfloat16"), "SB2": ("sbuf", [128, 224], "bfloat16"),
-    "PL": ("sbuf", [128, 18], "uint16"), "PS": ("sbuf", [128, 128], "bfloat16"), "Ye": ("sbuf", [128, 32], "float32"),
-    "s5": ("sbuf", [128, 128], "float32"), "s6": ("sbuf", [128, 128], "float32"),
-    "ULi": ("sbuf", [128, 8], "int32"),
-    "UL": ("sbuf", [128, 8], "uint16"), "JC": ("sbuf", [128, 32], "float32"), "hf": ("sbuf", [128, 128], "bfloat16"),
-    "idn": ("sbuf", [128, 128], "bfloat16"), "EB": ("sbuf", [128, 2048], "bfloat16"),
+    "tm": ("sbuf", [128, 128], "int32"), "t2": ("sbuf", [128, 128], "int32"), "KX": ("sbuf", [128, 2], "int32"),
+    "KF": ("sbuf", [128, 2], "float32"), "AD": ("sbuf", [128, 16], "float32"), "ULi": ("sbuf", [128, 8], "int32"),
+    "UL": ("sbuf", [128, 8], "uint16"), "idn": ("sbuf", [128, 128], "bfloat16"), "EB": ("sbuf", [128, 2048], "bfloat16"),
     "eq": ("sbuf", [128, 512], "float8_e4m3fn_x4"), "es": ("sbuf", [128, 512], "uint8"),
+    "i2": ("sbuf", [128, 400], "bfloat16"), "iC": ("sbuf", [128, 512], "bfloat16"), "mk": ("sbuf", [128, 384], "bfloat16"),
+    "R0": ("sbuf", [128, 384], "bfloat16"), "R4": ("sbuf", [128, 128], "bfloat16"), "R5": ("sbuf", [128, 80], "float32"),
+    "MX": ("sbuf", [128, 256], "bfloat16"), "TB": ("sbuf", [128, 336], "float32"), "SF": ("sbuf", [128, 256], "float32"),
+    "PL": ("sbuf", [128, 22], "uint16"), "PF": ("sbuf", [128, 2], "float32"), "PS": ("sbuf", [128, 128], "bfloat16"),
+    "mW": ("sbuf", [128, 128], "bfloat16"), "lb": ("sbuf", [128, 32], "float32"),
+    "l32": ("sbuf", [128, 32], "float32"), "ad": ("sbuf", [128, 32], "float32"), "sn": ("sbuf", [128, 32], "float32"),
+    "sl": ("sbuf", [128, 32], "float32"), "AM": ("sbuf", [128, 48], "bfloat16"), "JC": ("sbuf", [128, 80], "float32"),
+    "VR": ("sbuf", [128, 256], "bfloat16"),
     "seI": ("sbuf", [128, 24], "int32"), "paI": ("sbuf", [128, 24], "int32"), "paU": ("sbuf", [128, 24], "uint16"),
     "slI": ("sbuf", [128, 24], "int32"), "sh": ("sbuf", [128, 24], "float32"), "sb": ("sbuf", [128, 24], "float32"),
     "sw": ("sbuf", [128, 24], "float32"), "s24": ("sbuf", [128, 24], "float32"), "stU": ("sbuf", [128, 24], "uint16"),
+    "sp": ("sbuf", [128, 24], "float32"),
     "xb": ("sbuf", [128, 1536], "bfloat16"), "ub": ("sbuf", [128, 512], "bfloat16"),
     "vb": ("sbuf", [128, 512], "bfloat16"), "wq": ("sbuf", [128, 512], "float8_e4m3fn_x4"), "wp": ("sbuf", [128, 512], "uint8"),
     "uq": ("sbuf", [128, 128], "float8_e4m3fn_x4"), "us": ("sbuf", [128, 128], "uint8"),
     "upq": ("sbuf", [128, 128], "float8_e4m3fn_x4"), "ups": ("sbuf", [128, 128], "uint8"),
     "vq": ("sbuf", [128, 128], "float8_e4m3fn_x4"), "vs": ("sbuf", [128, 128], "uint8"),
-    "Nc": ("sbuf", [128, 784], "bfloat16"), "LT": ("sbuf", [128, 8], "uint16"), "LL": ("sbuf", [128, 32], "uint16"),
-    "ys": ("sbuf", [128, 8], "float32"), "st4": ("sbuf", [128, 8], "float32"), "t4": ("sbuf", [128, 8], "float32"),
-    "rd": ("sbuf", [128, 8], "float32"), "GM": ("sbuf", [128, 512], "bfloat16"), "SB": ("sbuf", [128, 512], "bfloat16"),
-    "YU": ("sbuf", [128, 34], "uint16"), "Yd": ("sbuf", [128, 40], "float32"), "s1": ("sbuf", [128, 32], "float32"),
-    "s2": ("sbuf", [128, 32], "float32"), "s3": ("sbuf", [128, 32], "float32"), "s4": ("sbuf", [128, 32], "float32"),
-    "oU": ("sbuf", [128, 32], "uint16"), "inv": ("sbuf", [128, 1024], "bfloat16"), "NP": ("sbuf", [128, 24], "uint16"),
+    "Nc": ("sbuf", [128, 784], "bfloat16"), "L": ("sbuf", [128, 114], "uint16"), "Lf": ("sbuf", [128, 114], "float32"),
+    "LL": ("sbuf", [128, 32], "uint16"), "g16": ("sbuf", [128, 16], "float32"), "yt": ("sbuf", [128, 2], "float32"),
+    "GM": ("sbuf", [128, 384], "bfloat16"), "SB": ("sbuf", [128, 384], "bfloat16"), "SB2": ("sbuf", [128, 256], "bfloat16"),
+    "GA": ("sbuf", [128, 256], "bfloat16"), "YB": ("sbuf", [128, 34], "uint16"), "TR": ("sbuf", [128, 48], "bfloat16"),
+    "eT": ("sbuf", [128, 48], "bfloat16"), "gT": ("sbuf", [128, 48], "bfloat16"), "EW": ("sbuf", [128, 36], "float32"),
+    "TQ": ("sbuf", [128, 16], "bfloat16"), "PW": ("sbuf", [128, 16], "float32"),
+    "P5": ("sbuf", [128, 80], "float32"), "S5": ("sbuf", [128, 80], "float32"), "oU": ("sbuf", [128, 16], "uint16"),
+    "inv": ("sbuf", [128, 768], "bfloat16"), "n1": ("sbuf", [128, 24], "float32"), "n2": ("sbuf", [128, 24], "float32"),
+    "n3": ("sbuf", [128, 24], "float32"), "NP": ("sbuf", [128, 24], "uint16"),
     "sg": ("sbuf", [128, 400], "bfloat16"), "C0": ("sbuf", [128, 272], "bfloat16"), "C1": ("sbuf", [128, 272], "bfloat16"),
     "SC": ("sbuf", [128, 272], "bfloat16"), "P1": ("sbuf", [128, 128], "bfloat16"), "P4": ("sbuf", [128, 128], "bfloat16"),
     "TU": ("sbuf", [128, 96], "uint16"), "Tr": ("sbuf", [128, 512], "bfloat16"),
@@ -85,7 +89,7 @@ def rank_program(g, core, T, topo):
         for k, n in list(snap.get(tok, {}).items()) + [tok]:
             know[q][k] = max(know[q].get(k, 0), n)
 
-    def order(q, rd, wr, dma=False):
+    def order(q, rd, wr):
         need = {}
         for r, w in [(r, False) for r in rd] + [(r, True) for r in wr]:
             bank = r[0].startswith("ps")
@@ -117,7 +121,7 @@ def rank_program(g, core, T, topo):
         record(q, rd, wr, ("c" + q, cnt[q]))
 
     def dma(q, out, in_, rd, wr):
-        order(q, rd, wr, True)
+        order(q, rd, wr)
         s = "d%d" % len(dmas)
         dmas.append((q, s))
         eng[q].dma_start(out, in_).then_inc(T.sem[s], 16)
@@ -126,35 +130,44 @@ def rank_program(g, core, T, topo):
     def sc(x):
         return v(x) if isinstance(x, tuple) else x
 
-    def tt(out, a, b, o, ind=None):
-        emit("V", lambda: g.vector.tensor_tensor(v(out), v(a).indirect(v(ind)) if ind else v(a), v(b), o), [a, b, ind], [out])
+    def via(a, ind):
+        return v(a).indirect(v(ind)) if ind else v(a)
 
-    def ts(out, a, s1, s2, o1, o2=None):
+    def tt(out, a, b, o, ind=None):
+        emit("V", lambda: g.vector.tensor_tensor(v(out), via(a, ind), v(b), o), [a, b, ind], [out])
+
+    def ts(out, a, s1, s2, o1, o2=None, ind=None):
         if o2 is None:
-            emit("V", lambda: g.vector.tensor_scalar(v(out), v(a), sc(s1), None, o1), [a, s1], [out])
+            emit("V", lambda: g.vector.tensor_scalar(v(out), via(a, ind), sc(s1), None, o1), [a, s1, ind], [out])
         else:
-            emit("V", lambda: g.vector.tensor_scalar(v(out), v(a), sc(s1), sc(s2), o1, o2), [a, s1, s2], [out])
+            emit("V", lambda: g.vector.tensor_scalar(v(out), via(a, ind), sc(s1), sc(s2), o1, o2), [a, s1, s2, ind], [out])
 
     def tc(out, a, ind=None, oind=None):
-        emit("V", lambda: g.vector.tensor_copy(v(out).indirect(v(oind)) if oind else v(out), v(a).indirect(v(ind)) if ind else v(a)),
-             [a, ind, oind], [out])
+        emit("V", lambda: g.vector.tensor_copy(via(out, oind), via(a, ind)), [a, ind, oind], [out])
 
     def act(out, a, f=AF.Copy, ind=None, **k):
-        emit("A", lambda: g.scalar.activation(v(out), v(a).indirect(v(ind)) if ind else v(a), f, **k), [a, ind], [out])
+        kw = {n: sc(x) for n, x in k.items()}
+        emit("A", lambda: g.scalar.activation(v(out), via(a, ind), f, **kw), [a, ind] + list(k.values()), [out])
 
     def fill(out, x):
         emit("V", lambda: g.vector.memset(v(out), x), [], [out])
 
-    def total(out, a):
-        emit("V", lambda: g.vector.tensor_reduce(v(out), v(a), AxisListType.X, op.add), [a], [out])
+    def const(out, x):
+        n = len(range(out[1], out[2], out[3]))
+        act(out, R("i2", 0, n), AF.Identity, scale=0.0, bias=float(x))
 
-    def scan(out, n, a, z="R0"):
-        emit("V", lambda: g.vector.tensor_tensor_scan(v(out), v(R(z, 0, n)), v(a), 0.0, op.mult, op.add), [R(z, 0, n), a], [out])
+    def fold(out, a, o):
+        emit("V", lambda: g.vector.tensor_reduce(v(out), v(a), AxisListType.X, o), [a], [out])
 
-    def hold(out, n, a):
+    def scan(out, z, a, o=op.add):
+        emit("V", lambda: g.vector.tensor_tensor_scan(v(out), v(z), v(a), 0.0, op.mult, o), [z, a], [out])
+
+    def hold(a, n):
         f = R("SF", 0, n)
         emit("V", lambda: g.vector.tensor_tensor_scan(v(f), v(R("MX", 0, n)), v(a), 0.0, op.add, op.max), [R("MX", 0, n), a], [f])
-        ts(out, R("SF", 15, n, 16), R("AD", 6, 7), None, op.add)
+
+    def held(out, a, b, k):
+        ts(out, R("SF", 16 * a + 15, 16 * b, 16), R("AD", k, k + 1), None, op.add)
 
     def quant(q, s, a):
         emit("V", lambda: g.vector.quantize_mx(v(q), v(s), v(a)), [a], [q, s])
@@ -167,136 +180,61 @@ def rank_program(g, core, T, topo):
         kw = {} if SCRATCH[out[0]][2] == "int32" else {"allow_small_or_imprecise_dtypes": True}
         emit("G", lambda: g.iota(v(out), pat, base, cm, **kw), [], [out])
 
+    def table(n, o, s, items):
+        for a, pat, base in items:
+            m = 1
+            for _, c in pat:
+                m *= c
+            iota(R(n, o + s * a, o + s * (a + m - 1) + 1, s), pat, base)
+
     rest = []
 
-    def slip():
-        if rest:
-            rest.pop(0)()
+    def slip(n=1):
+        for _ in range(n):
+            if rest:
+                rest.pop(0)()
 
     def dist(win, ind, n, o="SB", a=0):
         tt(R("GM", 0, n), win, R("mk", 0, n), op.mult, ind)
         slip()
-        scan(R(o, a, a + n), n, R("GM", 0, n))
+        scan(R(o, a, a + n), R("R0", 0, n), R("GM", 0, n))
         slip()
         return R(o, a + 15, a + n, 16)
 
     def b8(r):
         return v(r).bitcast(dt.uint8)
 
-    dma("Y", v(R("seI")), T.se[:, :], [], [R("seI")])
     dma("Y", v(R("ub")), T.u[:, :], [], [R("ub")])
-    for a, b in CH:
-        dma("Y", v(R("xb", 4 * a, 4 * b)), T.x[:, 4 * a:4 * b], [], [R("xb", 4 * a, 4 * b)])
+    for q, (a, b) in zip("YA", CH):
+        dma(q, v(R("xb", 4 * a, 4 * b)), T.x[:, 4 * a:4 * b], [], [R("xb", 4 * a, 4 * b)])
+    dma("A", v(R("seI")), T.se[:, :], [], [R("seI")])
     dma("Y", b8(R("wq")), T.wc[:, :], [], [R("wq")])
     dma("Y", v(R("wp")), T.ws[:, :], [], [R("wp")])
     dma("Y", v(R("vb")), T.v[:, :], [], [R("vb")])
     part = [T.cores[rank ^ s] for s in (1, 2, 3)]
-
-    def engs(a, b):
-        return topo.engines(a, b)
 
     def some(e):
         m = 0
         for k in e:
             m |= 1 << k
         return m
-    cut = [(0, 4), (4, 6), (6, 8)]
+
+    def tree_engines(a, b):
+        return topo.engines(a, b)[-8:]
     for r in range(3):
-        n = len(engs(part[r], core))
-        acc.setdefault("yL", []).append((R("yL", 32 * r, 32 * r + 32), True, "R", ("ay%d" % r, cut[r][1] - cut[r][0])))
+        n = len(topo.engines(part[r], core))
+        acc.setdefault("yL", []).append((R("yL", 32 * r, 32 * r + 32), True, "R", ("ay%d" % r, len(tree_engines(part[r], core)))))
         acc.setdefault("tL", []).append((R("tL", 32 * r, 32 * r + 32), True, "R", ("at%d" % r, n)))
         acc.setdefault("hP", []).append((R("hP", C * r, C * r + C), True, "R", ("as%d" % r, n)))
         for k, (a, b) in enumerate(HC):
             acc.setdefault("hL", []).append((R("hL", C * r + a, C * r + b), True, "R", ("ah%d_%d" % (r, k), n)))
 
-    iota(R("KX"), [[0, 32]], 0, 1)
-    iota(R("iC", 0, 384), [[1, 384]], -256)
-    iota(R("tm"), [[0, 8], [1, 16]], 0, -1)
-    iota(R("ULi"), [[16, 8]], 0)
-    for a, n in ((0, 2), (2, 2), (4, 4), (8, 8)):
-        iota(R("rL", a, a + n), [[1, n]], 0 if a else -1)
-        iota(R("rA", a, a + n), [[0, n]], 256 // max(a, 1))
-        iota(R("rK", a, a + n), [[0, n]], 2 * max(a, 1))
-    for a, n, w in ((0, 2, 1), (2, 2, 4), (4, 1, 16)):
-        iota(R("rN", a, a + n), [[w, n]], w)
-    iota(R("iC", 384, 512), [[1, 128]], 128)
-    fill(R("hf"), 0.5)
-    fill(R("R0"), 1.0)
-    fill(R("R0", 0, 512, 16), 0.0)
-    fill(R("PS"), 0.0)
-    fill(R("TB", 0, 128), -241.0)
-    fill(R("TB", 128, 288), -240.0)
-    fill(R("R4"), 1.0)
-    fill(R("R4", 0, 128, 4), 0.0)
-    for a, b, m in ((0, 2, 0), (2, 4, 1), (4, 8, 3), (8, 16, 7), (16, 17, 15), (17, 18, 1)):
-        ts(R("KX", a, b), R("KX", a, b), m, None, op.bitwise_and)
-    for k in range(1, 4):
-        w = R("KX", 16 + 2 ** k, 16 + 2 ** (k + 1))
-        ts(w, w, k, 1, op.logical_shift_right, op.bitwise_and)
-    tc(R("KF"), R("KX"))
-    q_ = R("KF", 16, 17)
-
-    def bit(k):
-        return R("KF", 16 + 2 ** k, 17 + 2 ** k)
-    ts(R("AD", 0, 1), q_, 0.0, None, op.is_equal)
-    ts(R("tm"), R("tm"), 15, None, op.bitwise_and)
-    ts(R("mk", 0, 128), R("tm"), 0.0, None, op.is_equal)
-    tc(R("LT", 0, 1), bit(0))
-    act(R("Nc", 0, 768, 2), R("iC", 0, 384))
-    act(R("Nc", 1, 768, 2), R("iC", 0, 384))
-    act(R("AD", 1, 2), R("AD", 0, 1), AF.Identity, scale=768.0)
-    act(R("AD", 2, 3), R("AD", 0, 1), AF.Identity, scale=128.0, bias=256.0)
-    for k in range(1, 4):
-        act(R("AD", 2 + k, 3 + k), bit(k), AF.Identity, bias=512.0)
-    act(R("mk", 128, 256), R("mk", 0, 128))
-    act(R("mk", 256, 512), R("mk", 0, 256))
-    act(R("AD", 6, 7), q_, AF.Identity, scale=512.0, bias=-7424.0)
-    act(R("MX"), R("mk", 0, 384), AF.Identity, scale=-33280.0, bias=512.0)
-    act(R("ys", 0, 1), q_, AF.Identity, scale=0.0, bias=-256.0)
-    act(R("H2", 0, 1), q_, AF.Identity, scale=0.0, bias=256.0)
-    act(R("H2", 1, 2), q_, AF.Identity, scale=0.0, bias=256.5)
-    act(R("sg", 384, 400), R("KF", 0, 16), AF.Identity, scale=0.0, bias=1.0)
-    act(R("Yd", 32, 40), R("KF", 0, 8), AF.Identity, scale=0.0, bias=1000.0)
-    act(R("bh"), R("KF", 16, 32), AF.Identity, bias=-0.5)
-    for m, n, w in ((0, 1, 8.0), (1, 2, 4.0), (3, 4, 2.0), (7, 8, 1.0)):
-        act(R("C0", 16 * m, 16 * (m + n)), R("mk", 16 * m, 16 * (m + n)), AF.Identity, scale=w)
-    ts(R("paI"), R("seI"), 1, None, op.arith_shift_right)
-    ts(R("slI"), R("seI"), 1, None, op.bitwise_and)
-    tc(R("paU"), R("paI"))
-    ts(R("sh"), R("slI"), -1.0, 0.5, op.mult, op.add)
-    tt(R("sb"), R("seI"), R("sh"), op.add)
-    ts(R("sb", 0, 1), R("sb", 0, 1), R("AD", 1, 2), None, op.add)
-    fill(R("EB"), 0.0)
-
-    def score(r, k):
-        a, b = CH[k]
-        bank = (0, 7)[k]
-        mm(bank, b - a, R("upq"), R("ups"), R("xq", C * r + a, C * r + b), R("xs", C * r + a, C * r + b))
-        act(R("sg", a, b), R("ps%d" % bank, 0, b - a), AF.Sign, bias=2.0 ** -93)
-
-    def pack_x(r, src):
-        for k, (a, b) in enumerate(CH):
-            quant(R("xq", C * r + a, C * r + b), R("xs", C * r + a, C * r + b), R(src, 4 * a, 4 * b))
-
-    HB = [[1, 2, 3, 4], [5, 6, 0, 7]]
-
-    def layer(r):
-        for k, (a, b) in enumerate(HC):
-            for t in range(4):
-                mm(HB[k][t], b - a, R("wq", 128 * t, 128 * t + 128), R("wp", 128 * t, 128 * t + 128),
-                   R("xq", C * r + a, C * r + b), R("xs", C * r + a, C * r + b))
-                act(R("hb", 4 * a + t, 4 * b, 4), R("ps%d" % HB[k][t], 0, b - a), scale=0.03125)
-
-    def pack_h(r, k):
-        a, b = HC[k]
-        quant(R("hq", C * r + a, C * r + b), R("hs", C * r + a, C * r + b), R("hb", 4 * a, 4 * b))
-
-    def remote(dst, out, in_, rd, sem):
-        order("G", rd, [], True)
+    def remote(dst, out, in_, rd, sem, e=None):
+        order("G", rd, [])
+        e = e or topo.engines(core, dst)
         rid, pid, _ = topo.addr(dst)
-        g.remote_dma(out_ap=out, in_ap=in_, remote_sem=T.sem[sem], local_sem=T.sem.loc, pid=pid, routing_id=rid,
-                     dma_engine_mask=topo.mask(core, dst))
-        loc[0] += len(engs(core, dst))
+        g.remote_dma(out_ap=out, in_ap=in_, remote_sem=T.sem[sem], local_sem=T.sem.loc, pid=pid, routing_id=rid, dma_engine_mask=some(e))
+        loc[0] += len(e)
 
     def send_h(r, k):
         a, b = C * r + HC[k][0], C * r + HC[k][1]
@@ -310,211 +248,304 @@ def rank_program(g, core, T, topo):
         w = (32 * r, 32 * r + 32)
         remote(part[r], v(R("tL", *w)), v(R("TU", *w)), [R("TU", *w)], "at%d" % r)
 
-    def send_y():
-        order("G", [R("YU", 0, 32)], [], True)
-        tr = []
-        for r in range(3):
-            rid, pid, _ = topo.addr(part[r])
-            tr.append(RemoteDMATransfer(dst_ids=[DstId(rid=rid, pnc=pid)], remote_sem=T.sem["ay%d" % r], src=v(R("YU", 0, 32)),
-                                        dma_engine_mask=some(engs(core, part[r])[cut[r][0]:cut[r][1]]), dst=v(R("yL", 32 * r, 32 * r + 32))))
-            loc[0] += cut[r][1] - cut[r][0]
-        g.remote_dma_fused(tr, local_sem=T.sem.loc)
+    def send_y(r):
+        remote(part[r], v(R("yL", 32 * r, 32 * r + 32)), v(R("YB", 1, 33)), [R("YB", 1, 33)], "ay%d" % r, tree_engines(core, part[r]))
 
-    emit("G", lambda: g.affine_select(v(R("idn")), v(R("hf")), [[-1, 128]], op.is_equal, 0.0, 0, 1), [R("hf")], [R("idn")])
-    def table(n, o, s, items):
-        for a, pat, base in items:
-            m = 1
-            for _, c in pat:
-                m *= c
-            iota(R(n, o + s * a, o + s * (a + m - 1) + 1, s), pat, base - 256 if n == "TB" else base)
     one = [[0, 1]]
-    table("TB", 0, 4, [(0, [[0, 2], [16, 8]], 127), (23, [[0, 2], [16, 4]], 63), (19, [[0, 2], [16, 2]], 31), (31, one, 271)])
-    table("TB", 1, 4, [(0, [[0, 4], [16, 4]], 63), (23, [[0, 4], [16, 2]], 31)])
-    table("TB", 2, 4, [(0, [[0, 8], [16, 2]], 31)])
-    up = [(0, [[0, 2], [1, 8]], 23), (23, [[0, 2], [1, 4]], 19), (19, [[0, 2], [1, 2]], 17)]
-    table("PS", 0, 4, [(0, [[2, 2], [0, 8]], -1), (23, [[2, 2], [0, 4]], -1), (19, [[2, 2], [0, 2]], -1), (17, [[2, 2]], -1), (31, one, 1)])
-    table("PS", 1, 4, [(0, [[0, 2], [2, 2], [0, 4]], -1), (23, [[0, 2], [2, 2], [0, 2]], -1), (19, [[0, 2], [2, 2]], -1)])
-    table("PS", 2, 4, [(0, [[0, 4], [2, 2], [0, 2]], -1), (23, [[0, 4], [2, 2]], -1)])
-    table("PS", 3, 4, [(0, [[0, 8], [2, 2]], -1)])
-    table("TB", 128, 4, [(0, [[1, 32]], 0)])
-    table("TB", 129, 4, up)
-    table("TB", 130, 4, [(0, [[0, 4], [1, 4]], 19), (23, [[0, 4], [1, 2]], 17)])
-    table("TB", 131, 4, [(0, [[0, 8], [1, 2]], 17)])
-    table("TB", 256, 1, up + [(16, one, 32), (31, one, 32)])
-    iota(R("JC"), [[16, 32]], 400, 1)
-    for b in range(4):
-        act(R("EB", 512 * b + b, 512 * b + 512, 4), R("idn"))
+    iota(R("tm"), [[1, 128]], 0, -1)
+    iota(R("KX"), [[0, 2]], 0, 1)
+    iota(R("ULi"), [[16, 8]], 0)
+    iota(R("i2"), [[2, 400]], -384)
+    table("TB", 0, 1, [(0, [[-1, 2]], 113), (2, [[1, 2]], 0), (4, [[1, 4]], 30), (8, [[1, 2], [2, 4]], 76),
+                       (16, [[32, 2], [64, 4], [2, 2]], -384), (32, [[1, 8], [0, 2]], 1),
+                       (48, [[-92, 2]], 100), (50, [[8, 2]], 4), (52, [[4, 4]], 2), (56, [[2, 8]], 1),
+                       (64, [[0, 2], [1, 8], [0, 2]], 0), (96, [[1, 8], [0, 2]], 8), (112, [[0, 96]], 1)])
+    table("TB", 128, 5, [(0, [[1, 16]], 0)])
+    table("TB", 129, 5, [(2, [[1, 7], [0, 2]], 1)])
+    table("TB", 130, 5, [(4, [[1, 3], [0, 4]], 1)])
+    table("TB", 132, 5, [(0, [[1, 16]], 18)])
+    table("TB", 129, 1, [(0, [[0, 3]], 0)])
+    table("lb", 0, 1, [(0, [[7, 2]], 1), (2, [[0, 2]], 4), (4, [[0, 4]], 2), (8, [[0, 8]], 1)])
+    iota(R("JC"), [[16, 16], [0, 5]], 400, 1)
+    iota(R("JC", 4, 80, 5), [[0, 16]], 1)
+    iota(R("VR", 0, 16), [[2, 16]], -256)
+    iota(R("VR", 16, 256), [[32, 15], [1, 16]], -224)
+    iota(R("iC"), [[1, 512]], -256)
 
-    def yrep(r):
-        act(R("YR", 512 * r, 512 * r + 512), R("iC"), ind=R("yL", 32 * r, 32 * r + 32))
+    fill(R("EB", 0, 512), 0.0)
+    act(R("EB", 1536, 2048), R("EB", 0, 512))
+    fill(R("EB", 512, 1536), 0.0)
+    ts(R("idn"), R("tm"), 0.0, 0.5, op.is_equal, op.mult)
+    ts(R("t2"), R("tm"), 15, None, op.bitwise_and)
+    for b in range(4):
+        o = R("EB", 512 * b + b, 512 * b + 512, 4)
+        if b in (1, 2):
+            tc(o, R("idn"))
+        else:
+            act(o, R("idn"))
+    ts(R("mk", 0, 128), R("t2"), 0.0, None, op.is_equal)
+    ts(R("KX", 0, 1), R("KX", 0, 1), 15, None, op.bitwise_and)
+    ts(R("KX", 1, 2), R("KX", 1, 2), 1, None, op.bitwise_and)
+    tc(R("UL"), R("ULi"))
+    tc(R("KF"), R("KX"))
+    quant(R("eq"), R("es"), R("EB"))
+    q_, bit, q0 = R("KF", 0, 1), R("KF", 1, 2), R("mk", 0, 1)
+    quant(R("uq"), R("us"), R("ub"))
+    tc(R("ups"), R("us"), ind=R("UL"))
+    emit("V", lambda: g.vector.tensor_copy(v(R("upq")).bitcast(dt.uint32), v(R("uq")).bitcast(dt.uint32).indirect(v(R("UL")))),
+         [R("uq"), R("UL")], [R("upq")])
+    act(R("mk", 128, 256), R("mk", 0, 128))
+    act(R("mk", 256, 384), R("mk", 0, 128))
+    act(R("AD", 0, 1), q0, AF.Identity, scale=768.0, bias=0.5)
+    const(R("sg", 384, 400), 0.5)
+    const(R("R0"), 1)
+    const(R("R0", 0, 384, 16), 0)
+    act(R("AD", 4, 5), bit)
+    act(R("AD", 5, 6), bit, AF.Identity, bias=768.0)
+    act(R("MX"), R("mk", 0, 256), AF.Identity, scale=-33792.0, bias=1024.0)
+    act(R("AD", 1, 2), q_, AF.Identity, scale=1024.0, bias=-15360.0)
+    act(R("Nc", 0, 768, 2), R("i2", 0, 384))
+    act(R("Nc", 1, 768, 2), R("i2", 0, 384))
+    act(R("AD", 3, 4), bit, AF.Identity, bias=384.0)
+    const(R("AD", 6, 7), 384)
+    const(R("AD", 7, 8), 385)
+
+    def score(r):
+        for k, (a, b) in enumerate(CH):
+            mm(k, b - a, R("upq"), R("ups"), R("xq", C * r + a, C * r + b), R("xs", C * r + a, C * r + b))
+
+    def signs():
+        for k, (a, b) in enumerate(CH):
+            ts(R("sg", a, b), R("ps%d" % k, 0, b - a), 0.0, 0.5, op.is_ge, op.subtract)
+
+    def pack_x(r, src, pieces=CH):
+        for a, b in pieces:
+            quant(R("xq", C * r + a, C * r + b), R("xs", C * r + a, C * r + b), R(src, 4 * a, 4 * b))
+
+    HB = [[2, 3, 4, 5], [6, 7, 0, 1]]
+
+    def layer(r, k):
+        a, b = HC[k]
+        for t in range(4):
+            mm(HB[k][t], b - a, R("wq", 128 * t, 128 * t + 128), R("wp", 128 * t, 128 * t + 128),
+               R("xq", C * r + a, C * r + b), R("xs", C * r + a, C * r + b))
+            act(R("hb", 4 * a + t, 4 * b, 4), R("ps%d" % HB[k][t], 0, b - a), scale=0.03125)
+
+    def pack_h(r, k):
+        a, b = HC[k]
+        quant(R("hq", C * r + a, C * r + b), R("hs", C * r + a, C * r + b), R("hb", 4 * a, 4 * b))
 
     def unpack(r, t):
-        mm(1 + t, C, R("eq", 128 * t, 128 * t + 128), R("es", 128 * t, 128 * t + 128), R("xq", C * r, C * r + C), R("xs", C * r, C * r + C))
+        mm(2 + t, C, R("eq", 128 * t, 128 * t + 128), R("es", 128 * t, 128 * t + 128), R("xq", C * r, C * r + C), R("xs", C * r, C * r + C))
         if FQ[r][t] == "V":
-            tc(R("fb", C * t, C * t + C), R("ps%d" % (1 + t), 0, C))
+            tc(R("fb", C * t, C * t + C), R("ps%d" % (2 + t), 0, C))
         else:
-            act(R("fb", C * t, C * t + C), R("ps%d" % (1 + t), 0, C))
+            act(R("fb", C * t, C * t + C), R("ps%d" % (2 + t), 0, C))
 
     def above(t):
         act(R("bb", C * t, C * t + C), R("fb", C * t, C * t + C), ind=R("paU"))
 
-    def level(l):
-        n, at, o = 2 << l, (2 << l) - 2, 16 * ((2 << l) - 2)
-        w = dist(R("Nc", 0, 768), R("LL", at, at + n), 16 * n, "SB2", o)
-        at += n
-        ts(R("LL", at, at + n), w, 2.0, 512.0, op.mult, op.add)
-        ts(R("LL", at + n, at + 2 * n), w, 2.0, 513.0, op.mult, op.add)
+    def arrived(r, t):
+        bk = HB[1][t]
+        mm(bk, C, R("eq", 128 * t, 128 * t + 128), R("es", 128 * t, 128 * t + 128), R("hL", C * r, C * r + C), R("hP", C * r, C * r + C))
+        act(R("ab", C * t, C * t + C), R("ps%d" % bk, 0, C))
 
-    tc(R("UL"), R("ULi"))
-    ts(R("NK", 0, 5), R("rN", 0, 5), q_, -1.0, op.is_gt, op.mult)
-    tt(R("eqm"), R("rL"), R("KF", 0, 16), op.is_equal)
-    tt(R("OH"), R("NK", 0, 4), R("NK", 1, 5), op.subtract)
-    quant(R("uq"), R("us"), R("ub"))
-    act(R("ups"), R("us"), ind=R("UL"))
-    emit("V", lambda: g.vector.tensor_copy(v(R("upq")).bitcast(dt.uint32), v(R("uq")).bitcast(dt.uint32).indirect(v(R("UL")))),
-         [R("uq"), R("UL")], [R("upq")])
-    tt(R("sx"), R("bh"), R("rA"), op.mult)
-    ts(R("ow"), R("rK"), q_, -1.0, op.is_gt, op.mult)
-    tt(R("C0", 240, 256), R("eqm"), R("sx"), op.mult)
+    def yrep(r):
+        act(R("YR", 512 * r, 512 * r + 512), R("iC"), ind=R("yL", 32 * r, 32 * r + 32))
+
+    def renew(r, pieces=((0, C),)):
+        for a, b in pieces:
+            for t in range(4):
+                tt(R("xn", 4 * a + t, 4 * b, 4), R("ab", C * t, C * t + C), R("bb", C * t + a, C * t + b), op.add,
+                   R("MU", 24 * r + a // 16, 24 * r + b // 16))
+
     pack_x(0, "xb")
-    score(0, 0)
-    score(0, 1)
-    quant(R("eq"), R("es"), R("EB"))
-    tt(R("C0", 256, 272), R("C0", 240, 256), R("ow"), op.mult)
-    ts(R("C0", 256, 257), R("AD", 0, 1), -256.0, None, op.mult)
-    for t in range(4):
-        unpack(0, t)
-    layer(0)
-    for t in range(4):
-        above(t)
-    w = dist(R("sg", 0, 400), R("paU"), C)
+    score(0)
+    ts(R("paI"), R("seI"), 1, None, op.arith_shift_right)
+    ts(R("slI"), R("seI"), 1, None, op.bitwise_and)
+    tc(R("paU"), R("paI"))
+    signs()
+    ts(R("sh"), R("slI"), -2.0, 1.0, op.mult, op.add)
+    ts(R("sb", 1, 24), R("paI", 1, 24), 2.0, 0.5, op.mult, op.add)
+    ts(R("sb", 0, 1), R("paI", 0, 1), 2.0, R("AD", 0, 1), op.mult, op.add)
+    layer(0, 0)
+    layer(0, 1)
+    rest.extend([lambda: tc(R("L", 112, 114), R("AD", 4, 6))])
+    w = dist(R("sg"), R("paU"), C)
     tt(R("sw"), w, R("sh"), op.mult)
+    hold(R("TB", 0, 208), 208)
     tt(R("s24"), R("sb"), R("sw"), op.subtract)
+    ts(R("PF"), R("SF", 31, 64, 32), R("AD", 1, 2), None, op.add)
     tc(R("stU"), R("s24"))
-    tc(R("Nc"), R("iC", 0, 384), oind=R("stU"))
-    for k in range(4):
-        tt(R("GM", 0, 16), R("Nc", 0, 768), R("mk", 0, 16), op.mult, R("LT", 2 * k, 2 * k + 1))
-        slip()
-        total(R("ys", k + 1, k + 2), R("GM", 0, 16))
-        slip()
-        if k < 3:
-            ts(R("LT", 2 * k + 2, 2 * k + 3), R("ys", k + 1, k + 2), 2.0, R("AD", k + 3, k + 4), op.mult, op.add)
-        if k == 1:
-            pack_h(0, 0)
-            pack_h(0, 1)
-            send_h(0, 0)
-            send_s(0)
-            send_h(0, 1)
-    ts(R("LL", 0, 2), R("H2"), R("ys", 4, 5), 2.0, op.add, op.mult)
+    held(R("PL", 0, 13), 0, 13, 1)
+    tc(R("Nc"), R("i2", 0, 384), oind=R("stU"))
+    ts(R("mW"), R("i2", 0, 128), R("PF", 0, 1), -1024.0, op.not_equal, op.mult)
+    const(R("PW"), 0)
+    act(R("AD", 8, 10), R("AD", 6, 8), AF.Identity, scale=0.0, bias=R("AD", 4, 5))
+    act(R("AD", 12, 13), q_, AF.Identity, bias=0.5)
+    act(R("lb", 16, 32), R("lb", 0, 16))
+    act(R("AD", 10, 12), R("AD", 8, 10), AF.Identity, scale=-1.0)
+    act(R("ad", 0, 16), R("TB", 48, 64), AF.Abs, scale=-1.0, bias=R("PF", 1, 2))
+    act(R("ad", 16, 32), R("TB", 48, 64), AF.Abs, scale=-1.0, bias=R("AD", 12, 13))
+    act(R("AM", 32, 48), R("mk", 0, 16))
+    for t in range(2):
+        unpack(0, t)
+    const(R("R5"), 1)
+    const(R("EW", 34, 36), 0)
+    act(R("AD", 2, 3), q_, AF.Identity, scale=512.0, bias=-7488.0)
+    const(R("R5", 0, 80, 5), 0)
+    for t in range(2, 4):
+        unpack(0, t)
+    const(R("inv", 0, C), 0)
+    nc = R("Nc", 0, 768)
+    up = R("AD", 3, 4)
+    ts(R("L", 0, 16), nc, up, None, op.add, ind=R("L", 112, 113))
+    pack_h(0, 0)
+    send_h(0, 0)
+    ts(R("L", 16, 48), nc, up, None, op.add, ind=R("L", 0, 2))
+    ts(R("L", 48, 112, 2), nc, up, None, op.add, ind=R("L", 30, 32))
+    ts(R("L", 49, 112, 2), nc, up, None, op.add, ind=R("L", 32, 34))
+    pack_h(0, 1)
+    send_s(0)
+    send_h(0, 1)
+    tt(R("GM", 0, 128), nc, R("mW"), op.add, R("L", 76, 84))
+    tc(R("Lf"), R("L"))
+    y4 = R("SB2", 31, 32)
+    fold(y4, R("GM", 0, 128), op.max)
+    tt(R("g16"), R("Lf"), R("mk", 0, 16), op.mult, R("PL", 0, 1))
+    ts(R("LL", 2, 4), R("AD", 6, 8), y4, None, op.add)
     rest.extend([
-        lambda: tt(R("t4", 0, 4), R("OH"), R("ys", 0, 4), op.mult),
-        lambda: ts(R("YU", 16, 17), R("ys", 4, 5), 256.0, None, op.add),
+        lambda: fold(R("yt", 0, 1), R("g16"), op.add),
+        lambda: ts(R("YB", 2, 3), y4, 384.0, 0.5, op.add, op.mult),
+        lambda: ts(R("YB", 0, 2), R("AD", 10, 12), R("yt", 0, 1), 0.5, op.add, op.mult),
+        lambda: tt(R("AM", 0, 32), R("lb"), R("ad"), op.is_gt),
+        lambda: tc(R("TR"), R("i2"), ind=R("YB", 0, 3)),
+        lambda: tc(R("TQ"), R("i2"), ind=R("YB", 0, 1)),
+        lambda: tc(R("EW", 18, 20), R("YB", 1, 3)),
+        lambda: tt(R("eT"), R("TQ"), R("TR"), op.is_equal, R("PL", 4, 7)),
+        lambda: ts(R("PW", 1, 8), R("SB2", 31, 128, 16), 384.0, 0.5, op.add, op.mult),
+        lambda: tt(R("gT"), R("eT"), R("AM"), op.mult),
+        lambda: fold(R("EW", 0, 1), R("gT", 0, 16), op.max),
+        lambda: fold(R("EW", 1, 2), R("gT", 16, 48), op.max),
     ])
     slip()
-    level(0)
-    rest.extend([
-        lambda: total(R("rd", 0, 1), R("t4", 0, 4)),
-        lambda: tt(R("st4", 0, 4), R("ys", 0, 4), R("ys", 1, 5), op.is_equal),
-        lambda: ts(R("YU", 31, 32), R("rd", 0, 1), R("AD", 2, 3), None, op.add),
-        lambda: total(R("rd", 1, 2), R("st4", 0, 4)),
-        lambda: tt(R("t4", 4, 8), R("st4", 0, 4), R("NK", 1, 5), op.mult),
-        lambda: ts(R("YU", 32, 33), R("rd", 0, 1), R("AD", 2, 3), None, op.add),
-        lambda: total(R("rd", 2, 3), R("t4", 4, 8)),
-    ])
-    level(1)
-    level(2)
-    act(R("GA", 0, 256), R("Nc", 0, 768), ind=R("LL", 14, 30))
-    ts(R("YU", 17, 31), R("SB2", 15, 224, 16), 256.0, None, op.add)
-    while rest:
+    for n in (2, 4, 8):
+        w = dist(nc, R("LL", n, 2 * n), 16 * n, "SB2", 16 * n)
+        ts(R("LL", 2 * n, 4 * n, 2), w, 384.0, None, op.add)
+        ts(R("LL", 2 * n + 1, 4 * n, 2), w, 385.0, None, op.add)
         slip()
-    hold(R("YU", 0, 16), 256, R("GA", 0, 256))
-    send_y()
-    hold(R("PL"), 288, R("TB"))
+    for t in range(CFG["ga"]):
+        above(t)
+    act(R("GA"), nc, ind=R("LL", 16, 32))
+    act(R("AD", 13, 14), q0, AF.Identity, scale=-1.0, bias=1.0)
+    act(R("AD", 14, 15), q0, AF.Identity, scale=-255.0, bias=256.0)
+    for t in range(CFG["ga"], 4):
+        above(t)
+    low = R("SB2", 47, 256, 16)
+    ts(R("EW", 20, 34), low, 384.0, 0.5, op.add, op.mult)
+    ts(R("YB", 3, 17), low, 384.0, 0.5, op.add, op.mult)
+    tt(R("EW", 2, 18), R("PW", 0, 9), R("EW", 20, 36), op.is_equal, R("PL", 2, 3))
+    slip(12)
+    tt(R("P5"), R("EW"), R("JC"), op.mult, R("PL", 8, 13))
+    hold(R("GA"), 256)
+    scan(R("S5"), R("R5"), R("P5"), op.max)
+    ts(R("YB", 17, 33), R("SF", 15, 256, 16), 0.5, R("AD", 2, 3), op.mult, op.add)
+    for r in range(3):
+        send_y(r)
+    tc(R("oU"), R("S5", 4, 80, 5))
+    tc(R("inv"), R("VR"), oind=R("oU"))
+    rest.append(lambda: ts(R("sp"), R("sw"), -1.0, 0.5, op.mult, op.add))
+    w = dist(R("inv", 0, C), R("paU"), C)
+    ts(R("n1"), w, -224.0, 15.0, op.is_ge, op.mult)
+    tt(R("n2"), w, R("sp"), op.add)
+    tt(R("n3"), R("n1"), R("sp"), op.mult)
+    tt(R("n1"), R("n2"), R("n3"), op.add)
+    ts(R("NP", 1, 24), R("n1", 1, 24), 256.0, None, op.add)
+    ts(R("NP", 0, 1), R("n1", 0, 1), R("AD", 13, 14), R("AD", 14, 15), op.mult, op.add)
+    for k in range(4):
+        table("TB", 208 + k, 4, [(0, [[16, 16 >> k], [0, 2 << k]], 31)])
+    table("TB", 208, 1, [(0, one, 15)])
+    iota(R("PS"), [[0, 128]], 0)
+    for k in range(4):
+        table("PS", k, 4, [(2 << k, [[0, (16 >> k) - 1], [2, 2], [0, 1 << k]], -1)])
+    table("PS", 0, 1, [(0, one, 1)])
+    act(R("sn", 0, 16), R("TB", 48, 64), AF.Sign, scale=-1.0, bias=R("PF", 1, 2))
+    act(R("sn", 16, 32), R("TB", 48, 64), AF.Sign, scale=-1.0, bias=R("AD", 12, 13))
+    act(R("l32"), R("lb"), AF.Identity, scale=32.0)
+    for t in range(CFG["ac"]):
+        arrived(0, t)
     yrep(0)
+    for t in range(CFG["ac"], 4):
+        arrived(0, t)
+    for m, x in ((1, 16.0), (2, 8.0), (4, 4.0), (8, 2.0)):
+        act(R("C0", 16 + 16 * m, 16 + 32 * m), R("mk", 0, 16 * m), AF.Identity, scale=x)
+    const(R("R4"), 1)
+    const(R("R4", 0, 128, 4), 0)
+    tt(R("sl"), R("sn"), R("l32"), op.mult)
+    tt(R("C0", 0, 32), R("sl"), R("AM", 0, 32), op.mult)
+    tt(R("C0", 0, 16), R("C0", 0, 16), R("C0", 16, 32), op.subtract)
+    act(R("C0", 0, 1), q0, AF.Identity, scale=-512.0)
+    const(R("C0", 16, 17), 512)
+    yrep(1)
+    yrep(2)
+    rest.extend([lambda: hold(R("TB", 208, 336), 128), lambda: held(R("PL", 14, 22), 0, 8, 1)])
+    w = dist(R("YR", 0, 512), R("NP"), C)
+    ts(R("MU", 0, 24), w, 256.0, None, op.add)
+    renew(0)
 
     def turned(r):
         c0, c1 = ("C0", "C1") if r == 1 else ("C1", "C0")
-        tt(R(c1), R("sg"), R(c0), op.mult, R("YU", 16, 33))
-        scan(R("SC"), 272, R(c1))
+        tt(R(c1), R("sg"), R(c0), op.mult, R("YB", 0, 17))
+        scan(R("SC"), R("R0", 0, 272), R(c1))
+        tt(R("P1"), R("SC"), R("PS"), op.mult, R("PL", 14, 22))
+        scan(R("P4"), R("R4"), R("P1"))
         pack_h(r, 0)
-        tt(R("P1"), R("SC"), R("PS"), op.mult, R("PL", 0, 8))
-        scan(R("P4"), 128, R("P1"), "R4")
-        ts(R("TU", 32 * r, 32 * r + 32), R("P4", 3, 128, 4), 256.0, R("SC", 255, 256), op.add, op.add)
-        pack_h(r, 1)
-        send_h(r, 0)
-        send_t(r)
-        send_s(r)
-        send_h(r, 1)
-
-    def trep(r):
-        act(R("Tr"), R("iC"), ind=R("TU", 32 * r, 32 * r + 32))
+        ts(R("TU", 32 * r, 32 * r + 32), R("P4", 3, 128, 4), R("SC", 31, 32), float(r), op.add, op.mult)
 
     def hlist(r):
         w = dist(R("Tr"), R("NP"), C)
         ts(R("HL", 24 * r, 24 * r + 24), w, 256.0, None, op.add)
-
-    def arrived(r):
-        for k, (a, b) in enumerate(HC):
-            for t in range(4):
-                bk = HB[1 - k][t]
-                mm(bk, b - a, R("eq", 128 * t, 128 * t + 128), R("es", 128 * t, 128 * t + 128),
-                   R("hL", C * r + a, C * r + b), R("hP", C * r + a, C * r + b))
-                act(R("ab", C * t + a, C * t + b), R("ps%d" % bk, 0, b - a))
 
     def maps(r):
         tc(R("Z"), R("YR", 512 * r, 512 * r + 512), oind=R("tL", 32 * r, 32 * r + 32))
         w = dist(R("Z"), R("HL", 24 * r, 24 * r + 24), C)
         ts(R("MU", 24 * r, 24 * r + 24), w, 256.0, None, op.add)
 
-    def renew(r):
-        for t in range(4):
-            tt(R("xn", t, 1536, 4), R("ab", C * t, C * t + C), R("bb", C * t, C * t + C), op.add, R("MU", 24 * r, 24 * r + 24))
-        pack_x(r + 1, "xn")
-
-
-    tc(R("Yd", 0, 32), R("YU", 0, 32))
-    tc(R("Ye"), R("YU", 0, 32))
-    tt(R("s1"), R("Yd"), R("Ye"), op.is_equal, R("PL", 16, 18))
-    tc(R("s5"), R("s1"), ind=R("PL", 8, 16))
-    scan(R("s6"), 128, R("s5"), "R4")
-    tt(R("s6", 127, 128), R("s6", 127, 128), R("rd", 2, 3), op.add)
-    ts(R("s4"), R("s6", 3, 128, 4), R("rd", 1, 2), 1.0, op.add, op.min)
-    tt(R("s2"), R("JC"), R("s4"), op.mult)
-    tt(R("s1"), R("s2"), R("Yd", 0, 32), op.max)
-    tc(R("oU"), R("s1"))
-    tc(R("inv"), R("iC"), oind=R("oU"))
-    hold(R("NP"), C, R("inv", 0, C))
-    arrived(0)
-    yrep(1)
-    yrep(2)
-    w = dist(R("YR", 0, 512), R("NP"), C)
-    ts(R("MU", 0, 24), w, 256.0, None, op.add)
-    renew(0)
     for r in (1, 2):
-        score(r, 0)
-        score(r, 1)
-        layer(r)
+        pack_x(r, "xn")
+        score(r)
+        signs()
+        layer(r, 0)
+        layer(r, 1)
         turned(r)
+        send_t(r)
+        send_h(r, 0)
+        act(R("Tr"), R("iC"), ind=R("TU", 32 * r, 32 * r + 32))
+        unpack(r, 0)
+        pack_h(r, 1)
+        send_s(r)
+        send_h(r, 1)
         if r == 1:
             quant(R("vq"), R("vs"), R("vb"))
-        trep(r)
-        for t in range(4):
-            if t == 3:
-                hlist(r)
+        for t in range(1, 4):
             unpack(r, t)
+        hlist(r)
         for t in range(4):
             above(t)
-        arrived(r)
+        for t in range(4):
+            arrived(r, t)
         maps(r)
-        if r == 2:
-            act(R("mr"), R("Z"), AF.Identity, ind=R("HL", 48, 72), bias=256.0)
-            dma("Y", T.im[:, :], T.mr[0:128:16, 0:C], [R("mr")], [])
-        renew(r)
-    for k, (a, b) in enumerate(CH):
+        if r == 1:
+            renew(r)
+    act(R("mr"), R("Z"), AF.Identity, ind=R("HL", 48, 72), bias=256.0)
+    dma("Y", T.im[:, :], T.mr[0:128:16, 0:C], [R("mr")], [])
+    for k, (a, b) in enumerate(LAST):
+        renew(2, [(a, b)])
+        pack_x(3, "xn", [(a, b)])
         q3, s3 = R("xq", 3 * C + a, 3 * C + b), R("xs", 3 * C + a, 3 * C + b)
-        mm((0, 7)[k], b - a, R("vq"), R("vs"), q3, s3)
-        act(R("yb", a, b), R("ps%d" % (0, 7)[k], 0, b - a))
+        mm(2 + k, b - a, R("vq"), R("vs"), q3, s3)
         dma("Y", T.oc[:, 4 * a:4 * b], b8(q3), [q3], [])
+        act(R("yb", a, b), R("ps%d" % (2 + k), 0, b - a))
         dma("A", T.y[:, a:b], v(R("yb", a, b)), [R("yb", a, b)], [])
     for k in range(4):
         dma("Y", T.osc[4 * k:4 * k + 4, :], T.xs[32 * k:32 * k + 4, 3 * C:4 * C], [R("xs", 3 * C, 4 * C)], [])

@@ -2,19 +2,18 @@ from concourse.bass import DstId, RemoteDMATransfer
 from concourse.mybir import dt, AluOpType, AxisListType, ActivationFunctionType as AF
 
 C = 384
-CH = [(0, 192), (192, 384)]
-HC = [(0, 128), (128, 384)]
+CH = [(0, 128), (128, 256), (256, 384)]
+HALF = [(0, 192), (192, 384)]
 LAST = [(0, 256), (256, 384)]
-FQ = ["AAAA", "VVAA", "VVAA"]
-CFG = {"ga": 1, "ac": 0}
+CFG = {"ga": 2, "ac": 0, "trv": 16, "fa": 2}
 SCRATCH = {
     "tm": ("sbuf", [128, 128], "int32"), "t2": ("sbuf", [128, 128], "int32"), "KX": ("sbuf", [128, 2], "int32"),
-    "KF": ("sbuf", [128, 2], "float32"), "AD": ("sbuf", [128, 16], "float32"), "ULi": ("sbuf", [128, 8], "int32"),
+    "KF": ("sbuf", [128, 2], "float32"), "AD": ("sbuf", [128, 16], "float32"),
     "UL": ("sbuf", [128, 8], "uint16"), "idn": ("sbuf", [128, 128], "bfloat16"), "EB": ("sbuf", [128, 2048], "bfloat16"),
     "eq": ("sbuf", [128, 512], "float8_e4m3fn_x4"), "es": ("sbuf", [128, 512], "uint8"),
     "i2": ("sbuf", [128, 400], "bfloat16"), "iC": ("sbuf", [128, 512], "bfloat16"), "mk": ("sbuf", [128, 384], "bfloat16"),
     "R0": ("sbuf", [128, 384], "bfloat16"), "R4": ("sbuf", [128, 128], "bfloat16"), "R5": ("sbuf", [128, 80], "float32"),
-    "MX": ("sbuf", [128, 256], "bfloat16"), "TB": ("sbuf", [128, 336], "float32"), "SF": ("sbuf", [128, 256], "float32"),
+    "MX": ("sbuf", [128, 288], "bfloat16"), "TB": ("sbuf", [128, 352], "float32"), "SF": ("sbuf", [128, 288], "float32"),
     "PL": ("sbuf", [128, 22], "uint16"), "PF": ("sbuf", [128, 2], "float32"), "PS": ("sbuf", [128, 128], "bfloat16"),
     "mW": ("sbuf", [128, 128], "bfloat16"), "lb": ("sbuf", [128, 32], "float32"),
     "l32": ("sbuf", [128, 32], "float32"), "ad": ("sbuf", [128, 32], "float32"), "sn": ("sbuf", [128, 32], "float32"),
@@ -32,12 +31,12 @@ SCRATCH = {
     "Nc": ("sbuf", [128, 784], "bfloat16"), "L": ("sbuf", [128, 114], "uint16"), "Lf": ("sbuf", [128, 114], "float32"),
     "LL": ("sbuf", [128, 32], "uint16"), "g16": ("sbuf", [128, 16], "float32"), "yt": ("sbuf", [128, 2], "float32"),
     "GM": ("sbuf", [128, 384], "bfloat16"), "SB": ("sbuf", [128, 384], "bfloat16"), "SB2": ("sbuf", [128, 256], "bfloat16"),
-    "GA": ("sbuf", [128, 256], "bfloat16"), "YB": ("sbuf", [128, 34], "uint16"), "TR": ("sbuf", [128, 48], "bfloat16"),
+    "GA": ("sbuf", [128, 128], "bfloat16"), "YB": ("sbuf", [128, 34], "uint16"), "TR": ("sbuf", [128, 48], "bfloat16"),
     "eT": ("sbuf", [128, 48], "bfloat16"), "gT": ("sbuf", [128, 48], "bfloat16"), "EW": ("sbuf", [128, 36], "float32"),
     "TQ": ("sbuf", [128, 16], "bfloat16"), "PW": ("sbuf", [128, 16], "float32"),
     "P5": ("sbuf", [128, 80], "float32"), "S5": ("sbuf", [128, 80], "float32"), "oU": ("sbuf", [128, 16], "uint16"),
-    "inv": ("sbuf", [128, 768], "bfloat16"), "n1": ("sbuf", [128, 24], "float32"), "n2": ("sbuf", [128, 24], "float32"),
-    "n3": ("sbuf", [128, 24], "float32"), "NP": ("sbuf", [128, 24], "uint16"),
+    "inv": ("sbuf", [128, 768], "bfloat16"), "NA": ("sbuf", [128, 48], "float32"), "NB": ("sbuf", [128, 48], "float32"),
+    "NS": ("sbuf", [128, 48], "float32"), "NP": ("sbuf", [128, 24], "uint16"),
     "sg": ("sbuf", [128, 400], "bfloat16"), "C0": ("sbuf", [128, 272], "bfloat16"), "C1": ("sbuf", [128, 272], "bfloat16"),
     "SC": ("sbuf", [128, 272], "bfloat16"), "P1": ("sbuf", [128, 128], "bfloat16"), "P4": ("sbuf", [128, 128], "bfloat16"),
     "TU": ("sbuf", [128, 96], "uint16"), "Tr": ("sbuf", [128, 512], "bfloat16"),
@@ -48,13 +47,12 @@ SCRATCH = {
     "hq": ("sbuf", [128, 1152], "float8_e4m3fn_x4"), "hs": ("sbuf", [128, 1152], "uint8"),
     "hL": ("sbuf", [128, 1152], "float8_e4m3fn_x4"), "hP": ("sbuf", [128, 1152], "uint8"),
     "fb": ("sbuf", [128, 1536], "bfloat16"), "bb": ("sbuf", [128, 1536], "bfloat16"), "ab": ("sbuf", [128, 1536], "bfloat16"),
-    "xn": ("sbuf", [128, 1536], "bfloat16"), "yb": ("sbuf", [128, 384], "float32"),
+    "ag": ("sbuf", [128, 1536], "bfloat16"), "xn": ("sbuf", [128, 1536], "bfloat16"), "yb": ("sbuf", [128, 384], "float32"),
 }
 for _k in range(8):
     SCRATCH["ps%d" % _k] = ("psum", [128, 512], "float32")
-SEMAPHORES = (["cV", "cA", "cT", "cG", "loc"] + ["d%d" % k for k in range(24)] + ["ay%d" % k for k in range(3)]
-              + ["at%d" % k for k in range(3)] + ["as%d" % k for k in range(3)]
-              + ["ah%d_%d" % (r, k) for r in range(3) for k in range(len(HC))])
+SEMAPHORES = (["cV", "cA", "cT", "cG", "loc"] + ["d%d" % k for k in range(24)]
+              + ["a%s%d" % (n, k) for n in "ytsh" for k in range(3)] + ["ai"])
 
 
 def rank_program(g, core, T, topo):
@@ -152,9 +150,9 @@ def rank_program(g, core, T, topo):
     def fill(out, x):
         emit("V", lambda: g.vector.memset(v(out), x), [], [out])
 
-    def const(out, x):
+    def const(out, x, src="i2", a=0):
         n = len(range(out[1], out[2], out[3]))
-        act(out, R("i2", 0, n), AF.Identity, scale=0.0, bias=float(x))
+        act(out, R(src, a, a + n), AF.Identity, scale=0.0, bias=float(x))
 
     def fold(out, a, o):
         emit("V", lambda: g.vector.tensor_reduce(v(out), v(a), AxisListType.X, o), [a], [out])
@@ -204,10 +202,13 @@ def rank_program(g, core, T, topo):
     def b8(r):
         return v(r).bitcast(dt.uint8)
 
+    def cols(n, r, a=0, b=C):
+        return R(n, C * r + a, C * r + b)
+
     dma("Y", v(R("ub")), T.u[:, :], [], [R("ub")])
-    for q, (a, b) in zip("YA", CH):
-        dma(q, v(R("xb", 4 * a, 4 * b)), T.x[:, 4 * a:4 * b], [], [R("xb", 4 * a, 4 * b)])
     dma("A", v(R("seI")), T.se[:, :], [], [R("seI")])
+    for q, (a, b) in zip("AYA", CH):
+        dma(q, v(R("xb", 4 * a, 4 * b)), T.x[:, 4 * a:4 * b], [], [R("xb", 4 * a, 4 * b)])
     dma("Y", b8(R("wq")), T.wc[:, :], [], [R("wq")])
     dma("Y", v(R("wp")), T.ws[:, :], [], [R("wp")])
     dma("Y", v(R("vb")), T.v[:, :], [], [R("vb")])
@@ -224,10 +225,11 @@ def rank_program(g, core, T, topo):
     for r in range(3):
         n = len(topo.engines(part[r], core))
         acc.setdefault("yL", []).append((R("yL", 32 * r, 32 * r + 32), True, "R", ("ay%d" % r, len(tree_engines(part[r], core)))))
+        if r == 0:
+            acc["yL"] = [(R("yL", 0, 16), True, "R", ("ai", n)), (R("yL", 16, 32), True, "R", ("ay0", n))]
         acc.setdefault("tL", []).append((R("tL", 32 * r, 32 * r + 32), True, "R", ("at%d" % r, n)))
-        acc.setdefault("hP", []).append((R("hP", C * r, C * r + C), True, "R", ("as%d" % r, n)))
-        for k, (a, b) in enumerate(HC):
-            acc.setdefault("hL", []).append((R("hL", C * r + a, C * r + b), True, "R", ("ah%d_%d" % (r, k), n)))
+        acc.setdefault("hP", []).append((cols("hP", r), True, "R", ("as%d" % r, n)))
+        acc.setdefault("hL", []).append((cols("hL", r), True, "R", ("ah%d" % r, n)))
 
     def remote(dst, out, in_, rd, sem, e=None):
         order("G", rd, [])
@@ -236,13 +238,9 @@ def rank_program(g, core, T, topo):
         g.remote_dma(out_ap=out, in_ap=in_, remote_sem=T.sem[sem], local_sem=T.sem.loc, pid=pid, routing_id=rid, dma_engine_mask=some(e))
         loc[0] += len(e)
 
-    def send_h(r, k):
-        a, b = C * r + HC[k][0], C * r + HC[k][1]
-        remote(part[r], b8(R("hL", a, b)), b8(R("hq", a, b)), [R("hq", a, b)], "ah%d_%d" % (r, k))
-
-    def send_s(r):
-        w = (C * r, C * r + C)
-        remote(part[r], v(R("hP", *w)), v(R("hs", *w)), [R("hs", *w)], "as%d" % r)
+    def send_h(r):
+        remote(part[r], b8(cols("hL", r)), b8(cols("hq", r)), [cols("hq", r)], "ah%d" % r)
+        remote(part[r], v(cols("hP", r)), v(cols("hs", r)), [cols("hs", r)], "as%d" % r)
 
     def send_t(r):
         w = (32 * r, 32 * r + 32)
@@ -254,301 +252,343 @@ def rank_program(g, core, T, topo):
     one = [[0, 1]]
     iota(R("tm"), [[1, 128]], 0, -1)
     iota(R("KX"), [[0, 2]], 0, 1)
-    iota(R("ULi"), [[16, 8]], 0)
     iota(R("i2"), [[2, 400]], -384)
     table("TB", 0, 1, [(0, [[-1, 2]], 113), (2, [[1, 2]], 0), (4, [[1, 4]], 30), (8, [[1, 2], [2, 4]], 76),
                        (16, [[32, 2], [64, 4], [2, 2]], -384), (32, [[1, 8], [0, 2]], 1),
-                       (48, [[-92, 2]], 100), (50, [[8, 2]], 4), (52, [[4, 4]], 2), (56, [[2, 8]], 1),
-                       (64, [[0, 2], [1, 8], [0, 2]], 0), (96, [[1, 8], [0, 2]], 8), (112, [[0, 96]], 1)])
+                       (48, [[-92, 2]], 100), (50, [[8, 2]], 4), (52, [[4, 4]], 2), (56, [[2, 8]], 1)])
+    table("lb", 0, 1, [(0, [[7, 2]], 1), (2, [[0, 2]], 4), (4, [[0, 4]], 2), (8, [[0, 8]], 1)])
+    table("TB", 0, 1, [(64, [[0, 2], [1, 8], [0, 2]], 0), (96, [[1, 8], [0, 2]], 8), (112, [[0, 112]], 1)])
     table("TB", 128, 5, [(0, [[1, 16]], 0)])
     table("TB", 129, 5, [(2, [[1, 7], [0, 2]], 1)])
     table("TB", 130, 5, [(4, [[1, 3], [0, 4]], 1)])
     table("TB", 132, 5, [(0, [[1, 16]], 18)])
     table("TB", 129, 1, [(0, [[0, 3]], 0)])
-    table("lb", 0, 1, [(0, [[7, 2]], 1), (2, [[0, 2]], 4), (4, [[0, 4]], 2), (8, [[0, 8]], 1)])
+    for k in range(4):
+        table("TB", 224 + k, 4, [(0, [[16, 16 >> k], [0, 2 << k]], 31)])
+    table("TB", 224, 1, [(0, one, 15)])
     iota(R("JC"), [[16, 16], [0, 5]], 400, 1)
     iota(R("JC", 4, 80, 5), [[0, 16]], 1)
     iota(R("VR", 0, 16), [[2, 16]], -256)
     iota(R("VR", 16, 256), [[32, 15], [1, 16]], -224)
-    iota(R("iC"), [[1, 512]], -256)
 
+    fill(R("EB", 512, 1026), 0.0)
+    const(R("R0"), 1, "EB", 512)
+    const(R("sg", 384, 400), 0.5, "EB", 512)
+    const(R("AD", 6, 7), 384, "EB", 512)
+    const(R("AD", 7, 8), 385, "EB", 512)
+    const(R("R0", 0, 384, 16), 0, "EB", 512)
     fill(R("EB", 0, 512), 0.0)
-    act(R("EB", 1536, 2048), R("EB", 0, 512))
-    fill(R("EB", 512, 1536), 0.0)
     ts(R("idn"), R("tm"), 0.0, 0.5, op.is_equal, op.mult)
     ts(R("t2"), R("tm"), 15, None, op.bitwise_and)
-    for b in range(4):
-        o = R("EB", 512 * b + b, 512 * b + 512, 4)
-        if b in (1, 2):
-            tc(o, R("idn"))
-        else:
-            act(o, R("idn"))
-    ts(R("mk", 0, 128), R("t2"), 0.0, None, op.is_equal)
     ts(R("KX", 0, 1), R("KX", 0, 1), 15, None, op.bitwise_and)
     ts(R("KX", 1, 2), R("KX", 1, 2), 1, None, op.bitwise_and)
-    tc(R("UL"), R("ULi"))
+    tc(R("EB", 0, 512, 4), R("idn"))
+    ts(R("mk", 0, 128), R("t2"), 0.0, None, op.is_equal)
     tc(R("KF"), R("KX"))
-    quant(R("eq"), R("es"), R("EB"))
+    tc(R("EB", 513, 1024, 4), R("idn"))
+    act(R("EB", 1026, 2048), R("EB", 0, 1022))
+    quant(R("eq", 0, 256), R("es", 0, 256), R("EB", 0, 1024))
+    ts(R("UL"), R("i2", 0, 64, 8), 384.0, None, op.add)
     q_, bit, q0 = R("KF", 0, 1), R("KF", 1, 2), R("mk", 0, 1)
+    act(R("mk", 128, 256), R("mk", 0, 128))
+    ts(R("paI"), R("seI"), 1, None, op.arith_shift_right)
+    ts(R("slI"), R("seI"), 1, None, op.bitwise_and)
     quant(R("uq"), R("us"), R("ub"))
-    tc(R("ups"), R("us"), ind=R("UL"))
+    ts(R("sb", 1, 24), R("paI", 1, 24), 2.0, 0.5, op.mult, op.add)
+    tc(R("paU"), R("paI"))
+    ts(R("sh"), R("slI"), -2.0, 1.0, op.mult, op.add)
+    act(R("ups"), R("us"), ind=R("UL"))
     emit("V", lambda: g.vector.tensor_copy(v(R("upq")).bitcast(dt.uint32), v(R("uq")).bitcast(dt.uint32).indirect(v(R("UL")))),
          [R("uq"), R("UL")], [R("upq")])
-    act(R("mk", 128, 256), R("mk", 0, 128))
     act(R("mk", 256, 384), R("mk", 0, 128))
+    act(R("AD", 1, 2), q_, AF.Identity, scale=1024.0, bias=-15360.0)
+    act(R("MX"), R("mk", 0, 288), AF.Identity, scale=-33792.0, bias=1024.0)
     act(R("AD", 0, 1), q0, AF.Identity, scale=768.0, bias=0.5)
-    const(R("sg", 384, 400), 0.5)
-    const(R("R0"), 1)
-    const(R("R0", 0, 384, 16), 0)
     act(R("AD", 4, 5), bit)
     act(R("AD", 5, 6), bit, AF.Identity, bias=768.0)
-    act(R("MX"), R("mk", 0, 256), AF.Identity, scale=-33792.0, bias=1024.0)
-    act(R("AD", 1, 2), q_, AF.Identity, scale=1024.0, bias=-15360.0)
     act(R("Nc", 0, 768, 2), R("i2", 0, 384))
     act(R("Nc", 1, 768, 2), R("i2", 0, 384))
     act(R("AD", 3, 4), bit, AF.Identity, bias=384.0)
-    const(R("AD", 6, 7), 384)
-    const(R("AD", 7, 8), 385)
 
-    def score(r):
-        for k, (a, b) in enumerate(CH):
-            mm(k, b - a, R("upq"), R("ups"), R("xq", C * r + a, C * r + b), R("xs", C * r + a, C * r + b))
+    SK, HK, FK, AK = [0, 1, 2], [3, 4, 5, 6], [7, 0, 1, 2], [3, 4, 5, 6]
 
-    def signs():
-        for k, (a, b) in enumerate(CH):
-            ts(R("sg", a, b), R("ps%d" % k, 0, b - a), 0.0, 0.5, op.is_ge, op.subtract)
+    def unit(t):
+        return R("eq", 128 * t, 128 * t + 128), R("es", 128 * t, 128 * t + 128)
 
-    def pack_x(r, src, pieces=CH):
-        for a, b in pieces:
-            quant(R("xq", C * r + a, C * r + b), R("xs", C * r + a, C * r + b), R(src, 4 * a, 4 * b))
+    def pack_x(r, src, a, b):
+        quant(cols("xq", r, a, b), cols("xs", r, a, b), R(src, 4 * a, 4 * b))
 
-    HB = [[2, 3, 4, 5], [6, 7, 0, 1]]
+    def score(r, k):
+        a, b = CH[k]
+        mm(SK[k], b - a, R("upq"), R("ups"), cols("xq", r, a, b), cols("xs", r, a, b))
 
-    def layer(r, k):
-        a, b = HC[k]
-        for t in range(4):
-            mm(HB[k][t], b - a, R("wq", 128 * t, 128 * t + 128), R("wp", 128 * t, 128 * t + 128),
-               R("xq", C * r + a, C * r + b), R("xs", C * r + a, C * r + b))
-            act(R("hb", 4 * a + t, 4 * b, 4), R("ps%d" % HB[k][t], 0, b - a), scale=0.03125)
+    def sign(k):
+        a, b = CH[k]
+        ts(R("sg", a, b), R("ps%d" % SK[k], 0, b - a), 0.0, 0.5, op.is_ge, op.subtract)
+
+    def layer(r, t, cast=True):
+        mm(HK[t], C, R("wq", 128 * t, 128 * t + 128), R("wp", 128 * t, 128 * t + 128), cols("xq", r), cols("xs", r))
+        if cast:
+            act(R("hb", t, 4 * C, 4), R("ps%d" % HK[t], 0, C), scale=0.03125)
+
+    def scaled(t, a, b):
+        ts(R("hb", 4 * a + t, 4 * b, 4), R("ps%d" % HK[t], a, b), 0.03125, None, op.mult)
 
     def pack_h(r, k):
-        a, b = HC[k]
-        quant(R("hq", C * r + a, C * r + b), R("hs", C * r + a, C * r + b), R("hb", 4 * a, 4 * b))
+        a, b = CH[k]
+        quant(cols("hq", r, a, b), cols("hs", r, a, b), R("hb", 4 * a, 4 * b))
 
     def unpack(r, t):
-        mm(2 + t, C, R("eq", 128 * t, 128 * t + 128), R("es", 128 * t, 128 * t + 128), R("xq", C * r, C * r + C), R("xs", C * r, C * r + C))
-        if FQ[r][t] == "V":
-            tc(R("fb", C * t, C * t + C), R("ps%d" % (2 + t), 0, C))
-        else:
-            act(R("fb", C * t, C * t + C), R("ps%d" % (2 + t), 0, C))
+        mm(FK[t], C, *unit(t), cols("xq", r), cols("xs", r))
+
+    def own(f, t, a=0, b=C):
+        f(cols("fb", t, a, b), R("ps%d" % FK[t], a, b))
 
     def above(t):
-        act(R("bb", C * t, C * t + C), R("fb", C * t, C * t + C), ind=R("paU"))
+        act(cols("bb", t), cols("fb", t), ind=R("paU"))
 
     def arrived(r, t):
-        bk = HB[1][t]
-        mm(bk, C, R("eq", 128 * t, 128 * t + 128), R("es", 128 * t, 128 * t + 128), R("hL", C * r, C * r + C), R("hP", C * r, C * r + C))
-        act(R("ab", C * t, C * t + C), R("ps%d" % bk, 0, C))
+        mm(AK[t], C, *unit(t), cols("hL", r), cols("hP", r))
+        act(cols("ab", t), R("ps%d" % AK[t], 0, C))
 
     def yrep(r):
         act(R("YR", 512 * r, 512 * r + 512), R("iC"), ind=R("yL", 32 * r, 32 * r + 32))
 
-    def renew(r, pieces=((0, C),)):
-        for a, b in pieces:
-            for t in range(4):
-                tt(R("xn", 4 * a + t, 4 * b, 4), R("ab", C * t, C * t + C), R("bb", C * t + a, C * t + b), op.add,
-                   R("MU", 24 * r + a // 16, 24 * r + b // 16))
+    def renew(r, t, a=0, b=C):
+        tt(R("xn", 4 * a + t, 4 * b, 4), cols("ab", t), cols("bb", t, a, b), op.add, R("MU", 24 * r + a // 16, 24 * r + b // 16))
 
-    pack_x(0, "xb")
-    score(0)
-    ts(R("paI"), R("seI"), 1, None, op.arith_shift_right)
-    ts(R("slI"), R("seI"), 1, None, op.bitwise_and)
-    tc(R("paU"), R("paI"))
-    signs()
-    ts(R("sh"), R("slI"), -2.0, 1.0, op.mult, op.add)
-    ts(R("sb", 1, 24), R("paI", 1, 24), 2.0, 0.5, op.mult, op.add)
-    ts(R("sb", 0, 1), R("paI", 0, 1), 2.0, R("AD", 0, 1), op.mult, op.add)
-    layer(0, 0)
-    layer(0, 1)
-    rest.extend([lambda: tc(R("L", 112, 114), R("AD", 4, 6))])
-    w = dist(R("sg"), R("paU"), C)
-    tt(R("sw"), w, R("sh"), op.mult)
-    hold(R("TB", 0, 208), 208)
-    tt(R("s24"), R("sb"), R("sw"), op.subtract)
+    def dist2(win, ind, at):
+        for a, b in HALF:
+            tt(R("GM", a, b), win, R("mk", 0, b - a), op.mult, R(ind, at + a // 16, at + b // 16))
+            slip()
+        for a, b in HALF:
+            scan(R("SB", a, b), R("R0", 0, b - a), R("GM", a, b))
+            slip()
+
+    def maps(win, ind, at, r):
+        dist2(win, ind, at)
+        for a, b in HALF:
+            ts(R("MU", 24 * r + a // 16, 24 * r + b // 16), R("SB", a + 15, b, 16), 256.0, None, op.add)
+
+    def picked(r, t, a=0, b=C):
+        act(cols("ag", t, a, b), cols("ab", t), ind=R("MU", 24 * r + a // 16, 24 * r + b // 16))
+
+    def add(t, a, b):
+        tt(R("xn", 4 * a + t, 4 * b, 4), cols("ag", t, a, b), cols("bb", t, a, b), op.add)
+
+    def state(r):
+        picked(r, 3)
+        for a, b in HALF:
+            renew(r, 0, a, b)
+        renew(r, 1)
+        renew(r, 2)
+        add(3, 0, 128)
+        add(3, 128, C)
+        for k, (a, b) in enumerate(CH):
+            pack_x(r + 1, "xn", a, b)
+            score(r + 1, k)
+
+    for k, (a, b) in enumerate(CH):
+        pack_x(0, "xb", a, b)
+        score(0, k)
+        if k == 0:
+            quant(R("eq", 256, 512), R("es", 256, 512), R("EB", 1024, 2048))
+    hold(R("TB", 0, 64), 64)
+    for k in range(len(CH)):
+        sign(k)
     ts(R("PF"), R("SF", 31, 64, 32), R("AD", 1, 2), None, op.add)
-    tc(R("stU"), R("s24"))
-    held(R("PL", 0, 13), 0, 13, 1)
-    tc(R("Nc"), R("i2", 0, 384), oind=R("stU"))
-    ts(R("mW"), R("i2", 0, 128), R("PF", 0, 1), -1024.0, op.not_equal, op.mult)
-    const(R("PW"), 0)
+    held(R("PL", 0, 4), 0, 4, 1)
     act(R("AD", 8, 10), R("AD", 6, 8), AF.Identity, scale=0.0, bias=R("AD", 4, 5))
     act(R("AD", 12, 13), q_, AF.Identity, bias=0.5)
     act(R("lb", 16, 32), R("lb", 0, 16))
     act(R("AD", 10, 12), R("AD", 8, 10), AF.Identity, scale=-1.0)
-    act(R("ad", 0, 16), R("TB", 48, 64), AF.Abs, scale=-1.0, bias=R("PF", 1, 2))
-    act(R("ad", 16, 32), R("TB", 48, 64), AF.Abs, scale=-1.0, bias=R("AD", 12, 13))
+    for f, o in ((AF.Abs, "ad"), (AF.Sign, "sn")):
+        act(R(o, 0, 16), R("TB", 48, 64), f, scale=-1.0, bias=R("PF", 1, 2))
+        act(R(o, 16, 32), R("TB", 48, 64), f, scale=-1.0, bias=R("AD", 12, 13))
+    act(R("l32"), R("lb"), AF.Identity, scale=32.0)
+    for t in range(4):
+        layer(0, t)
+    rest.extend([lambda: None, lambda: tc(R("L", 112, 114), R("AD", 4, 6)),
+                 lambda: ts(R("sb", 0, 1), R("paI", 0, 1), 2.0, R("AD", 0, 1), op.mult, op.add),
+                 lambda: ts(R("mW"), R("i2", 0, 128), R("PF", 0, 1), -1024.0, op.not_equal, op.mult)])
+    dist2(R("sg"), "paU", 0)
+    tt(R("sw"), R("SB", 15, C, 16), R("sh"), op.mult)
+    tt(R("AM", 0, 32), R("lb"), R("ad"), op.is_gt)
+    tt(R("sl"), R("sn"), R("l32"), op.mult)
+    tt(R("s24"), R("sb"), R("sw"), op.subtract)
+    tt(R("C0", 0, 32), R("sl"), R("AM", 0, 32), op.mult)
+    tc(R("stU"), R("s24"))
+    tt(R("C0", 0, 16), R("C0", 0, 16), R("C0", 16, 32), op.subtract)
+    tc(R("Nc"), R("i2", 0, 384), oind=R("stU"))
+    const(R("PW"), 0)
     act(R("AM", 32, 48), R("mk", 0, 16))
-    for t in range(2):
+    for t in range(4):
         unpack(0, t)
-    const(R("R5"), 1)
-    const(R("EW", 34, 36), 0)
-    act(R("AD", 2, 3), q_, AF.Identity, scale=512.0, bias=-7488.0)
-    const(R("R5", 0, 80, 5), 0)
-    for t in range(2, 4):
-        unpack(0, t)
-    const(R("inv", 0, C), 0)
+        own(act, t)
+        if t == 1:
+            const(R("R5"), 1)
+            const(R("EW", 34, 36), 0)
+            act(R("AD", 2, 3), q_, AF.Identity, scale=512.0, bias=-7488.0)
+            const(R("R5", 0, 80, 5), 0)
     nc = R("Nc", 0, 768)
     up = R("AD", 3, 4)
-    ts(R("L", 0, 16), nc, up, None, op.add, ind=R("L", 112, 113))
     pack_h(0, 0)
-    send_h(0, 0)
+    ts(R("L", 0, 16), nc, up, None, op.add, ind=R("L", 112, 113))
+    pack_h(0, 1)
     ts(R("L", 16, 48), nc, up, None, op.add, ind=R("L", 0, 2))
+    pack_h(0, 2)
+    send_h(0)
+    iota(R("inv", 0, C), [[0, C]], 0)
+    iota(R("iC"), [[1, 512]], -256)
     ts(R("L", 48, 112, 2), nc, up, None, op.add, ind=R("L", 30, 32))
     ts(R("L", 49, 112, 2), nc, up, None, op.add, ind=R("L", 32, 34))
-    pack_h(0, 1)
-    send_s(0)
-    send_h(0, 1)
+    hold(R("TB", 64, 352), 288)
     tt(R("GM", 0, 128), nc, R("mW"), op.add, R("L", 76, 84))
     tc(R("Lf"), R("L"))
     y4 = R("SB2", 31, 32)
     fold(y4, R("GM", 0, 128), op.max)
     tt(R("g16"), R("Lf"), R("mk", 0, 16), op.mult, R("PL", 0, 1))
+    held(R("PL", 4, 22), 0, 18, 1)
     ts(R("LL", 2, 4), R("AD", 6, 8), y4, None, op.add)
     rest.extend([
-        lambda: fold(R("yt", 0, 1), R("g16"), op.add),
-        lambda: ts(R("YB", 2, 3), y4, 384.0, 0.5, op.add, op.mult),
+        lambda: (fold(R("yt", 0, 1), R("g16"), op.add), ts(R("YB", 2, 3), y4, 384.0, 0.5, op.add, op.mult)),
         lambda: ts(R("YB", 0, 2), R("AD", 10, 12), R("yt", 0, 1), 0.5, op.add, op.mult),
-        lambda: tt(R("AM", 0, 32), R("lb"), R("ad"), op.is_gt),
+        lambda: quant(R("vq"), R("vs"), R("vb")),
         lambda: tc(R("TR"), R("i2"), ind=R("YB", 0, 3)),
-        lambda: tc(R("TQ"), R("i2"), ind=R("YB", 0, 1)),
-        lambda: tc(R("EW", 18, 20), R("YB", 1, 3)),
+        lambda: (tc(R("TQ"), R("i2"), ind=R("YB", 0, 1)), tc(R("EW", 18, 20), R("YB", 1, 3))),
         lambda: tt(R("eT"), R("TQ"), R("TR"), op.is_equal, R("PL", 4, 7)),
         lambda: ts(R("PW", 1, 8), R("SB2", 31, 128, 16), 384.0, 0.5, op.add, op.mult),
         lambda: tt(R("gT"), R("eT"), R("AM"), op.mult),
-        lambda: fold(R("EW", 0, 1), R("gT", 0, 16), op.max),
-        lambda: fold(R("EW", 1, 2), R("gT", 16, 48), op.max),
+        lambda: (fold(R("EW", 0, 1), R("gT", 0, 16), op.max), fold(R("EW", 1, 2), R("gT", 16, 48), op.max)),
     ])
     slip()
     for n in (2, 4, 8):
         w = dist(nc, R("LL", n, 2 * n), 16 * n, "SB2", 16 * n)
         ts(R("LL", 2 * n, 4 * n, 2), w, 384.0, None, op.add)
         ts(R("LL", 2 * n + 1, 4 * n, 2), w, 385.0, None, op.add)
-        slip()
+        if n < 8:
+            slip()
     for t in range(CFG["ga"]):
         above(t)
-    act(R("GA"), nc, ind=R("LL", 16, 32))
-    act(R("AD", 13, 14), q0, AF.Identity, scale=-1.0, bias=1.0)
-    act(R("AD", 14, 15), q0, AF.Identity, scale=-255.0, bias=256.0)
+    act(R("GA"), nc, ind=R("LL", 24, 32))
+    const(R("NA", 0, 48, 2), 0)
+    act(R("NB", 0, 48, 2), R("sw"), AF.Identity, scale=-15.0, bias=7.5)
+    act(R("sp", 1, 24), R("sw", 1, 24), AF.Identity, scale=-1.0, bias=256.5)
+    act(R("AD", 13, 14), q0, AF.Identity, bias=-1.0)
+    act(R("AD", 14, 15), q0, AF.Identity, scale=-1.5, bias=256.5)
+    act(R("sp", 0, 1), R("sw", 0, 1), AF.Identity, scale=R("AD", 13, 14), bias=R("AD", 14, 15))
     for t in range(CFG["ga"], 4):
         above(t)
     low = R("SB2", 47, 256, 16)
     ts(R("EW", 20, 34), low, 384.0, 0.5, op.add, op.mult)
     ts(R("YB", 3, 17), low, 384.0, 0.5, op.add, op.mult)
+    remote(part[0], v(R("yL", 0, 16)), v(R("YB", 1, 17)), [R("YB", 1, 17)], "ai")
+    tt(R("GM", 128, 256), nc, R("mk", 0, 128), op.mult, R("LL", 16, 24))
     tt(R("EW", 2, 18), R("PW", 0, 9), R("EW", 20, 36), op.is_equal, R("PL", 2, 3))
     slip(12)
+    scan(R("SB", 0, 128), R("R0", 0, 128), R("GM", 128, 256))
     tt(R("P5"), R("EW"), R("JC"), op.mult, R("PL", 8, 13))
-    hold(R("GA"), 256)
+    hold(R("GA"), 128)
+    ts(R("YB", 17, 25), R("SB", 15, 128, 16), 384.0, 0.5, op.add, op.mult)
     scan(R("S5"), R("R5"), R("P5"), op.max)
-    ts(R("YB", 17, 33), R("SF", 15, 256, 16), 0.5, R("AD", 2, 3), op.mult, op.add)
-    for r in range(3):
-        send_y(r)
+    ts(R("YB", 25, 33), R("SF", 15, 128, 16), 0.5, R("AD", 2, 3), op.mult, op.add)
+    remote(part[0], v(R("yL", 16, 32)), v(R("YB", 17, 33)), [R("YB", 17, 33)], "ay0")
+    send_y(1)
+    send_y(2)
     tc(R("oU"), R("S5", 4, 80, 5))
     tc(R("inv"), R("VR"), oind=R("oU"))
-    rest.append(lambda: ts(R("sp"), R("sw"), -1.0, 0.5, op.mult, op.add))
-    w = dist(R("inv", 0, C), R("paU"), C)
-    ts(R("n1"), w, -224.0, 15.0, op.is_ge, op.mult)
-    tt(R("n2"), w, R("sp"), op.add)
-    tt(R("n3"), R("n1"), R("sp"), op.mult)
-    tt(R("n1"), R("n2"), R("n3"), op.add)
-    ts(R("NP", 1, 24), R("n1", 1, 24), 256.0, None, op.add)
-    ts(R("NP", 0, 1), R("n1", 0, 1), R("AD", 13, 14), R("AD", 14, 15), op.mult, op.add)
-    for k in range(4):
-        table("TB", 208 + k, 4, [(0, [[16, 16 >> k], [0, 2 << k]], 31)])
-    table("TB", 208, 1, [(0, one, 15)])
+    dist2(R("inv", 0, C), "paU", 0)
+    for a, b in HALF:
+        w = R("SB", a + 15, b, 16)
+        ts(R("NA", a // 8 + 1, b // 8, 2), w, -224.0, None, op.is_ge)
+        tt(R("NB", a // 8 + 1, b // 8, 2), w, R("sp", a // 16, b // 16), op.add)
+    for a, b in HALF:
+        scan(R("NS", a // 8, b // 8), R("NA", a // 8, b // 8), R("NB", a // 8, b // 8))
+    for a, b in HALF:
+        tc(R("NP", a // 16, b // 16), R("NS", a // 8 + 1, b // 8, 2))
     iota(R("PS"), [[0, 128]], 0)
     for k in range(4):
         table("PS", k, 4, [(2 << k, [[0, (16 >> k) - 1], [2, 2], [0, 1 << k]], -1)])
     table("PS", 0, 1, [(0, one, 1)])
-    act(R("sn", 0, 16), R("TB", 48, 64), AF.Sign, scale=-1.0, bias=R("PF", 1, 2))
-    act(R("sn", 16, 32), R("TB", 48, 64), AF.Sign, scale=-1.0, bias=R("AD", 12, 13))
-    act(R("l32"), R("lb"), AF.Identity, scale=32.0)
     for t in range(CFG["ac"]):
         arrived(0, t)
-    yrep(0)
+    for a in (0, 16):
+        act(R("YR", 16 * a, 16 * a + 256), R("iC"), ind=R("yL", a, a + 16))
     for t in range(CFG["ac"], 4):
         arrived(0, t)
+    maps(R("YR", 0, 512), "NP", 0, 0)
+    state(0)
     for m, x in ((1, 16.0), (2, 8.0), (4, 4.0), (8, 2.0)):
         act(R("C0", 16 + 16 * m, 16 + 32 * m), R("mk", 0, 16 * m), AF.Identity, scale=x)
     const(R("R4"), 1)
-    const(R("R4", 0, 128, 4), 0)
-    tt(R("sl"), R("sn"), R("l32"), op.mult)
-    tt(R("C0", 0, 32), R("sl"), R("AM", 0, 32), op.mult)
-    tt(R("C0", 0, 16), R("C0", 0, 16), R("C0", 16, 32), op.subtract)
     act(R("C0", 0, 1), q0, AF.Identity, scale=-512.0)
     const(R("C0", 16, 17), 512)
+    const(R("R4", 0, 128, 4), 0)
     yrep(1)
-    yrep(2)
-    rest.extend([lambda: hold(R("TB", 208, 336), 128), lambda: held(R("PL", 14, 22), 0, 8, 1)])
-    w = dist(R("YR", 0, 512), R("NP"), C)
-    ts(R("MU", 0, 24), w, 256.0, None, op.add)
-    renew(0)
-
-    def turned(r):
-        c0, c1 = ("C0", "C1") if r == 1 else ("C1", "C0")
-        tt(R(c1), R("sg"), R(c0), op.mult, R("YB", 0, 17))
-        scan(R("SC"), R("R0", 0, 272), R(c1))
-        tt(R("P1"), R("SC"), R("PS"), op.mult, R("PL", 14, 22))
-        scan(R("P4"), R("R4"), R("P1"))
-        pack_h(r, 0)
-        ts(R("TU", 32 * r, 32 * r + 32), R("P4", 3, 128, 4), R("SC", 31, 32), float(r), op.add, op.mult)
-
-    def hlist(r):
-        w = dist(R("Tr"), R("NP"), C)
-        ts(R("HL", 24 * r, 24 * r + 24), w, 256.0, None, op.add)
-
-    def maps(r):
-        tc(R("Z"), R("YR", 512 * r, 512 * r + 512), oind=R("tL", 32 * r, 32 * r + 32))
-        w = dist(R("Z"), R("HL", 24 * r, 24 * r + 24), C)
-        ts(R("MU", 24 * r, 24 * r + 24), w, 256.0, None, op.add)
 
     for r in (1, 2):
-        pack_x(r, "xn")
-        score(r)
-        signs()
-        layer(r, 0)
-        layer(r, 1)
-        turned(r)
-        send_t(r)
-        send_h(r, 0)
-        act(R("Tr"), R("iC"), ind=R("TU", 32 * r, 32 * r + 32))
-        unpack(r, 0)
-        pack_h(r, 1)
-        send_s(r)
-        send_h(r, 1)
-        if r == 1:
-            quant(R("vq"), R("vs"), R("vb"))
-        for t in range(1, 4):
+        c0, c1 = ("C0", "C1") if r == 1 else ("C1", "C0")
+        for k in range(len(CH)):
+            sign(k)
+        for t in (0, 2, 1, 3):
+            layer(r, t, t < 2)
+        for t in range(4):
             unpack(r, t)
-        hlist(r)
+        for t in range(CFG["fa"]):
+            own(act, t)
+        tt(R(c1), R("sg"), R(c0), op.mult, R("YB", 0, 17))
+        scaled(2, *HALF[0])
+        scan(R("SC"), R("R0", 0, 272), R(c1))
+        scaled(2, *HALF[1])
+        tt(R("P1"), R("SC"), R("PS"), op.mult, R("PL", 14, 22))
+        scaled(3, *HALF[0])
+        scan(R("P4"), R("R4"), R("P1"))
+        scaled(3, *HALF[1])
+        ts(R("TU", 32 * r, 32 * r + 32), R("P4", 3, 128, 4), R("SC", 31, 32), float(r), op.add, op.mult)
+        send_t(r)
+        k = CFG["trv"]
+        act(R("Tr", 16 * k, 512), R("iC"), ind=R("TU", 32 * r + k, 32 * r + 32))
+        for m in range(len(CH)):
+            pack_h(r, m)
+        send_h(r)
+        if k:
+            tc(R("Tr", 0, 16 * k), R("iC"), ind=R("TU", 32 * r, 32 * r + k))
+        for t in range(CFG["fa"], 4):
+            own(act, t)
+        dist2(R("Tr"), "NP", 0)
+        ts(R("HL", 24 * r, 24 * r + 24), R("SB", 15, C, 16), 256.0, None, op.add)
         for t in range(4):
             above(t)
         for t in range(4):
             arrived(r, t)
-        maps(r)
+        tc(R("Z"), R("YR", 512 * r, 512 * r + 512), oind=R("tL", 32 * r, 32 * r + 32))
+        maps(R("Z"), "HL", 24 * r, r)
         if r == 1:
-            renew(r)
-    act(R("mr"), R("Z"), AF.Identity, ind=R("HL", 48, 72), bias=256.0)
-    dma("Y", T.im[:, :], T.mr[0:128:16, 0:C], [R("mr")], [])
+            state(r)
+            yrep(2)
+    (a, b), (c, d) = LAST
+    renew(2, 0, *HALF[0])
+    renew(2, 0, HALF[0][1], b)
+    for t in range(1, 4):
+        renew(2, t, a, b)
+    for t in range(4):
+        picked(2, t, c, d)
+    add(0, c, d)
     for k, (a, b) in enumerate(LAST):
-        renew(2, [(a, b)])
-        pack_x(3, "xn", [(a, b)])
-        q3, s3 = R("xq", 3 * C + a, 3 * C + b), R("xs", 3 * C + a, 3 * C + b)
-        mm(2 + k, b - a, R("vq"), R("vs"), q3, s3)
+        pack_x(3, "xn", a, b)
+        q3, s3 = cols("xq", 3, a, b), cols("xs", 3, a, b)
+        mm(SK[k], b - a, R("vq"), R("vs"), q3, s3)
         dma("Y", T.oc[:, 4 * a:4 * b], b8(q3), [q3], [])
-        act(R("yb", a, b), R("ps%d" % (2 + k), 0, b - a))
-        dma("A", T.y[:, a:b], v(R("yb", a, b)), [R("yb", a, b)], [])
-    for k in range(4):
-        dma("Y", T.osc[4 * k:4 * k + 4, :], T.xs[32 * k:32 * k + 4, 3 * C:4 * C], [R("xs", 3 * C, 4 * C)], [])
+        if k:
+            for m in range(4):
+                dma("Y", T.osc[4 * m:4 * m + 4, :], T.xs[32 * m:32 * m + 4, 3 * C:4 * C], [cols("xs", 3)], [])
+        (tc if k else act)(R("yb", a, b), R("ps%d" % SK[k], 0, b - a))
+        dma("AY"[k], T.y[:, a:b], v(R("yb", a, b)), [R("yb", a, b)], [])
+        if not k:
+            for t in range(1, 4):
+                add(t, c, d)
+            act(R("mr"), R("Z"), AF.Identity, ind=R("HL", 48, 72), bias=256.0)
+            dma("A", T.im[:, :], T.mr[0:128:16, 0:C], [R("mr")], [])
     for q, s in dmas:
         wait(q, (s, 16))
     for q in ("V", "A", "T", "G"):

@@ -1,11 +1,11 @@
-from concourse.bass import DstId, RemoteDMATransfer
 from concourse.mybir import dt, AluOpType, AxisListType, ActivationFunctionType as AF
 
 C = 384
 CH = [(0, 128), (128, 256), (256, 384)]
 HALF = [(0, 192), (192, 384)]
 LAST = [(0, 256), (256, 384)]
-CFG = {"ga": 2, "ac": 0, "trv": 16, "fa": 2}
+HP = [[(0, 128), (128, C)], [(0, C)], [(0, C)]]
+TV = 12
 SCRATCH = {
     "tm": ("sbuf", [128, 128], "int32"), "t2": ("sbuf", [128, 128], "int32"), "KX": ("sbuf", [128, 2], "int32"),
     "KF": ("sbuf", [128, 2], "float32"), "AD": ("sbuf", [128, 16], "float32"),
@@ -13,8 +13,8 @@ SCRATCH = {
     "eq": ("sbuf", [128, 512], "float8_e4m3fn_x4"), "es": ("sbuf", [128, 512], "uint8"),
     "i2": ("sbuf", [128, 400], "bfloat16"), "iC": ("sbuf", [128, 512], "bfloat16"), "mk": ("sbuf", [128, 384], "bfloat16"),
     "R0": ("sbuf", [128, 384], "bfloat16"), "R4": ("sbuf", [128, 128], "bfloat16"), "R5": ("sbuf", [128, 80], "float32"),
-    "MX": ("sbuf", [128, 288], "bfloat16"), "TB": ("sbuf", [128, 352], "float32"), "SF": ("sbuf", [128, 288], "float32"),
-    "PL": ("sbuf", [128, 22], "uint16"), "PF": ("sbuf", [128, 2], "float32"), "PS": ("sbuf", [128, 128], "bfloat16"),
+    "MX": ("sbuf", [128, 160], "bfloat16"), "TB": ("sbuf", [128, 384], "float32"), "SF": ("sbuf", [128, 320], "float32"),
+    "PL": ("sbuf", [128, 24], "uint16"), "PF": ("sbuf", [128, 2], "float32"), "PS": ("sbuf", [128, 128], "bfloat16"),
     "mW": ("sbuf", [128, 128], "bfloat16"), "lb": ("sbuf", [128, 32], "float32"),
     "l32": ("sbuf", [128, 32], "float32"), "ad": ("sbuf", [128, 32], "float32"), "sn": ("sbuf", [128, 32], "float32"),
     "sl": ("sbuf", [128, 32], "float32"), "AM": ("sbuf", [128, 48], "bfloat16"), "JC": ("sbuf", [128, 80], "float32"),
@@ -30,16 +30,15 @@ SCRATCH = {
     "vq": ("sbuf", [128, 128], "float8_e4m3fn_x4"), "vs": ("sbuf", [128, 128], "uint8"),
     "Nc": ("sbuf", [128, 784], "bfloat16"), "L": ("sbuf", [128, 114], "uint16"), "Lf": ("sbuf", [128, 114], "float32"),
     "LL": ("sbuf", [128, 32], "uint16"), "g16": ("sbuf", [128, 16], "float32"), "yt": ("sbuf", [128, 2], "float32"),
-    "GM": ("sbuf", [128, 384], "bfloat16"), "SB": ("sbuf", [128, 384], "bfloat16"), "SB2": ("sbuf", [128, 256], "bfloat16"),
-    "GA": ("sbuf", [128, 128], "bfloat16"), "YB": ("sbuf", [128, 34], "uint16"), "TR": ("sbuf", [128, 48], "bfloat16"),
-    "eT": ("sbuf", [128, 48], "bfloat16"), "gT": ("sbuf", [128, 48], "bfloat16"), "EW": ("sbuf", [128, 36], "float32"),
-    "TQ": ("sbuf", [128, 16], "bfloat16"), "PW": ("sbuf", [128, 16], "float32"),
+    "GM": ("sbuf", [128, 384], "bfloat16"), "SB": ("sbuf", [128, 384], "bfloat16"), "SB2": ("sbuf", [128, 288], "bfloat16"),
+    "GA": ("sbuf", [128, 256], "bfloat16"), "YB": ("sbuf", [128, 34], "uint16"), "TR": ("sbuf", [128, 48], "bfloat16"),
+    "eT": ("sbuf", [128, 48], "bfloat16"), "gT": ("sbuf", [128, 48], "bfloat16"), "EW": ("sbuf", [128, 34], "float32"),
+    "TQ": ("sbuf", [128, 16], "bfloat16"), "PW": ("sbuf", [128, 16], "bfloat16"),
     "P5": ("sbuf", [128, 80], "float32"), "S5": ("sbuf", [128, 80], "float32"), "oU": ("sbuf", [128, 16], "uint16"),
-    "inv": ("sbuf", [128, 768], "bfloat16"), "NA": ("sbuf", [128, 48], "float32"), "NB": ("sbuf", [128, 48], "float32"),
-    "NS": ("sbuf", [128, 48], "float32"), "NP": ("sbuf", [128, 24], "uint16"),
+    "inv": ("sbuf", [128, 768], "bfloat16"), "NS": ("sbuf", [128, 24], "float32"), "NP": ("sbuf", [128, 24], "uint16"),
     "sg": ("sbuf", [128, 400], "bfloat16"), "C0": ("sbuf", [128, 272], "bfloat16"), "C1": ("sbuf", [128, 272], "bfloat16"),
     "SC": ("sbuf", [128, 272], "bfloat16"), "P1": ("sbuf", [128, 128], "bfloat16"), "P4": ("sbuf", [128, 128], "bfloat16"),
-    "TU": ("sbuf", [128, 96], "uint16"), "Tr": ("sbuf", [128, 512], "bfloat16"),
+    "TU": ("sbuf", [128, 96], "uint16"), "Tr": ("sbuf", [128, 544], "bfloat16"),
     "HL": ("sbuf", [128, 72], "uint16"), "yL": ("sbuf", [128, 96], "uint16"), "tL": ("sbuf", [128, 96], "uint16"),
     "YR": ("sbuf", [128, 1536], "bfloat16"), "Z": ("sbuf", [128, 512], "bfloat16"), "MU": ("sbuf", [128, 72], "uint16"),
     "mr": ("sbuf", [128, 384], "float32"),
@@ -52,7 +51,8 @@ SCRATCH = {
 for _k in range(8):
     SCRATCH["ps%d" % _k] = ("psum", [128, 512], "float32")
 SEMAPHORES = (["cV", "cA", "cT", "cG", "loc"] + ["d%d" % k for k in range(24)]
-              + ["a%s%d" % (n, k) for n in "ytsh" for k in range(3)] + ["ai"])
+              + ["a%s%d" % (n, k) for n in "yts" for k in range(3)] + ["ai"]
+              + ["ah%d%d" % (r, k) for r in range(3) for k in range(len(HP[r]))])
 
 
 def rank_program(g, core, T, topo):
@@ -160,8 +160,8 @@ def rank_program(g, core, T, topo):
     def scan(out, z, a, o=op.add):
         emit("V", lambda: g.vector.tensor_tensor_scan(v(out), v(z), v(a), 0.0, op.mult, o), [z, a], [out])
 
-    def hold(a, n):
-        f = R("SF", 0, n)
+    def hold(a, n, o=0):
+        f = R("SF", o, o + n)
         emit("V", lambda: g.vector.tensor_tensor_scan(v(f), v(R("MX", 0, n)), v(a), 0.0, op.add, op.max), [R("MX", 0, n), a], [f])
 
     def held(out, a, b, k):
@@ -222,14 +222,20 @@ def rank_program(g, core, T, topo):
 
     def tree_engines(a, b):
         return topo.engines(a, b)[-8:]
+
+    def lands(r, sem, n):
+        acc.setdefault(r[0], []).append((r, True, "R", (sem, n)))
     for r in range(3):
         n = len(topo.engines(part[r], core))
-        acc.setdefault("yL", []).append((R("yL", 32 * r, 32 * r + 32), True, "R", ("ay%d" % r, len(tree_engines(part[r], core)))))
-        if r == 0:
-            acc["yL"] = [(R("yL", 0, 16), True, "R", ("ai", n)), (R("yL", 16, 32), True, "R", ("ay0", n))]
-        acc.setdefault("tL", []).append((R("tL", 32 * r, 32 * r + 32), True, "R", ("at%d" % r, n)))
-        acc.setdefault("hP", []).append((cols("hP", r), True, "R", ("as%d" % r, n)))
-        acc.setdefault("hL", []).append((cols("hL", r), True, "R", ("ah%d" % r, n)))
+        lands(cols("hP", r), "as%d" % r, n)
+        for k, (a, b) in enumerate(HP[r]):
+            lands(cols("hL", r, a, b), "ah%d%d" % (r, k), n)
+        if r:
+            lands(R("yL", 32 * r, 32 * r + 32), "ay%d" % r, len(tree_engines(part[r], core)))
+            lands(R("tL", 32 * r, 32 * r + 32), "at%d" % r, n)
+        else:
+            lands(R("yL", 0, 16), "ai", n)
+            lands(R("YR", 256, 512), "ay0", n)
 
     def remote(dst, out, in_, rd, sem, e=None):
         order("G", rd, [])
@@ -238,8 +244,11 @@ def rank_program(g, core, T, topo):
         g.remote_dma(out_ap=out, in_ap=in_, remote_sem=T.sem[sem], local_sem=T.sem.loc, pid=pid, routing_id=rid, dma_engine_mask=some(e))
         loc[0] += len(e)
 
-    def send_h(r):
-        remote(part[r], b8(cols("hL", r)), b8(cols("hq", r)), [cols("hq", r)], "ah%d" % r)
+    def send_h(r, k):
+        a, b = HP[r][k]
+        remote(part[r], b8(cols("hL", r, a, b)), b8(cols("hq", r, a, b)), [cols("hq", r, a, b)], "ah%d%d" % (r, k))
+
+    def send_s(r):
         remote(part[r], v(cols("hP", r)), v(cols("hs", r)), [cols("hs", r)], "as%d" % r)
 
     def send_t(r):
@@ -257,7 +266,7 @@ def rank_program(g, core, T, topo):
                        (16, [[32, 2], [64, 4], [2, 2]], -384), (32, [[1, 8], [0, 2]], 1),
                        (48, [[-92, 2]], 100), (50, [[8, 2]], 4), (52, [[4, 4]], 2), (56, [[2, 8]], 1)])
     table("lb", 0, 1, [(0, [[7, 2]], 1), (2, [[0, 2]], 4), (4, [[0, 4]], 2), (8, [[0, 8]], 1)])
-    table("TB", 0, 1, [(64, [[0, 2], [1, 8], [0, 2]], 0), (96, [[1, 8], [0, 2]], 8), (112, [[0, 112]], 1)])
+    table("TB", 0, 1, [(64, [[0, 2], [1, 8], [0, 2]], 0), (96, [[1, 8], [0, 2]], 8), (112, [[0, 96]], 1)])
     table("TB", 128, 5, [(0, [[1, 16]], 0)])
     table("TB", 129, 5, [(2, [[1, 7], [0, 2]], 1)])
     table("TB", 130, 5, [(4, [[1, 3], [0, 4]], 1)])
@@ -265,11 +274,7 @@ def rank_program(g, core, T, topo):
     table("TB", 129, 1, [(0, [[0, 3]], 0)])
     for k in range(4):
         table("TB", 224 + k, 4, [(0, [[16, 16 >> k], [0, 2 << k]], 31)])
-    table("TB", 224, 1, [(0, one, 15)])
-    iota(R("JC"), [[16, 16], [0, 5]], 400, 1)
-    iota(R("JC", 4, 80, 5), [[0, 16]], 1)
-    iota(R("VR", 0, 16), [[2, 16]], -256)
-    iota(R("VR", 16, 256), [[32, 15], [1, 16]], -224)
+    table("TB", 224, 1, [(0, one, 15), (128, [[1, 2], [2, 16]], 0)])
 
     fill(R("EB", 512, 1026), 0.0)
     const(R("R0"), 1, "EB", 512)
@@ -286,11 +291,16 @@ def rank_program(g, core, T, topo):
     ts(R("mk", 0, 128), R("t2"), 0.0, None, op.is_equal)
     tc(R("KF"), R("KX"))
     tc(R("EB", 513, 1024, 4), R("idn"))
-    act(R("EB", 1026, 2048), R("EB", 0, 1022))
     quant(R("eq", 0, 256), R("es", 0, 256), R("EB", 0, 1024))
     ts(R("UL"), R("i2", 0, 64, 8), 384.0, None, op.add)
     q_, bit, q0 = R("KF", 0, 1), R("KF", 1, 2), R("mk", 0, 1)
     act(R("mk", 128, 256), R("mk", 0, 128))
+    act(R("mk", 256, 384), R("mk", 0, 128))
+    act(R("AD", 1, 2), q_, AF.Identity, scale=1024.0, bias=-15360.0)
+    act(R("AD", 0, 1), q0, AF.Identity, scale=768.0, bias=0.5)
+    act(R("AD", 4, 5), bit)
+    act(R("AD", 5, 6), bit, AF.Identity, bias=768.0)
+    act(R("MX"), R("mk", 0, 160), AF.Identity, scale=-33792.0, bias=1024.0)
     ts(R("paI"), R("seI"), 1, None, op.arith_shift_right)
     ts(R("slI"), R("seI"), 1, None, op.bitwise_and)
     quant(R("uq"), R("us"), R("ub"))
@@ -300,15 +310,10 @@ def rank_program(g, core, T, topo):
     act(R("ups"), R("us"), ind=R("UL"))
     emit("V", lambda: g.vector.tensor_copy(v(R("upq")).bitcast(dt.uint32), v(R("uq")).bitcast(dt.uint32).indirect(v(R("UL")))),
          [R("uq"), R("UL")], [R("upq")])
-    act(R("mk", 256, 384), R("mk", 0, 128))
-    act(R("AD", 1, 2), q_, AF.Identity, scale=1024.0, bias=-15360.0)
-    act(R("MX"), R("mk", 0, 288), AF.Identity, scale=-33792.0, bias=1024.0)
-    act(R("AD", 0, 1), q0, AF.Identity, scale=768.0, bias=0.5)
-    act(R("AD", 4, 5), bit)
-    act(R("AD", 5, 6), bit, AF.Identity, bias=768.0)
     act(R("Nc", 0, 768, 2), R("i2", 0, 384))
     act(R("Nc", 1, 768, 2), R("i2", 0, 384))
     act(R("AD", 3, 4), bit, AF.Identity, bias=384.0)
+    act(R("EB", 1026, 2048), R("EB", 0, 1022))
 
     SK, HK, FK, AK = [0, 1, 2], [3, 4, 5, 6], [7, 0, 1, 2], [3, 4, 5, 6]
 
@@ -326,10 +331,10 @@ def rank_program(g, core, T, topo):
         a, b = CH[k]
         ts(R("sg", a, b), R("ps%d" % SK[k], 0, b - a), 0.0, 0.5, op.is_ge, op.subtract)
 
-    def layer(r, t, cast=True):
-        mm(HK[t], C, R("wq", 128 * t, 128 * t + 128), R("wp", 128 * t, 128 * t + 128), cols("xq", r), cols("xs", r))
+    def layer(r, t, banks=HK, a=0, b=C, cast=True):
+        mm(banks[t], b - a, R("wq", 128 * t, 128 * t + 128), R("wp", 128 * t, 128 * t + 128), cols("xq", r, a, b), cols("xs", r, a, b))
         if cast:
-            act(R("hb", t, 4 * C, 4), R("ps%d" % HK[t], 0, C), scale=0.03125)
+            act(R("hb", 4 * a + t, 4 * b, 4), R("ps%d" % banks[t], 0, b - a), scale=0.03125)
 
     def scaled(t, a, b):
         ts(R("hb", 4 * a + t, 4 * b, 4), R("ps%d" % HK[t], a, b), 0.03125, None, op.mult)
@@ -338,11 +343,11 @@ def rank_program(g, core, T, topo):
         a, b = CH[k]
         quant(cols("hq", r, a, b), cols("hs", r, a, b), R("hb", 4 * a, 4 * b))
 
-    def unpack(r, t):
-        mm(FK[t], C, *unit(t), cols("xq", r), cols("xs", r))
+    def unpack(r, t, banks=FK):
+        mm(banks[t], C, *unit(t), cols("xq", r), cols("xs", r))
 
-    def own(f, t, a=0, b=C):
-        f(cols("fb", t, a, b), R("ps%d" % FK[t], a, b))
+    def own(t, banks=FK):
+        act(cols("fb", t), R("ps%d" % banks[t], 0, C))
 
     def above(t):
         act(cols("bb", t), cols("fb", t), ind=R("paU"))
@@ -365,10 +370,10 @@ def rank_program(g, core, T, topo):
             scan(R("SB", a, b), R("R0", 0, b - a), R("GM", a, b))
             slip()
 
-    def maps(win, ind, at, r):
+    def maps(win, ind, at, r, x, y):
         dist2(win, ind, at)
         for a, b in HALF:
-            ts(R("MU", 24 * r + a // 16, 24 * r + b // 16), R("SB", a + 15, b, 16), 256.0, None, op.add)
+            ts(R("MU", 24 * r + a // 16, 24 * r + b // 16), R("SB", a + 15, b, 16), x, y, op.add, op.mult)
 
     def picked(r, t, a=0, b=C):
         act(cols("ag", t, a, b), cols("ab", t), ind=R("MU", 24 * r + a // 16, 24 * r + b // 16))
@@ -377,11 +382,12 @@ def rank_program(g, core, T, topo):
         tt(R("xn", 4 * a + t, 4 * b, 4), cols("ag", t, a, b), cols("bb", t, a, b), op.add)
 
     def state(r):
+        picked(r, 2)
         picked(r, 3)
         for a, b in HALF:
             renew(r, 0, a, b)
         renew(r, 1)
-        renew(r, 2)
+        add(2, 0, C)
         add(3, 0, 128)
         add(3, 128, C)
         for k, (a, b) in enumerate(CH):
@@ -391,13 +397,17 @@ def rank_program(g, core, T, topo):
     for k, (a, b) in enumerate(CH):
         pack_x(0, "xb", a, b)
         score(0, k)
-        if k == 0:
-            quant(R("eq", 256, 512), R("es", 256, 512), R("EB", 1024, 2048))
-    hold(R("TB", 0, 64), 64)
     for k in range(len(CH)):
         sign(k)
-    ts(R("PF"), R("SF", 31, 64, 32), R("AD", 1, 2), None, op.add)
-    held(R("PL", 0, 4), 0, 4, 1)
+    for t in range(4):
+        layer(0, t, HK, *HP[0][0])
+    hold(R("TB", 0, 64), 64)
+    tc(R("L", 112, 114), R("AD", 4, 6))
+    rest.extend([lambda: None, lambda: None, lambda: ts(R("PF"), R("SF", 31, 64, 32), R("AD", 1, 2), None, op.add),
+                 lambda: (ts(R("sb", 0, 1), R("paI", 0, 1), 2.0, R("AD", 0, 1), op.mult, op.add), held(R("PL", 0, 4), 0, 4, 1))])
+    dist2(R("sg"), "paU", 0)
+    for t in range(4):
+        layer(0, t, FK, *HP[0][1])
     act(R("AD", 8, 10), R("AD", 6, 8), AF.Identity, scale=0.0, bias=R("AD", 4, 5))
     act(R("AD", 12, 13), q_, AF.Identity, bias=0.5)
     act(R("lb", 16, 32), R("lb", 0, 16))
@@ -406,117 +416,107 @@ def rank_program(g, core, T, topo):
         act(R(o, 0, 16), R("TB", 48, 64), f, scale=-1.0, bias=R("PF", 1, 2))
         act(R(o, 16, 32), R("TB", 48, 64), f, scale=-1.0, bias=R("AD", 12, 13))
     act(R("l32"), R("lb"), AF.Identity, scale=32.0)
-    for t in range(4):
-        layer(0, t)
-    rest.extend([lambda: None, lambda: tc(R("L", 112, 114), R("AD", 4, 6)),
-                 lambda: ts(R("sb", 0, 1), R("paI", 0, 1), 2.0, R("AD", 0, 1), op.mult, op.add),
-                 lambda: ts(R("mW"), R("i2", 0, 128), R("PF", 0, 1), -1024.0, op.not_equal, op.mult)])
-    dist2(R("sg"), "paU", 0)
     tt(R("sw"), R("SB", 15, C, 16), R("sh"), op.mult)
-    tt(R("AM", 0, 32), R("lb"), R("ad"), op.is_gt)
-    tt(R("sl"), R("sn"), R("l32"), op.mult)
+    quant(R("eq", 256, 384), R("es", 256, 384), R("EB", 1024, 1536))
     tt(R("s24"), R("sb"), R("sw"), op.subtract)
-    tt(R("C0", 0, 32), R("sl"), R("AM", 0, 32), op.mult)
+    quant(R("eq", 384, 512), R("es", 384, 512), R("EB", 1536, 2048))
     tc(R("stU"), R("s24"))
-    tt(R("C0", 0, 16), R("C0", 0, 16), R("C0", 16, 32), op.subtract)
+    pack_h(0, 0)
+    send_h(0, 0)
     tc(R("Nc"), R("i2", 0, 384), oind=R("stU"))
     const(R("PW"), 0)
     act(R("AM", 32, 48), R("mk", 0, 16))
     for t in range(4):
-        unpack(0, t)
-        own(act, t)
+        unpack(0, t, HK)
+        own(t, HK)
         if t == 1:
             const(R("R5"), 1)
-            const(R("EW", 34, 36), 0)
+            const(R("SB2", 256, 288), 0)
             act(R("AD", 2, 3), q_, AF.Identity, scale=512.0, bias=-7488.0)
             const(R("R5", 0, 80, 5), 0)
     nc = R("Nc", 0, 768)
     up = R("AD", 3, 4)
-    pack_h(0, 0)
-    ts(R("L", 0, 16), nc, up, None, op.add, ind=R("L", 112, 113))
     pack_h(0, 1)
-    ts(R("L", 16, 48), nc, up, None, op.add, ind=R("L", 0, 2))
+    ts(R("L", 0, 16), nc, up, None, op.add, ind=R("L", 112, 113))
     pack_h(0, 2)
-    send_h(0)
+    ts(R("L", 16, 48), nc, up, None, op.add, ind=R("L", 0, 2))
+    ts(R("mW"), R("i2", 0, 128), R("PF", 0, 1), -1024.0, op.not_equal, op.mult)
+    tt(R("AM", 0, 32), R("lb"), R("ad"), op.is_gt)
+    send_h(0, 1)
+    send_s(0)
+    iota(R("JC"), [[16, 16], [0, 5]], 400, 1)
+    iota(R("JC", 4, 80, 5), [[0, 16]], 1)
+    iota(R("VR", 0, 16), [[1, 16]], 240)
+    iota(R("VR", 16, 256), [[32, 15], [1, 16]], -240)
     iota(R("inv", 0, C), [[0, C]], 0)
-    iota(R("iC"), [[1, 512]], -256)
     ts(R("L", 48, 112, 2), nc, up, None, op.add, ind=R("L", 30, 32))
     ts(R("L", 49, 112, 2), nc, up, None, op.add, ind=R("L", 32, 34))
-    hold(R("TB", 64, 352), 288)
+    hold(R("TB", 64, 208), 144)
     tt(R("GM", 0, 128), nc, R("mW"), op.add, R("L", 76, 84))
     tc(R("Lf"), R("L"))
     y4 = R("SB2", 31, 32)
     fold(y4, R("GM", 0, 128), op.max)
     tt(R("g16"), R("Lf"), R("mk", 0, 16), op.mult, R("PL", 0, 1))
-    held(R("PL", 4, 22), 0, 18, 1)
+    held(R("PL", 4, 13), 0, 9, 1)
     ts(R("LL", 2, 4), R("AD", 6, 8), y4, None, op.add)
     rest.extend([
         lambda: (fold(R("yt", 0, 1), R("g16"), op.add), ts(R("YB", 2, 3), y4, 384.0, 0.5, op.add, op.mult)),
-        lambda: ts(R("YB", 0, 2), R("AD", 10, 12), R("yt", 0, 1), 0.5, op.add, op.mult),
+        lambda: (ts(R("YB", 0, 2), R("AD", 10, 12), R("yt", 0, 1), 0.5, op.add, op.mult), tt(R("sl"), R("sn"), R("l32"), op.mult)),
         lambda: quant(R("vq"), R("vs"), R("vb")),
         lambda: tc(R("TR"), R("i2"), ind=R("YB", 0, 3)),
         lambda: (tc(R("TQ"), R("i2"), ind=R("YB", 0, 1)), tc(R("EW", 18, 20), R("YB", 1, 3))),
         lambda: tt(R("eT"), R("TQ"), R("TR"), op.is_equal, R("PL", 4, 7)),
-        lambda: ts(R("PW", 1, 8), R("SB2", 31, 128, 16), 384.0, 0.5, op.add, op.mult),
-        lambda: tt(R("gT"), R("eT"), R("AM"), op.mult),
+        lambda: (tc(R("PW", 1, 8), R("SB2", 31, 128, 16)), tt(R("C0", 0, 32), R("sl"), R("AM", 0, 32), op.mult)),
+        lambda: (tt(R("gT"), R("eT"), R("AM"), op.mult), tt(R("C0", 0, 16), R("C0", 0, 16), R("C0", 16, 32), op.subtract)),
         lambda: (fold(R("EW", 0, 1), R("gT", 0, 16), op.max), fold(R("EW", 1, 2), R("gT", 16, 48), op.max)),
     ])
     slip()
+    low = R("SB2", 47, 256, 16)
     for n in (2, 4, 8):
         w = dist(nc, R("LL", n, 2 * n), 16 * n, "SB2", 16 * n)
+        if n == 8:
+            tt(R("EW", 2, 18), R("PW", 0, 9), R("SB2", 47, 288, 16), op.is_equal, R("PL", 2, 3))
+            ts(R("EW", 20, 34), low, 384.0, 0.5, op.add, op.mult)
         ts(R("LL", 2 * n, 4 * n, 2), w, 384.0, None, op.add)
         ts(R("LL", 2 * n + 1, 4 * n, 2), w, 385.0, None, op.add)
         if n < 8:
             slip()
-    for t in range(CFG["ga"]):
-        above(t)
-    act(R("GA"), nc, ind=R("LL", 24, 32))
-    const(R("NA", 0, 48, 2), 0)
-    act(R("NB", 0, 48, 2), R("sw"), AF.Identity, scale=-15.0, bias=7.5)
-    act(R("sp", 1, 24), R("sw", 1, 24), AF.Identity, scale=-1.0, bias=256.5)
-    act(R("AD", 13, 14), q0, AF.Identity, bias=-1.0)
-    act(R("AD", 14, 15), q0, AF.Identity, scale=-1.5, bias=256.5)
+    act(R("sp", 1, 24), R("sw", 1, 24), AF.Identity, scale=-16.0, bias=280.0)
+    act(R("AD", 13, 14), q0, AF.Identity, scale=16.0, bias=-16.0)
+    act(R("AD", 14, 15), q0, AF.Identity, scale=-520.0, bias=280.0)
     act(R("sp", 0, 1), R("sw", 0, 1), AF.Identity, scale=R("AD", 13, 14), bias=R("AD", 14, 15))
-    for t in range(CFG["ga"], 4):
+    for t in range(3):
         above(t)
-    low = R("SB2", 47, 256, 16)
-    ts(R("EW", 20, 34), low, 384.0, 0.5, op.add, op.mult)
+    act(R("GA"), nc, ind=R("LL", 16, 32))
+    above(3)
     ts(R("YB", 3, 17), low, 384.0, 0.5, op.add, op.mult)
-    remote(part[0], v(R("yL", 0, 16)), v(R("YB", 1, 17)), [R("YB", 1, 17)], "ai")
-    tt(R("GM", 128, 256), nc, R("mk", 0, 128), op.mult, R("LL", 16, 24))
-    tt(R("EW", 2, 18), R("PW", 0, 9), R("EW", 20, 36), op.is_equal, R("PL", 2, 3))
-    slip(12)
-    scan(R("SB", 0, 128), R("R0", 0, 128), R("GM", 128, 256))
     tt(R("P5"), R("EW"), R("JC"), op.mult, R("PL", 8, 13))
-    hold(R("GA"), 128)
-    ts(R("YB", 17, 25), R("SB", 15, 128, 16), 384.0, 0.5, op.add, op.mult)
+    remote(part[0], v(R("yL", 0, 16)), v(R("YB", 1, 17)), [R("YB", 1, 17)], "ai")
+    remote(part[0], v(R("YR", 256, 512)), v(R("GA")), [R("GA")], "ay0")
+    iota(R("iC"), [[1, 512]], -256)
+    hold(R("TB", 224, 384), 160)
     scan(R("S5"), R("R5"), R("P5"), op.max)
-    ts(R("YB", 25, 33), R("SF", 15, 128, 16), 0.5, R("AD", 2, 3), op.mult, op.add)
-    remote(part[0], v(R("yL", 16, 32)), v(R("YB", 17, 33)), [R("YB", 17, 33)], "ay0")
-    send_y(1)
-    send_y(2)
+    held(R("PL", 14, 24), 0, 10, 1)
     tc(R("oU"), R("S5", 4, 80, 5))
+    hold(R("GA", 0, 128), 128)
     tc(R("inv"), R("VR"), oind=R("oU"))
+    hold(R("GA", 128, 256), 128, 128)
+    rest.append(lambda: (ts(R("YB", 17, 33), R("SF", 15, 256, 16), 0.5, R("AD", 2, 3), op.mult, op.add), send_y(1), send_y(2)))
     dist2(R("inv", 0, C), "paU", 0)
     for a, b in HALF:
-        w = R("SB", a + 15, b, 16)
-        ts(R("NA", a // 8 + 1, b // 8, 2), w, -224.0, None, op.is_ge)
-        tt(R("NB", a // 8 + 1, b // 8, 2), w, R("sp", a // 16, b // 16), op.add)
+        tt(R("NS", a // 16, b // 16), R("SB", a + 15, b, 16), R("sp", a // 16, b // 16), op.add)
     for a, b in HALF:
-        scan(R("NS", a // 8, b // 8), R("NA", a // 8, b // 8), R("NB", a // 8, b // 8))
-    for a, b in HALF:
-        tc(R("NP", a // 16, b // 16), R("NS", a // 8 + 1, b // 8, 2))
+        tc(R("NP", a // 16, b // 16), R("NS", a // 16, b // 16))
     iota(R("PS"), [[0, 128]], 0)
     for k in range(4):
         table("PS", k, 4, [(2 << k, [[0, (16 >> k) - 1], [2, 2], [0, 1 << k]], -1)])
     table("PS", 0, 1, [(0, one, 1)])
-    for t in range(CFG["ac"]):
+    arrived(0, 0)
+    act(R("YR", 0, 256), R("i2"), ind=R("yL", 0, 16))
+    act(R("YR", 512, 544), R("YR", 0, 32), ind=R("PL", 22, 24))
+    for t in range(1, 4):
         arrived(0, t)
-    for a in (0, 16):
-        act(R("YR", 16 * a, 16 * a + 256), R("iC"), ind=R("yL", a, a + 16))
-    for t in range(CFG["ac"], 4):
-        arrived(0, t)
-    maps(R("YR", 0, 512), "NP", 0, 0)
+    maps(R("YR", 0, 544), "NP", 0, 0, 384.0, 0.5)
     state(0)
     for m, x in ((1, 16.0), (2, 8.0), (4, 4.0), (8, 2.0)):
         act(R("C0", 16 + 16 * m, 16 + 32 * m), R("mk", 0, 16 * m), AF.Identity, scale=x)
@@ -531,11 +531,11 @@ def rank_program(g, core, T, topo):
         for k in range(len(CH)):
             sign(k)
         for t in (0, 2, 1, 3):
-            layer(r, t, t < 2)
+            layer(r, t, cast=t < 2)
         for t in range(4):
             unpack(r, t)
-        for t in range(CFG["fa"]):
-            own(act, t)
+        own(0)
+        own(1)
         tt(R(c1), R("sg"), R(c0), op.mult, R("YB", 0, 17))
         scaled(2, *HALF[0])
         scan(R("SC"), R("R0", 0, 272), R(c1))
@@ -546,15 +546,16 @@ def rank_program(g, core, T, topo):
         scaled(3, *HALF[1])
         ts(R("TU", 32 * r, 32 * r + 32), R("P4", 3, 128, 4), R("SC", 31, 32), float(r), op.add, op.mult)
         send_t(r)
-        k = CFG["trv"]
-        act(R("Tr", 16 * k, 512), R("iC"), ind=R("TU", 32 * r + k, 32 * r + 32))
+        act(R("Tr", 16 * TV, 512), R("iC"), ind=R("TU", 32 * r + TV, 32 * r + 32))
         for m in range(len(CH)):
             pack_h(r, m)
-        send_h(r)
-        if k:
-            tc(R("Tr", 0, 16 * k), R("iC"), ind=R("TU", 32 * r, 32 * r + k))
-        for t in range(CFG["fa"], 4):
-            own(act, t)
+        send_h(r, 0)
+        send_s(r)
+        tc(R("Tr", 0, 32), R("iC"), ind=R("TU", 32 * r, 32 * r + 2))
+        tc(R("Tr", 32, 16 * TV), R("iC"), ind=R("TU", 32 * r + 2, 32 * r + TV))
+        tc(R("Tr", 512, 544), R("Tr", 0, 32), ind=R("PL", 22, 24))
+        own(2)
+        own(3)
         dist2(R("Tr"), "NP", 0)
         ts(R("HL", 24 * r, 24 * r + 24), R("SB", 15, C, 16), 256.0, None, op.add)
         for t in range(4):
@@ -562,7 +563,7 @@ def rank_program(g, core, T, topo):
         for t in range(4):
             arrived(r, t)
         tc(R("Z"), R("YR", 512 * r, 512 * r + 512), oind=R("tL", 32 * r, 32 * r + 32))
-        maps(R("Z"), "HL", 24 * r, r)
+        maps(R("Z"), "HL", 24 * r, r, 256.0, 1.0)
         if r == 1:
             state(r)
             yrep(2)
@@ -573,7 +574,10 @@ def rank_program(g, core, T, topo):
         renew(2, t, a, b)
     for t in range(4):
         picked(2, t, c, d)
+    act(R("mr"), R("Z"), AF.Identity, ind=R("HL", 48, 72), bias=256.0)
+    dma("A", T.im[:, :], T.mr[0:128:16, 0:C], [R("mr")], [])
     add(0, c, d)
+    add(1, c, d)
     for k, (a, b) in enumerate(LAST):
         pack_x(3, "xn", a, b)
         q3, s3 = cols("xq", 3, a, b), cols("xs", 3, a, b)
@@ -581,14 +585,12 @@ def rank_program(g, core, T, topo):
         dma("Y", T.oc[:, 4 * a:4 * b], b8(q3), [q3], [])
         if k:
             for m in range(4):
-                dma("Y", T.osc[4 * m:4 * m + 4, :], T.xs[32 * m:32 * m + 4, 3 * C:4 * C], [cols("xs", 3)], [])
+                dma("YA"[m // 2], T.osc[4 * m:4 * m + 4, :], T.xs[32 * m:32 * m + 4, 3 * C:4 * C], [cols("xs", 3)], [])
         (tc if k else act)(R("yb", a, b), R("ps%d" % SK[k], 0, b - a))
-        dma("AY"[k], T.y[:, a:b], v(R("yb", a, b)), [R("yb", a, b)], [])
+        dma("A", T.y[:, a:b], v(R("yb", a, b)), [R("yb", a, b)], [])
         if not k:
-            for t in range(1, 4):
+            for t in range(2, 4):
                 add(t, c, d)
-            act(R("mr"), R("Z"), AF.Identity, ind=R("HL", 48, 72), bias=256.0)
-            dma("A", T.im[:, :], T.mr[0:128:16, 0:C], [R("mr")], [])
     for q, s in dmas:
         wait(q, (s, 16))
     for q in ("V", "A", "T", "G"):

from concourse.mybir import dt, AluOpType, AxisListType, ActivationFunctionType as AF

C = 384
CH = [(0, 128), (128, 256), (256, 384)]
HALF = [(0, 192), (192, 384)]
LAST = [(0, 256), (256, 384)]
HP = [[(0, 128), (128, C)], [(0, C)], [(0, C)]]
TV = 12
SCRATCH = {
    "tm": ("sbuf", [128, 128], "int32"), "t2": ("sbuf", [128, 128], "int32"), "KX": ("sbuf", [128, 2], "int32"),
    "KF": ("sbuf", [128, 2], "float32"), "AD": ("sbuf", [128, 16], "float32"),
    "UL": ("sbuf", [128, 8], "uint16"), "idn": ("sbuf", [128, 128], "bfloat16"), "EB": ("sbuf", [128, 2048], "bfloat16"),
    "eq": ("sbuf", [128, 512], "float8_e4m3fn_x4"), "es": ("sbuf", [128, 512], "uint8"),
    "i2": ("sbuf", [128, 400], "bfloat16"), "iC": ("sbuf", [128, 512], "bfloat16"), "mk": ("sbuf", [128, 384], "bfloat16"),
    "R0": ("sbuf", [128, 384], "bfloat16"), "R4": ("sbuf", [128, 128], "bfloat16"), "R5": ("sbuf", [128, 80], "float32"),
    "MX": ("sbuf", [128, 160], "bfloat16"), "TB": ("sbuf", [128, 384], "float32"), "SF": ("sbuf", [128, 320], "float32"),
    "PL": ("sbuf", [128, 24], "uint16"), "PF": ("sbuf", [128, 2], "float32"), "PS": ("sbuf", [128, 128], "bfloat16"),
    "mW": ("sbuf", [128, 128], "bfloat16"), "lb": ("sbuf", [128, 32], "float32"),
    "l32": ("sbuf", [128, 32], "float32"), "ad": ("sbuf", [128, 32], "float32"), "sn": ("sbuf", [128, 32], "float32"),
    "sl": ("sbuf", [128, 32], "float32"), "AM": ("sbuf", [128, 48], "bfloat16"), "JC": ("sbuf", [128, 80], "float32"),
    "VR": ("sbuf", [128, 256], "bfloat16"),
    "seI": ("sbuf", [128, 24], "int32"), "paI": ("sbuf", [128, 24], "int32"), "paU": ("sbuf", [128, 24], "uint16"),
    "slI": ("sbuf", [128, 24], "int32"), "sh": ("sbuf", [128, 24], "float32"), "sb": ("sbuf", [128, 24], "float32"),
    "sw": ("sbuf", [128, 24], "float32"), "s24": ("sbuf", [128, 24], "float32"), "stU": ("sbuf", [128, 24], "uint16"),
    "sp": ("sbuf", [128, 24], "float32"),
    "xb": ("sbuf", [128, 1536], "bfloat16"), "ub": ("sbuf", [128, 512], "bfloat16"),
    "vb": ("sbuf", [128, 512], "bfloat16"), "wq": ("sbuf", [128, 512], "float8_e4m3fn_x4"), "wp": ("sbuf", [128, 512], "uint8"),
    "uq": ("sbuf", [128, 128], "float8_e4m3fn_x4"), "us": ("sbuf", [128, 128], "uint8"),
    "upq": ("sbuf", [128, 128], "float8_e4m3fn_x4"), "ups": ("sbuf", [128, 128], "uint8"),
    "vq": ("sbuf", [128, 128], "float8_e4m3fn_x4"), "vs": ("sbuf", [128, 128], "uint8"),
    "Nc": ("sbuf", [128, 784], "bfloat16"), "L": ("sbuf", [128, 114], "uint16"), "Lf": ("sbuf", [128, 114], "float32"),
    "LL": ("sbuf", [128, 32], "uint16"), "g16": ("sbuf", [128, 16], "float32"), "yt": ("sbuf", [128, 2], "float32"),
    "GM": ("sbuf", [128, 384], "bfloat16"), "SB": ("sbuf", [128, 384], "bfloat16"), "SB2": ("sbuf", [128, 288], "bfloat16"),
    "GA": ("sbuf", [128, 256], "bfloat16"), "YB": ("sbuf", [128, 34], "uint16"), "TR": ("sbuf", [128, 48], "bfloat16"),
    "eT": ("sbuf", [128, 48], "bfloat16"), "gT": ("sbuf", [128, 48], "bfloat16"), "EW": ("sbuf", [128, 34], "float32"),
    "TQ": ("sbuf", [128, 16], "bfloat16"), "PW": ("sbuf", [128, 16], "bfloat16"),
    "P5": ("sbuf", [128, 80], "float32"), "S5": ("sbuf", [128, 80], "float32"), "oU": ("sbuf", [128, 16], "uint16"),
    "inv": ("sbuf", [128, 768], "bfloat16"), "NS": ("sbuf", [128, 24], "float32"), "NP": ("sbuf", [128, 24], "uint16"),
    "sg": ("sbuf", [128, 400], "bfloat16"), "C0": ("sbuf", [128, 272], "bfloat16"), "C1": ("sbuf", [128, 272], "bfloat16"),
    "SC": ("sbuf", [128, 272], "bfloat16"), "P1": ("sbuf", [128, 128], "bfloat16"), "P4": ("sbuf", [128, 128], "bfloat16"),
    "TU": ("sbuf", [128, 96], "uint16"), "Tr": ("sbuf", [128, 544], "bfloat16"),
    "HL": ("sbuf", [128, 72], "uint16"), "yL": ("sbuf", [128, 96], "uint16"), "tL": ("sbuf", [128, 96], "uint16"),
    "YR": ("sbuf", [128, 1536], "bfloat16"), "Z": ("sbuf", [128, 512], "bfloat16"), "MU": ("sbuf", [128, 72], "uint16"),
    "mr": ("sbuf", [128, 384], "float32"),
    "xq": ("sbuf", [128, 1536], "float8_e4m3fn_x4"), "xs": ("sbuf", [128, 1536], "uint8"), "hb": ("sbuf", [128, 1536], "bfloat16"),
    "hq": ("sbuf", [128, 1152], "float8_e4m3fn_x4"), "hs": ("sbuf", [128, 1152], "uint8"),
    "hL": ("sbuf", [128, 1152], "float8_e4m3fn_x4"), "hP": ("sbuf", [128, 1152], "uint8"),
    "fb": ("sbuf", [128, 1536], "bfloat16"), "bb": ("sbuf", [128, 1536], "bfloat16"), "ab": ("sbuf", [128, 1536], "bfloat16"),
    "ag": ("sbuf", [128, 1536], "bfloat16"), "xn": ("sbuf", [128, 1536], "bfloat16"), "yb": ("sbuf", [128, 384], "float32"),
}
for _k in range(8):
    SCRATCH["ps%d" % _k] = ("psum", [128, 512], "float32")
SEMAPHORES = (["cV", "cA", "cT", "cG", "loc"] + ["d%d" % k for k in range(24)]
              + ["a%s%d" % (n, k) for n in "yts" for k in range(3)] + ["ai"]
              + ["ah%d%d" % (r, k) for r in range(3) for k in range(len(HP[r]))])


def rank_program(g, core, T, topo):
    rank = T.rank_of(core)
    if rank is None:
        return
    op = AluOpType
    eng = {"V": g.vector, "A": g.scalar, "T": g.tensor, "G": g, "Y": g.sync}
    cnt = {q: 0 for q in eng}
    know = {q: {} for q in eng}
    snap = {}
    acc = {}
    dmas = []
    loc = [0]

    def R(n, a=0, b=None, s=1):
        return (n, a, SCRATCH[n][1][1] if b is None else b, s)

    def v(r):
        n, a, b, s = r
        return T[n][:, a:b] if s == 1 else T[n][:, a:b:s]

    def meet(a, b):
        if a[3] == b[3] and a[3] > 1 and (a[1] - b[1]) % a[3]:
            return False
        return a[1] < b[2] and b[1] < a[2]

    def wait(q, tok):
        if know[q].get(tok[0], 0) >= tok[1]:
            return
        eng[q].wait_ge(T.sem[tok[0]], tok[1])
        for k, n in list(snap.get(tok, {}).items()) + [tok]:
            know[q][k] = max(know[q].get(k, 0), n)

    def order(q, rd, wr):
        need = {}
        for r, w in [(r, False) for r in rd] + [(r, True) for r in wr]:
            bank = r[0].startswith("ps")
            for r0, w0, q0, tok in acc.get(r[0], []):
                if bank:
                    if q0 == q and not (w0 or w) or (q0 == q and q == "T"):
                        continue
                elif not (w or w0) or not meet(r, r0):
                    continue
                need[tok[0]] = max(need.get(tok[0], 0), tok[1])
        for k in sorted(need):
            wait(q, (k, need[k]))

    def record(q, rd, wr, tok):
        snap[tok] = dict(know[q])
        for r, w in [(r, False) for r in rd] + [(r, True) for r in wr]:
            l = acc.setdefault(r[0], [])
            if w and r[3] == 1:
                l[:] = [e for e in l if not (r[1] <= e[0][1] and e[0][2] <= r[2])]
            if w and r[0].startswith("ps"):
                l[:] = []
            l.append((r, w, q, tok))

    def emit(q, fn, rd, wr):
        rd = [r for r in rd if isinstance(r, tuple)]
        order(q, rd, wr)
        cnt[q] += 1
        fn().then_inc(T.sem["c" + q], 1)
        record(q, rd, wr, ("c" + q, cnt[q]))

    def dma(q, out, in_, rd, wr):
        order(q, rd, wr)
        s = "d%d" % len(dmas)
        dmas.append((q, s))
        eng[q].dma_start(out, in_).then_inc(T.sem[s], 16)
        record(q, rd, wr, (s, 16))

    def sc(x):
        return v(x) if isinstance(x, tuple) else x

    def via(a, ind):
        return v(a).indirect(v(ind)) if ind else v(a)

    def tt(out, a, b, o, ind=None):
        emit("V", lambda: g.vector.tensor_tensor(v(out), via(a, ind), v(b), o), [a, b, ind], [out])

    def ts(out, a, s1, s2, o1, o2=None, ind=None):
        if o2 is None:
            emit("V", lambda: g.vector.tensor_scalar(v(out), via(a, ind), sc(s1), None, o1), [a, s1, ind], [out])
        else:
            emit("V", lambda: g.vector.tensor_scalar(v(out), via(a, ind), sc(s1), sc(s2), o1, o2), [a, s1, s2, ind], [out])

    def tc(out, a, ind=None, oind=None):
        emit("V", lambda: g.vector.tensor_copy(via(out, oind), via(a, ind)), [a, ind, oind], [out])

    def act(out, a, f=AF.Copy, ind=None, **k):
        kw = {n: sc(x) for n, x in k.items()}
        emit("A", lambda: g.scalar.activation(v(out), via(a, ind), f, **kw), [a, ind] + list(k.values()), [out])

    def fill(out, x):
        emit("V", lambda: g.vector.memset(v(out), x), [], [out])

    def const(out, x, src="i2", a=0):
        n = len(range(out[1], out[2], out[3]))
        act(out, R(src, a, a + n), AF.Identity, scale=0.0, bias=float(x))

    def fold(out, a, o):
        emit("V", lambda: g.vector.tensor_reduce(v(out), v(a), AxisListType.X, o), [a], [out])

    def scan(out, z, a, o=op.add):
        emit("V", lambda: g.vector.tensor_tensor_scan(v(out), v(z), v(a), 0.0, op.mult, o), [z, a], [out])

    def hold(a, n, o=0):
        f = R("SF", o, o + n)
        emit("V", lambda: g.vector.tensor_tensor_scan(v(f), v(R("MX", 0, n)), v(a), 0.0, op.add, op.max), [R("MX", 0, n), a], [f])

    def held(out, a, b, k):
        ts(out, R("SF", 16 * a + 15, 16 * b, 16), R("AD", k, k + 1), None, op.add)

    def quant(q, s, a):
        emit("V", lambda: g.vector.quantize_mx(v(q), v(s), v(a)), [a], [q, s])

    def mm(bank, n, lq, ls, rq, rs):
        o = R("ps%d" % bank, 0, n)
        emit("T", lambda: g.tensor.matmul_mx(v(o), v(lq), v(ls), v(rq), v(rs), True, True), [lq, ls, rq, rs], [o])

    def iota(out, pat, base, cm=0):
        kw = {} if SCRATCH[out[0]][2] == "int32" else {"allow_small_or_imprecise_dtypes": True}
        emit("G", lambda: g.iota(v(out), pat, base, cm, **kw), [], [out])

    def table(n, o, s, items):
        for a, pat, base in items:
            m = 1
            for _, c in pat:
                m *= c
            iota(R(n, o + s * a, o + s * (a + m - 1) + 1, s), pat, base)

    rest = []

    def slip(n=1):
        for _ in range(n):
            if rest:
                rest.pop(0)()

    def dist(win, ind, n, o="SB", a=0):
        tt(R("GM", 0, n), win, R("mk", 0, n), op.mult, ind)
        slip()
        scan(R(o, a, a + n), R("R0", 0, n), R("GM", 0, n))
        slip()
        return R(o, a + 15, a + n, 16)

    def b8(r):
        return v(r).bitcast(dt.uint8)

    def cols(n, r, a=0, b=C):
        return R(n, C * r + a, C * r + b)

    dma("Y", v(R("ub")), T.u[:, :], [], [R("ub")])
    dma("A", v(R("seI")), T.se[:, :], [], [R("seI")])
    for q, (a, b) in zip("AYA", CH):
        dma(q, v(R("xb", 4 * a, 4 * b)), T.x[:, 4 * a:4 * b], [], [R("xb", 4 * a, 4 * b)])
    dma("Y", b8(R("wq")), T.wc[:, :], [], [R("wq")])
    dma("Y", v(R("wp")), T.ws[:, :], [], [R("wp")])
    dma("Y", v(R("vb")), T.v[:, :], [], [R("vb")])
    part = [T.cores[rank ^ s] for s in (1, 2, 3)]

    def some(e):
        m = 0
        for k in e:
            m |= 1 << k
        return m

    def tree_engines(a, b):
        return topo.engines(a, b)[-8:]

    def lands(r, sem, n):
        acc.setdefault(r[0], []).append((r, True, "R", (sem, n)))
    for r in range(3):
        n = len(topo.engines(part[r], core))
        lands(cols("hP", r), "as%d" % r, n)
        for k, (a, b) in enumerate(HP[r]):
            lands(cols("hL", r, a, b), "ah%d%d" % (r, k), n)
        if r:
            lands(R("yL", 32 * r, 32 * r + 32), "ay%d" % r, len(tree_engines(part[r], core)))
            lands(R("tL", 32 * r, 32 * r + 32), "at%d" % r, n)
        else:
            lands(R("yL", 0, 16), "ai", n)
            lands(R("YR", 256, 512), "ay0", n)

    def remote(dst, out, in_, rd, sem, e=None):
        order("G", rd, [])
        e = e or topo.engines(core, dst)
        rid, pid, _ = topo.addr(dst)
        g.remote_dma(out_ap=out, in_ap=in_, remote_sem=T.sem[sem], local_sem=T.sem.loc, pid=pid, routing_id=rid, dma_engine_mask=some(e))
        loc[0] += len(e)

    def send_h(r, k):
        a, b = HP[r][k]
        remote(part[r], b8(cols("hL", r, a, b)), b8(cols("hq", r, a, b)), [cols("hq", r, a, b)], "ah%d%d" % (r, k))

    def send_s(r):
        remote(part[r], v(cols("hP", r)), v(cols("hs", r)), [cols("hs", r)], "as%d" % r)

    def send_t(r):
        w = (32 * r, 32 * r + 32)
        remote(part[r], v(R("tL", *w)), v(R("TU", *w)), [R("TU", *w)], "at%d" % r)

    def send_y(r):
        remote(part[r], v(R("yL", 32 * r, 32 * r + 32)), v(R("YB", 1, 33)), [R("YB", 1, 33)], "ay%d" % r, tree_engines(core, part[r]))

    one = [[0, 1]]
    iota(R("tm"), [[1, 128]], 0, -1)
    iota(R("KX"), [[0, 2]], 0, 1)
    iota(R("i2"), [[2, 400]], -384)
    table("TB", 0, 1, [(0, [[-1, 2]], 113), (2, [[1, 2]], 0), (4, [[1, 4]], 30), (8, [[1, 2], [2, 4]], 76),
                       (16, [[32, 2], [64, 4], [2, 2]], -384), (32, [[1, 8], [0, 2]], 1),
                       (48, [[-92, 2]], 100), (50, [[8, 2]], 4), (52, [[4, 4]], 2), (56, [[2, 8]], 1)])
    table("lb", 0, 1, [(0, [[7, 2]], 1), (2, [[0, 2]], 4), (4, [[0, 4]], 2), (8, [[0, 8]], 1)])
    table("TB", 0, 1, [(64, [[0, 2], [1, 8], [0, 2]], 0), (96, [[1, 8], [0, 2]], 8), (112, [[0, 96]], 1)])
    table("TB", 128, 5, [(0, [[1, 16]], 0)])
    table("TB", 129, 5, [(2, [[1, 7], [0, 2]], 1)])
    table("TB", 130, 5, [(4, [[1, 3], [0, 4]], 1)])
    table("TB", 132, 5, [(0, [[1, 16]], 18)])
    table("TB", 129, 1, [(0, [[0, 3]], 0)])
    for k in range(4):
        table("TB", 224 + k, 4, [(0, [[16, 16 >> k], [0, 2 << k]], 31)])
    table("TB", 224, 1, [(0, one, 15), (128, [[1, 2], [2, 16]], 0)])

    fill(R("EB", 512, 1026), 0.0)
    const(R("R0"), 1, "EB", 512)
    const(R("sg", 384, 400), 0.5, "EB", 512)
    const(R("AD", 6, 7), 384, "EB", 512)
    const(R("AD", 7, 8), 385, "EB", 512)
    const(R("R0", 0, 384, 16), 0, "EB", 512)
    fill(R("EB", 0, 512), 0.0)
    ts(R("idn"), R("tm"), 0.0, 0.5, op.is_equal, op.mult)
    ts(R("t2"), R("tm"), 15, None, op.bitwise_and)
    ts(R("KX", 0, 1), R("KX", 0, 1), 15, None, op.bitwise_and)
    ts(R("KX", 1, 2), R("KX", 1, 2), 1, None, op.bitwise_and)
    tc(R("EB", 0, 512, 4), R("idn"))
    ts(R("mk", 0, 128), R("t2"), 0.0, None, op.is_equal)
    tc(R("KF"), R("KX"))
    tc(R("EB", 513, 1024, 4), R("idn"))
    quant(R("eq", 0, 256), R("es", 0, 256), R("EB", 0, 1024))
    ts(R("UL"), R("i2", 0, 64, 8), 384.0, None, op.add)
    q_, bit, q0 = R("KF", 0, 1), R("KF", 1, 2), R("mk", 0, 1)
    act(R("mk", 128, 256), R("mk", 0, 128))
    act(R("mk", 256, 384), R("mk", 0, 128))
    act(R("AD", 1, 2), q_, AF.Identity, scale=1024.0, bias=-15360.0)
    act(R("AD", 0, 1), q0, AF.Identity, scale=768.0, bias=0.5)
    act(R("AD", 4, 5), bit)
    act(R("AD", 5, 6), bit, AF.Identity, bias=768.0)
    act(R("MX"), R("mk", 0, 160), AF.Identity, scale=-33792.0, bias=1024.0)
    ts(R("paI"), R("seI"), 1, None, op.arith_shift_right)
    ts(R("slI"), R("seI"), 1, None, op.bitwise_and)
    quant(R("uq"), R("us"), R("ub"))
    ts(R("sb", 1, 24), R("paI", 1, 24), 2.0, 0.5, op.mult, op.add)
    tc(R("paU"), R("paI"))
    ts(R("sh"), R("slI"), -2.0, 1.0, op.mult, op.add)
    act(R("ups"), R("us"), ind=R("UL"))
    emit("V", lambda: g.vector.tensor_copy(v(R("upq")).bitcast(dt.uint32), v(R("uq")).bitcast(dt.uint32).indirect(v(R("UL")))),
         [R("uq"), R("UL")], [R("upq")])
    act(R("Nc", 0, 768, 2), R("i2", 0, 384))
    act(R("Nc", 1, 768, 2), R("i2", 0, 384))
    act(R("AD", 3, 4), bit, AF.Identity, bias=384.0)
    act(R("EB", 1026, 2048), R("EB", 0, 1022))

    SK, HK, FK, AK = [0, 1, 2], [3, 4, 5, 6], [7, 0, 1, 2], [3, 4, 5, 6]

    def unit(t):
        return R("eq", 128 * t, 128 * t + 128), R("es", 128 * t, 128 * t + 128)

    def pack_x(r, src, a, b):
        quant(cols("xq", r, a, b), cols("xs", r, a, b), R(src, 4 * a, 4 * b))

    def score(r, k):
        a, b = CH[k]
        mm(SK[k], b - a, R("upq"), R("ups"), cols("xq", r, a, b), cols("xs", r, a, b))

    def sign(k):
        a, b = CH[k]
        ts(R("sg", a, b), R("ps%d" % SK[k], 0, b - a), 0.0, 0.5, op.is_ge, op.subtract)

    def layer(r, t, banks=HK, a=0, b=C, cast=True):
        mm(banks[t], b - a, R("wq", 128 * t, 128 * t + 128), R("wp", 128 * t, 128 * t + 128), cols("xq", r, a, b), cols("xs", r, a, b))
        if cast:
            act(R("hb", 4 * a + t, 4 * b, 4), R("ps%d" % banks[t], 0, b - a), scale=0.03125)

    def scaled(t, a, b):
        ts(R("hb", 4 * a + t, 4 * b, 4), R("ps%d" % HK[t], a, b), 0.03125, None, op.mult)

    def pack_h(r, k):
        a, b = CH[k]
        quant(cols("hq", r, a, b), cols("hs", r, a, b), R("hb", 4 * a, 4 * b))

    def unpack(r, t, banks=FK):
        mm(banks[t], C, *unit(t), cols("xq", r), cols("xs", r))

    def own(t, banks=FK):
        act(cols("fb", t), R("ps%d" % banks[t], 0, C))

    def above(t):
        act(cols("bb", t), cols("fb", t), ind=R("paU"))

    def arrived(r, t):
        mm(AK[t], C, *unit(t), cols("hL", r), cols("hP", r))
        act(cols("ab", t), R("ps%d" % AK[t], 0, C))

    def yrep(r):
        act(R("YR", 512 * r, 512 * r + 512), R("iC"), ind=R("yL", 32 * r, 32 * r + 32))

    def renew(r, t, a=0, b=C):
        tt(R("xn", 4 * a + t, 4 * b, 4), cols("ab", t), cols("bb", t, a, b), op.add, R("MU", 24 * r + a // 16, 24 * r + b // 16))

    def dist2(win, ind, at):
        for a, b in HALF:
            tt(R("GM", a, b), win, R("mk", 0, b - a), op.mult, R(ind, at + a // 16, at + b // 16))
            slip()
        for a, b in HALF:
            scan(R("SB", a, b), R("R0", 0, b - a), R("GM", a, b))
            slip()

    def maps(win, ind, at, r, x, y):
        dist2(win, ind, at)
        for a, b in HALF:
            ts(R("MU", 24 * r + a // 16, 24 * r + b // 16), R("SB", a + 15, b, 16), x, y, op.add, op.mult)

    def picked(r, t, a=0, b=C):
        act(cols("ag", t, a, b), cols("ab", t), ind=R("MU", 24 * r + a // 16, 24 * r + b // 16))

    def add(t, a, b):
        tt(R("xn", 4 * a + t, 4 * b, 4), cols("ag", t, a, b), cols("bb", t, a, b), op.add)

    def state(r):
        picked(r, 2)
        picked(r, 3)
        for a, b in HALF:
            renew(r, 0, a, b)
        renew(r, 1)
        add(2, 0, C)
        add(3, 0, 128)
        add(3, 128, C)
        for k, (a, b) in enumerate(CH):
            pack_x(r + 1, "xn", a, b)
            score(r + 1, k)

    for k, (a, b) in enumerate(CH):
        pack_x(0, "xb", a, b)
        score(0, k)
    for k in range(len(CH)):
        sign(k)
    for t in range(4):
        layer(0, t, HK, *HP[0][0])
    hold(R("TB", 0, 64), 64)
    tc(R("L", 112, 114), R("AD", 4, 6))
    rest.extend([lambda: None, lambda: None, lambda: ts(R("PF"), R("SF", 31, 64, 32), R("AD", 1, 2), None, op.add),
                 lambda: (ts(R("sb", 0, 1), R("paI", 0, 1), 2.0, R("AD", 0, 1), op.mult, op.add), held(R("PL", 0, 4), 0, 4, 1))])
    dist2(R("sg"), "paU", 0)
    for t in range(4):
        layer(0, t, FK, *HP[0][1])
    act(R("AD", 8, 10), R("AD", 6, 8), AF.Identity, scale=0.0, bias=R("AD", 4, 5))
    act(R("AD", 12, 13), q_, AF.Identity, bias=0.5)
    act(R("lb", 16, 32), R("lb", 0, 16))
    act(R("AD", 10, 12), R("AD", 8, 10), AF.Identity, scale=-1.0)
    for f, o in ((AF.Abs, "ad"), (AF.Sign, "sn")):
        act(R(o, 0, 16), R("TB", 48, 64), f, scale=-1.0, bias=R("PF", 1, 2))
        act(R(o, 16, 32), R("TB", 48, 64), f, scale=-1.0, bias=R("AD", 12, 13))
    act(R("l32"), R("lb"), AF.Identity, scale=32.0)
    tt(R("sw"), R("SB", 15, C, 16), R("sh"), op.mult)
    quant(R("eq", 256, 384), R("es", 256, 384), R("EB", 1024, 1536))
    tt(R("s24"), R("sb"), R("sw"), op.subtract)
    quant(R("eq", 384, 512), R("es", 384, 512), R("EB", 1536, 2048))
    tc(R("stU"), R("s24"))
    pack_h(0, 0)
    send_h(0, 0)
    tc(R("Nc"), R("i2", 0, 384), oind=R("stU"))
    const(R("PW"), 0)
    act(R("AM", 32, 48), R("mk", 0, 16))
    for t in range(4):
        unpack(0, t, HK)
        own(t, HK)
        if t == 1:
            const(R("R5"), 1)
            const(R("SB2", 256, 288), 0)
            act(R("AD", 2, 3), q_, AF.Identity, scale=512.0, bias=-7488.0)
            const(R("R5", 0, 80, 5), 0)
    nc = R("Nc", 0, 768)
    up = R("AD", 3, 4)
    pack_h(0, 1)
    ts(R("L", 0, 16), nc, up, None, op.add, ind=R("L", 112, 113))
    pack_h(0, 2)
    ts(R("L", 16, 48), nc, up, None, op.add, ind=R("L", 0, 2))
    ts(R("mW"), R("i2", 0, 128), R("PF", 0, 1), -1024.0, op.not_equal, op.mult)
    tt(R("AM", 0, 32), R("lb"), R("ad"), op.is_gt)
    send_h(0, 1)
    send_s(0)
    iota(R("JC"), [[16, 16], [0, 5]], 400, 1)
    iota(R("JC", 4, 80, 5), [[0, 16]], 1)
    iota(R("VR", 0, 16), [[1, 16]], 240)
    iota(R("VR", 16, 256), [[32, 15], [1, 16]], -240)
    iota(R("inv", 0, C), [[0, C]], 0)
    ts(R("L", 48, 112, 2), nc, up, None, op.add, ind=R("L", 30, 32))
    ts(R("L", 49, 112, 2), nc, up, None, op.add, ind=R("L", 32, 34))
    hold(R("TB", 64, 208), 144)
    tt(R("GM", 0, 128), nc, R("mW"), op.add, R("L", 76, 84))
    tc(R("Lf"), R("L"))
    y4 = R("SB2", 31, 32)
    fold(y4, R("GM", 0, 128), op.max)
    tt(R("g16"), R("Lf"), R("mk", 0, 16), op.mult, R("PL", 0, 1))
    held(R("PL", 4, 13), 0, 9, 1)
    ts(R("LL", 2, 4), R("AD", 6, 8), y4, None, op.add)
    rest.extend([
        lambda: (fold(R("yt", 0, 1), R("g16"), op.add), ts(R("YB", 2, 3), y4, 384.0, 0.5, op.add, op.mult)),
        lambda: (ts(R("YB", 0, 2), R("AD", 10, 12), R("yt", 0, 1), 0.5, op.add, op.mult), tt(R("sl"), R("sn"), R("l32"), op.mult)),
        lambda: quant(R("vq"), R("vs"), R("vb")),
        lambda: tc(R("TR"), R("i2"), ind=R("YB", 0, 3)),
        lambda: (tc(R("TQ"), R("i2"), ind=R("YB", 0, 1)), tc(R("EW", 18, 20), R("YB", 1, 3))),
        lambda: tt(R("eT"), R("TQ"), R("TR"), op.is_equal, R("PL", 4, 7)),
        lambda: (tc(R("PW", 1, 8), R("SB2", 31, 128, 16)), tt(R("C0", 0, 32), R("sl"), R("AM", 0, 32), op.mult)),
        lambda: (tt(R("gT"), R("eT"), R("AM"), op.mult), tt(R("C0", 0, 16), R("C0", 0, 16), R("C0", 16, 32), op.subtract)),
        lambda: (fold(R("EW", 0, 1), R("gT", 0, 16), op.max), fold(R("EW", 1, 2), R("gT", 16, 48), op.max)),
    ])
    slip()
    low = R("SB2", 47, 256, 16)
    for n in (2, 4, 8):
        w = dist(nc, R("LL", n, 2 * n), 16 * n, "SB2", 16 * n)
        if n == 8:
            tt(R("EW", 2, 18), R("PW", 0, 9), R("SB2", 47, 288, 16), op.is_equal, R("PL", 2, 3))
            ts(R("EW", 20, 34), low, 384.0, 0.5, op.add, op.mult)
        ts(R("LL", 2 * n, 4 * n, 2), w, 384.0, None, op.add)
        ts(R("LL", 2 * n + 1, 4 * n, 2), w, 385.0, None, op.add)
        if n < 8:
            slip()
    act(R("sp", 1, 24), R("sw", 1, 24), AF.Identity, scale=-16.0, bias=280.0)
    act(R("AD", 13, 14), q0, AF.Identity, scale=16.0, bias=-16.0)
    act(R("AD", 14, 15), q0, AF.Identity, scale=-520.0, bias=280.0)
    act(R("sp", 0, 1), R("sw", 0, 1), AF.Identity, scale=R("AD", 13, 14), bias=R("AD", 14, 15))
    for t in range(3):
        above(t)
    act(R("GA"), nc, ind=R("LL", 16, 32))
    above(3)
    ts(R("YB", 3, 17), low, 384.0, 0.5, op.add, op.mult)
    tt(R("P5"), R("EW"), R("JC"), op.mult, R("PL", 8, 13))
    remote(part[0], v(R("yL", 0, 16)), v(R("YB", 1, 17)), [R("YB", 1, 17)], "ai")
    remote(part[0], v(R("YR", 256, 512)), v(R("GA")), [R("GA")], "ay0")
    iota(R("iC"), [[1, 512]], -256)
    hold(R("TB", 224, 384), 160)
    scan(R("S5"), R("R5"), R("P5"), op.max)
    held(R("PL", 14, 24), 0, 10, 1)
    tc(R("oU"), R("S5", 4, 80, 5))
    hold(R("GA", 0, 128), 128)
    tc(R("inv"), R("VR"), oind=R("oU"))
    hold(R("GA", 128, 256), 128, 128)
    rest.append(lambda: (ts(R("YB", 17, 33), R("SF", 15, 256, 16), 0.5, R("AD", 2, 3), op.mult, op.add), send_y(1), send_y(2)))
    dist2(R("inv", 0, C), "paU", 0)
    for a, b in HALF:
        tt(R("NS", a // 16, b // 16), R("SB", a + 15, b, 16), R("sp", a // 16, b // 16), op.add)
    for a, b in HALF:
        tc(R("NP", a // 16, b // 16), R("NS", a // 16, b // 16))
    iota(R("PS"), [[0, 128]], 0)
    for k in range(4):
        table("PS", k, 4, [(2 << k, [[0, (16 >> k) - 1], [2, 2], [0, 1 << k]], -1)])
    table("PS", 0, 1, [(0, one, 1)])
    arrived(0, 0)
    act(R("YR", 0, 256), R("i2"), ind=R("yL", 0, 16))
    act(R("YR", 512, 544), R("YR", 0, 32), ind=R("PL", 22, 24))
    for t in range(1, 4):
        arrived(0, t)
    maps(R("YR", 0, 544), "NP", 0, 0, 384.0, 0.5)
    state(0)
    for m, x in ((1, 16.0), (2, 8.0), (4, 4.0), (8, 2.0)):
        act(R("C0", 16 + 16 * m, 16 + 32 * m), R("mk", 0, 16 * m), AF.Identity, scale=x)
    const(R("R4"), 1)
    act(R("C0", 0, 1), q0, AF.Identity, scale=-512.0)
    const(R("C0", 16, 17), 512)
    const(R("R4", 0, 128, 4), 0)
    yrep(1)

    for r in (1, 2):
        c0, c1 = ("C0", "C1") if r == 1 else ("C1", "C0")
        for k in range(len(CH)):
            sign(k)
        for t in (0, 2, 1, 3):
            layer(r, t, cast=t < 2)
        for t in range(4):
            unpack(r, t)
        own(0)
        own(1)
        tt(R(c1), R("sg"), R(c0), op.mult, R("YB", 0, 17))
        scaled(2, *HALF[0])
        scan(R("SC"), R("R0", 0, 272), R(c1))
        scaled(2, *HALF[1])
        tt(R("P1"), R("SC"), R("PS"), op.mult, R("PL", 14, 22))
        scaled(3, *HALF[0])
        scan(R("P4"), R("R4"), R("P1"))
        scaled(3, *HALF[1])
        ts(R("TU", 32 * r, 32 * r + 32), R("P4", 3, 128, 4), R("SC", 31, 32), float(r), op.add, op.mult)
        send_t(r)
        act(R("Tr", 16 * TV, 512), R("iC"), ind=R("TU", 32 * r + TV, 32 * r + 32))
        for m in range(len(CH)):
            pack_h(r, m)
        send_h(r, 0)
        send_s(r)
        tc(R("Tr", 0, 32), R("iC"), ind=R("TU", 32 * r, 32 * r + 2))
        tc(R("Tr", 32, 16 * TV), R("iC"), ind=R("TU", 32 * r + 2, 32 * r + TV))
        tc(R("Tr", 512, 544), R("Tr", 0, 32), ind=R("PL", 22, 24))
        own(2)
        own(3)
        dist2(R("Tr"), "NP", 0)
        ts(R("HL", 24 * r, 24 * r + 24), R("SB", 15, C, 16), 256.0, None, op.add)
        for t in range(4):
            above(t)
        for t in range(4):
            arrived(r, t)
        tc(R("Z"), R("YR", 512 * r, 512 * r + 512), oind=R("tL", 32 * r, 32 * r + 32))
        maps(R("Z"), "HL", 24 * r, r, 256.0, 1.0)
        if r == 1:
            state(r)
            yrep(2)
    (a, b), (c, d) = LAST
    renew(2, 0, *HALF[0])
    renew(2, 0, HALF[0][1], b)
    for t in range(1, 4):
        renew(2, t, a, b)
    for t in range(4):
        picked(2, t, c, d)
    act(R("mr"), R("Z"), AF.Identity, ind=R("HL", 48, 72), bias=256.0)
    dma("A", T.im[:, :], T.mr[0:128:16, 0:C], [R("mr")], [])
    add(0, c, d)
    add(1, c, d)
    for k, (a, b) in enumerate(LAST):
        pack_x(3, "xn", a, b)
        q3, s3 = cols("xq", 3, a, b), cols("xs", 3, a, b)
        mm(SK[k], b - a, R("vq"), R("vs"), q3, s3)
        dma("Y", T.oc[:, 4 * a:4 * b], b8(q3), [q3], [])
        if k:
            for m in range(4):
                dma("YA"[m // 2], T.osc[4 * m:4 * m + 4, :], T.xs[32 * m:32 * m + 4, 3 * C:4 * C], [cols("xs", 3)], [])
        (tc if k else act)(R("yb", a, b), R("ps%d" % SK[k], 0, b - a))
        dma("A", T.y[:, a:b], v(R("yb", a, b)), [R("yb", a, b)], [])
        if not k:
            for t in range(2, 4):
                add(t, c, d)
    for q, s in dmas:
        wait(q, (s, 16))
    for q in ("V", "A", "T", "G"):
        g.wait_ge(T.sem["c" + q], cnt[q])
    g.wait_ge(T.sem.loc, loc[0])
